import numpy as np
import ml_dtypes


def mxq(x, axis, fmt="e4m3"):
    dtype, down = {"e4m3": (ml_dtypes.float8_e4m3fn, 7), "e5m2": (ml_dtypes.float8_e5m2, 14)}[fmt]
    v = np.moveaxis(np.asarray(x, np.float32).astype(ml_dtypes.bfloat16).astype(np.float64), axis, -1)
    blocks = v.reshape(v.shape[:-1] + (-1, 32))
    amax = np.abs(blocks).max(-1, keepdims=True)
    byte = np.maximum(np.where(amax > 0, np.frexp(amax)[1] - 1 + 127, 0) - down, 1)
    scale = np.exp2(byte - 127.0)
    codes = (blocks / scale).astype(np.float32).astype(dtype).astype(np.float64)
    return np.moveaxis((codes * scale).reshape(v.shape), -1, axis)


WIDE = False


def mx_kscale(k):
    if not WIDE:
        return np.ones(k)
    levels = np.array([10, -10, 5, -5, 0])
    if k % 512:
        return np.exp2(np.random.permutation(np.resize(levels, k // 32))).repeat(32)
    a = np.empty((k // 512, 16))
    for p in range(k // 512):
        a[p, :8] = np.random.permutation(np.resize(levels, 8))
        for g in range(8):
            far = levels[np.abs(levels - a[p, g]) >= 10]
            a[p, g + 8] = far[np.random.randint(len(far))]
    return np.exp2(a.ravel()).repeat(32)


def f64(x):
    return np.asarray(x).astype(np.float64)


def striped(idx):
    return np.tile(idx.reshape(-1, 16).T, (8, 1)).astype(np.uint16)


def unstriped(offs):
    return offs[:16].T.reshape(-1).astype(np.int64)


E2M1 = np.array([0.0, 0.5, 1.0, 1.5, 2.0, 3.0, 4.0, 6.0, -0.0, -0.5, -1.0, -1.5, -2.0, -3.0, -4.0, -6.0])


def pack_weight(w, fmt):
    k, n = w.shape
    w = f64(np.asarray(w, np.float32).astype(ml_dtypes.bfloat16)).reshape(k // 32, 32, n)
    amax = np.abs(w).max(1)
    if fmt == "e4m3":
        byte = np.frexp(amax)[1] - 1 + 127 - 7
    else:
        mant, ex = np.frexp(amax / 6.0)
        byte = np.where(mant > 0.5, ex, ex - 1) + 127
    byte = np.clip(np.where(amax > 0, byte, 1), 1, 254)
    scaled = (w * np.exp2(127.0 - byte)[:, None, :]).reshape(k, n).astype(np.float32)
    by_word = np.ascontiguousarray(scaled.reshape(k // 512, 128, 4, n).transpose(0, 1, 3, 2))
    if fmt == "e4m3":
        words = by_word.astype(ml_dtypes.float8_e4m3fn).view(np.uint8)
    else:
        c = by_word.astype(ml_dtypes.float4_e2m1fn).view(np.uint8) & 0xF
        words = (c[..., 0::2] | (c[..., 1::2] << 4)).reshape(k // 512, 128, 2 * n)
    return np.ascontiguousarray(words), np.ascontiguousarray(byte.astype(np.uint8).reshape(k // 512, 16, n))


def unpack_weight(words, scales, fmt):
    g, _, n = scales.shape
    words = np.ascontiguousarray(words).reshape(g, 128, n, -1)
    if fmt == "e4m3":
        vals = words.view(ml_dtypes.float8_e4m3fn).astype(np.float64)
    else:
        nib = np.empty((g, 128, n, 4), np.uint8)
        nib[..., 0::2] = words & 0xF
        nib[..., 1::2] = words >> 4
        vals = E2M1[nib]
    vals = vals * np.repeat(np.exp2(scales.astype(np.float64) - 127.0), 8, axis=1)[..., None]
    return vals.transpose(0, 1, 3, 2).reshape(g * 512, n)


def gelu(v):
    return 0.5 * v * (1.0 + np.tanh(np.sqrt(2.0 / np.pi) * (v + 0.044715 * v**3)))


def often(T, S):
    return np.random.permutation(T)[(T * np.random.uniform(0, 1, S) ** 4).astype(np.int64)]


KP, KE, H, N, T, S = 1024, 512, 1024, 512, 4096, 1024

def setup_inputs():
    n = np.random.standard_normal
    s = mx_kscale(KP)[:, None]
    s2 = mx_kscale(KE)[:, None]
    u = mx_kscale(H)[:, None]
    tab_words, tab_scales = pack_weight(n((KP, T)) * s, "e4m3")
    tab2_words, tab2_scales = pack_weight(n((KE, T)) * s2, "e2m1")
    wf_words, wf_scales = pack_weight(0.7 * n((KP, H)) / np.sqrt(KP) / s, "e2m1")
    wt_words, wt_scales = pack_weight(1.2 * n((H, N)) / np.sqrt(H) / u, "e4m3")
    return {
        "tab_words": tab_words, "tab_scales": tab_scales,
        "offs": striped(often(T, S)),
        "tab2_words": tab2_words, "tab2_scales": tab2_scales,
        "offs2": striped(often(T, S)),
        "wf_words": wf_words, "wf_scales": wf_scales,
        "ws": (0.8 * n((KE, H)) / np.sqrt(KE) / s2).astype(np.float32),
        "gain": (2.0 * np.exp(0.3 * n(H)) * u[:, 0]).astype(np.float32),
        "wt_words": wt_words, "wt_scales": wt_scales,
        "cat": (0.6 * n((N, S))).astype(np.float32),
    }

def reference(tab_words, tab_scales, offs, tab2_words, tab2_scales, offs2,
              wf_words, wf_scales, ws, gain, wt_words, wt_scales, cat):
    v = unpack_weight(tab_words, tab_scales, "e4m3")[:, unstriped(offs)]
    v2 = unpack_weight(tab2_words, tab2_scales, "e2m1")[:, unstriped(offs2)]
    wf = unpack_weight(wf_words, wf_scales, "e2m1")
    wt = unpack_weight(wt_words, wt_scales, "e4m3")
    sysm = mxq(f64(ws), 0, "e4m3").T @ v2
    flux = wf.T @ v
    d = sysm - flux
    h = d / (1.0 + d * d) * f64(gain)[:, None]
    return (wt.T @ mxq(h, 0, "e4m3")) + f64(cat)

@@ -1,0 +1,200 @@
+from contextlib import ExitStack
+
+import concourse.mybir as mybir
+
+KP, KE, H, N, T, S = 1024, 512, 1024, 512, 4096, 1024
+FLOPS = 2 * S * (KP * H + KE * H + H * N)
+
+F32 = mybir.dt.float32
+BF16 = mybir.dt.bfloat16
+I32 = mybir.dt.int32
+U32 = mybir.dt.uint32
+U16 = mybir.dt.uint16
+U8 = mybir.dt.uint8
+FP8X4 = mybir.dt.float8_e4m3fn_x4
+FP4X4 = mybir.dt.float4_e2m1fn_x4
+ALU = mybir.AluOpType
+ACT = mybir.ActivationFunctionType
+
+P = 128
+HALF = 512
+LIST_COLS = HALF // 16
+LAST_PIECES = ((0, 256), (256, 128), (384, 128))
+
+
+def tile_list_transit_template_detrending_kernel(
+    tc, tab_words, tab_scales, offs, tab2_words, tab2_scales, offs2,
+    wf_words, wf_scales, ws, gain, wt_words, wt_scales, cat, out,
+):
+    nc = tc.nc
+    with ExitStack() as ctx:
+        keep = ctx.enter_context(tc.tile_pool(name="keep", bufs=1))
+        work = ctx.enter_context(tc.tile_pool(name="work", bufs=2))
+        ps1 = ctx.enter_context(tc.psum_pool(name="ps1", bufs=4))
+        ps2 = ctx.enter_context(tc.psum_pool(name="ps2", bufs=4))
+
+        def held(shape, dtype, name):
+            return keep.tile(shape, dtype, name=name, align_bytes=64)
+
+        list1 = keep.tile([P, S // 16], U16, name="list1")
+        list2 = keep.tile([P, S // 16], U16, name="list2")
+        t2_words = held([P, T], U16, "t2_words")
+        t2_scales = held([P, T], U8, "t2_scales")
+        t1_words = [held([P, T], I32, "t1_words%d" % a) for a in range(2)]
+        t1_scales = held([P, T], U8, "t1_scales")
+        ws_raw = [held([P, 4, HALF], F32, "ws_raw%d" % b) for b in range(2)]
+        wf_raw = held([P, 2, H], U16, "wf_raw")
+        wf_sraw = held([P, 2, H], U8, "wf_sraw")
+        wt_codes = held([P, 2, N], I32, "wt_codes")
+        wt_sc = held([P, 2, N], U8, "wt_sc")
+        cat_sb = [held([P, 4, HALF], F32, "cat%d" % jh) for jh in range(2)]
+        g = held([P, 2, 4], F32, "g")
+        g1_s1 = held([P, S], U8, "g1_s1")
+        warm = held([P, 16], F32, "warm")
+
+        nc.vector.memset(t2_scales[:].bitcast(I32), 0)
+        nc.vector.memset(warm[:], 1.0)
+        nc.vector.memset(t1_scales[:].bitcast(I32), 0)
+        nc.vector.memset(wf_sraw[:].rearrange("p a c -> p (a c)").bitcast(I32), 0)
+        nc.vector.memset(wt_sc[:].rearrange("p a c -> p (a c)").bitcast(I32), 0)
+        nc.vector.memset(g1_s1[:].bitcast(I32), 0)
+        warm_out = held([P, 16], F32, "warm_out")
+        nc.scalar.activation(warm_out[:], warm[:], ACT.Abs_reciprocal_sqrt)
+
+        nc.sync.dma_start(list2[:], offs2)
+        nc.sync.dma_start(t2_words[:].bitcast(I32), tab2_words[0].bitcast(I32))
+        ws_v = ws.rearrange("(p j) c -> p j c", j=4)
+        for b in range(2):
+            nc.sync.dma_start(ws_raw[b][:], ws_v[:, :, b * HALF:(b + 1) * HALF])
+        nc.sync.dma_start(list1[:], offs)
+        nc.sync.dma_start(g[:], gain.rearrange("(b p t) -> p b t", b=2, t=4))
+        nc.sync.dma_start(wf_raw[:].bitcast(I32), wf_words.rearrange("a p c -> p a c").bitcast(I32))
+        for a in range(2):
+            nc.sync.dma_start(t1_words[a][:], tab_words[a].rearrange("p t i -> p (t i)").bitcast(I32))
+        for q in range(4):
+            nc.gpsimd.dma_start(t2_scales[32 * q:32 * q + 4, :].bitcast(I32),
+                                tab2_scales[0, 4 * q:4 * q + 4, :].bitcast(I32))
+        for q in range(4):
+            nc.gpsimd.dma_start(t1_scales[32 * q:32 * q + 8, :].bitcast(I32),
+                                tab_scales[:, 4 * q:4 * q + 4, :].bitcast(I32))
+        for q in range(4):
+            nc.gpsimd.dma_start(wf_sraw[32 * q:32 * q + 4, :, :].bitcast(I32),
+                                wf_scales[:, 4 * q:4 * q + 4, :].rearrange("a r c -> r a c").bitcast(I32))
+
+        g_flat = g[:].rearrange("p b t -> p (b t)")
+        g_neg = held([P, 8], F32, "g_neg")
+        g_safe = held([P, 8], F32, "g_safe")
+        g_inv = held([P, 8], F32, "g_inv")
+        nc.vector.tensor_scalar(g_neg[:], g_flat, -1.0, None, ALU.mult)
+        nc.vector.scalar_tensor_tensor(g_safe[:], g_flat, 0.0, g_flat, ALU.is_equal, ALU.add)
+        nc.vector.reciprocal(g_inv[:], g_safe[:])
+
+        g2_w = [held([P, HALF], U16, "g2_w%d" % jh) for jh in range(2)]
+        g2_s = [held([P, HALF], U8, "g2_s%d" % jh) for jh in range(2)]
+        for jh in range(2):
+            cols = list2[:, jh * LIST_COLS:(jh + 1) * LIST_COLS]
+            nc.vector.tensor_copy(g2_w[jh][:], t2_words[:].indirect(cols))
+            nc.vector.tensor_copy(g2_s[jh][:], t2_scales[:].indirect(cols))
+
+        ws_codes = [held([P, HALF], U32, "ws_codes%d" % b) for b in range(2)]
+        ws_sc = [held([P, HALF], U8, "ws_sc%d" % b) for b in range(2)]
+        for b in range(2):
+            ws_bf = work.tile([P, 4 * HALF], BF16, name="ws_bf", align_bytes=64)
+            nc.scalar.copy(ws_bf[:].rearrange("p (t m j) -> p m j t", t=4, j=4),
+                           ws_raw[b][:].rearrange("p j (m t) -> p m j t", t=4))
+            nc.vector.quantize_mx(ws_codes[b][:].bitcast(FP8X4), ws_sc[b][:], ws_bf[:])
+
+        resid = [[held([P, 4, HALF], F32, "resid%d%d" % (jh, b)) for b in range(2)] for jh in range(2)]
+        for b in range(2):
+            for jh in range(2):
+                for t in range(4):
+                    acc = ps1.tile([P, HALF], F32, name="acc1")
+                    m = slice(t * P, (t + 1) * P)
+                    nc.tensor.matmul_mx(acc[:], lhsT=ws_codes[b][:, m].bitcast(FP8X4), lhsT_scale=ws_sc[b][:, m],
+                                        rhs=g2_w[jh][:].bitcast(FP4X4), rhs_scale=g2_s[jh][:], start=True, stop=True)
+                    nc.scalar.activation(resid[jh][b][:, t, :], acc[:], ACT.Copy, scale=g[:, b, t:t + 1])
+
+        g1_s0 = held([P, S], U8, "g1_s0")
+        nc.vector.tensor_copy(g1_s0[:], t1_scales[:].indirect(list1[:]))
+        nc.sync.dma_start(g1_s1[0:100, :].bitcast(I32), g1_s0[4:104, :].bitcast(I32))
+        g1_s = (g1_s0, g1_s1)
+
+        nc.sync.dma_start(wt_codes[:], wt_words.rearrange("a p c i -> p a (c i)").bitcast(I32))
+        for q in range(4):
+            nc.sync.dma_start(wt_sc[32 * q:32 * q + 4, :, :].bitcast(I32),
+                              wt_scales[:, 4 * q:4 * q + 4, :].rearrange("a r c -> r a c").bitcast(I32))
+        cat_v = cat.rearrange("(nt p) j -> p nt j", p=P)
+        out_v = out.rearrange("(nt p) j -> p nt j", p=P)
+        for jh in range(2):
+            nc.sync.dma_start(cat_sb[jh][:], cat_v[:, :, jh * HALF:(jh + 1) * HALF])
+
+        wf_codes = held([P, 2, H], U16, "wf_codes")
+        wf_sc = held([P, 2, H], U8, "wf_sc")
+        nc.vector.tensor_copy(wf_codes[:].rearrange("p a (b t m) -> p (a b) m t", b=2, t=4),
+                              wf_raw[:].rearrange("p a (b m t) -> p (a b) m t", b=2, t=4))
+        nc.vector.tensor_copy(wf_sc[:].rearrange("p a (b t m) -> p (a b) m t", b=2, t=4),
+                              wf_sraw[:].rearrange("p a (b m t) -> p (a b) m t", b=2, t=4))
+
+        g1_w = [[held([P, HALF], U32, "g1_w%d%d" % (a, jh)) for jh in range(2)] for a in range(2)]
+        for a in range(2):
+            for jh in range(2):
+                cols = list1[:, jh * LIST_COLS:(jh + 1) * LIST_COLS]
+                nc.vector.tensor_copy(g1_w[a][jh][:], t1_words[a][:].bitcast(U32).indirect(cols))
+
+        h_codes = [[held([P, HALF], U32, "h_codes%d%d" % (jh, b)) for b in range(2)] for jh in range(2)]
+        h_sc = [[held([P, HALF], U8, "h_sc%d%d" % (jh, b)) for b in range(2)] for jh in range(2)]
+
+        def flux(jh, b):
+            js = slice(jh * HALF, (jh + 1) * HALF)
+            for t in range(4):
+                acc = ps1.tile([P, HALF], F32, name="acc1")
+                m = slice(b * HALF + t * P, b * HALF + (t + 1) * P)
+                for a in range(2):
+                    nc.tensor.matmul_mx(acc[:], lhsT=wf_codes[:, a, m].bitcast(FP4X4), lhsT_scale=wf_sc[:, a, m],
+                                        rhs=g1_w[a][jh][:].bitcast(FP8X4), rhs_scale=g1_s[a][:, js],
+                                        start=(a == 0), stop=(a == 1))
+                r = resid[jh][b][:, t, :]
+                nc.vector.scalar_tensor_tensor(r, acc[:], g_neg[:, 4 * b + t:4 * b + t + 1], r, ALU.mult, ALU.add)
+
+        def damp(jh, b, c0, w):
+            cs = slice(c0, c0 + w)
+            x = work.tile([P, 4, w], F32, name="x", align_bytes=64, bufs=3)
+            for t in range(4):
+                nc.scalar.activation(x[:, t, :], resid[jh][b][:, t, cs], ACT.Square,
+                                     scale=g_inv[:, 4 * b + t:4 * b + t + 1])
+            for t in range(4):
+                nc.scalar.activation(x[:, t, :], x[:, t, :], ACT.Abs_reciprocal_sqrt, bias=1.0)
+            for t in range(4):
+                nc.scalar.activation(x[:, t, :], x[:, t, :], ACT.Square)
+            h = work.tile([P, 4 * w], BF16, name="h", align_bytes=64)
+            nc.vector.tensor_tensor(h[:].rearrange("p (c i t) -> p c t i", i=4, t=4),
+                                    resid[jh][b][:, :, cs].rearrange("p t (c i) -> p c t i", i=4),
+                                    x[:].rearrange("p t (c i) -> p c t i", i=4), ALU.mult)
+            nc.vector.quantize_mx(h_codes[jh][b][:, cs].bitcast(FP8X4), h_sc[jh][b][:, cs], h[:])
+
+        def project(jh, c0, w):
+            cs = slice(c0, c0 + w)
+            per_bank = HALF // w
+            for n0 in range(0, 4, per_bank):
+                acc = ps2.tile([P, per_bank, w], F32, name="acc2")
+                for k in range(per_bank):
+                    m = slice((n0 + k) * P, (n0 + k + 1) * P)
+                    for b in range(2):
+                        nc.tensor.matmul_mx(acc[:, k, :], lhsT=wt_codes[:, b, m].bitcast(FP8X4), lhsT_scale=wt_sc[:, b, m],
+                                            rhs=h_codes[jh][b][:, cs].bitcast(FP8X4), rhs_scale=h_sc[jh][b][:, cs],
+                                            start=(b == 0), stop=(b == 1))
+                o = cat_sb[jh][:, n0:n0 + per_bank, cs]
+                nc.vector.tensor_tensor(o, acc[:], o, ALU.add)
+            nc.sync.dma_start(out_v[:, :, jh * HALF + c0:jh * HALF + c0 + w], cat_sb[jh][:, :, cs])
+
+        flux(0, 0)
+        flux(0, 1)
+        damp(0, 0, 0, HALF)
+        flux(1, 0)
+        damp(0, 1, 0, HALF)
+        flux(1, 1)
+        project(0, 0, HALF)
+        damp(1, 0, 0, HALF)
+        for c0, w in LAST_PIECES:
+            damp(1, 1, c0, w)
+            project(1, c0, w)

@@ -33,22 +33,20 @@ def tile_list_transit_template_detrending_kernel(
         ps1 = ctx.enter_context(tc.psum_pool(name="ps1", bufs=4))
         ps2 = ctx.enter_context(tc.psum_pool(name="ps2", bufs=4))
 
-        def held(shape, dtype, name):
-            return keep.tile(shape, dtype, name=name, align_bytes=64)
+        def held(shape, dtype, name, tag=""):
+            return keep.tile(shape, dtype, name=name, tag=tag, align_bytes=64)
 
         list1 = keep.tile([P, S // 16], U16, name="list1")
         list2 = keep.tile([P, S // 16], U16, name="list2")
         t2_words = held([P, T], U16, "t2_words")
         t2_scales = held([P, T], U8, "t2_scales")
-        t1_words = [held([P, T], I32, "t1_words%d" % a) for a in range(2)]
-        t1_scales = held([P, T], U8, "t1_scales")
-        ws_raw = [held([P, 4, HALF], F32, "ws_raw%d" % b) for b in range(2)]
+        t1_words = [held([P, T], I32, "t1_words%d" % a, "big%d" % a) for a in range(2)]
+        t1_scales = held([P, T], U8, "t1_scales", "mid")
+        ws_raw = [held([P, 4, 256], F32, "ws_raw%d" % u) for u in range(4)]
         wf_raw = held([P, 2, H], U16, "wf_raw")
         wf_sraw = held([P, 2, H], U8, "wf_sraw")
-        wt_codes = held([P, 2, N], I32, "wt_codes")
         wt_sc = held([P, 2, N], U8, "wt_sc")
-        cat_sb = [held([P, 4, HALF], F32, "cat%d" % jh) for jh in range(2)]
-        g = held([P, 2, 4], F32, "g")
+        g = held([P, 2, 8], F32, "g")
         g1_s1 = held([P, S], U8, "g1_s1")
         warm = held([P, 16], F32, "warm")
 
@@ -61,32 +59,42 @@ def tile_list_transit_template_detrending_kernel(
         warm_out = held([P, 16], F32, "warm_out")
         nc.scalar.activation(warm_out[:], warm[:], ACT.Abs_reciprocal_sqrt)
 
-        nc.sync.dma_start(list2[:], offs2)
-        nc.sync.dma_start(t2_words[:].bitcast(I32), tab2_words[0].bitcast(I32))
-        ws_v = ws.rearrange("(p j) c -> p j c", j=4)
-        for b in range(2):
-            nc.sync.dma_start(ws_raw[b][:], ws_v[:, :, b * HALF:(b + 1) * HALF])
-        nc.sync.dma_start(list1[:], offs)
-        nc.sync.dma_start(g[:], gain.rearrange("(b p t) -> p b t", b=2, t=4))
-        nc.sync.dma_start(wf_raw[:].bitcast(I32), wf_words.rearrange("a p c -> p a c").bitcast(I32))
-        for a in range(2):
-            nc.sync.dma_start(t1_words[a][:], tab_words[a].rearrange("p t i -> p (t i)").bitcast(I32))
-        for q in range(4):
-            nc.gpsimd.dma_start(t2_scales[32 * q:32 * q + 4, :].bitcast(I32),
-                                tab2_scales[0, 4 * q:4 * q + 4, :].bitcast(I32))
-        for q in range(4):
-            nc.gpsimd.dma_start(t1_scales[32 * q:32 * q + 8, :].bitcast(I32),
-                                tab_scales[:, 4 * q:4 * q + 4, :].bitcast(I32))
-        for q in range(4):
-            nc.gpsimd.dma_start(wf_sraw[32 * q:32 * q + 4, :, :].bitcast(I32),
-                                wf_scales[:, 4 * q:4 * q + 4, :].rearrange("a r c -> r a c").bitcast(I32))
+        def scale_rows(tile, dram):
+            for q in range(4):
+                nc.sync.dma_start(tile[32 * q:32 * q + 4, :, :].bitcast(I32),
+                                  dram[:, 4 * q:4 * q + 4, :].rearrange("a r c -> r a c").bitcast(I32))
 
-        g_flat = g[:].rearrange("p b t -> p (b t)")
-        g_neg = held([P, 8], F32, "g_neg")
-        g_safe = held([P, 8], F32, "g_safe")
-        g_inv = held([P, 8], F32, "g_inv")
-        nc.vector.tensor_scalar(g_neg[:], g_flat, -1.0, None, ALU.mult)
-        nc.vector.scalar_tensor_tensor(g_safe[:], g_flat, 0.0, g_flat, ALU.is_equal, ALU.add)
+        ws_v = ws.rearrange("(p j) c -> p j c", j=4)
+        def load_ws(u):
+            nc.sync.dma_start(ws_raw[u][:], ws_v[:, :, u * 256:(u + 1) * 256])
+
+        nc.sync.dma_start(list2[:], offs2)
+        for b in range(2):
+            nc.sync.dma_start(g[:, b, 0:4], gain[b * HALF:(b + 1) * HALF].rearrange("(p t) -> p t", t=4))
+        nc.sync.dma_start(list1[:], offs)
+        for u in range(2):
+            nc.sync.dma_start(t2_words[:, u * 2048:(u + 1) * 2048].bitcast(I32),
+                              tab2_words[0, :, u * 4096:(u + 1) * 4096].bitcast(I32))
+        nc.sync.dma_start(wf_raw[:].bitcast(I32), wf_words.rearrange("a p c -> p a c").bitcast(I32))
+        load_ws(0)
+        for q in range(4):
+            nc.sync.dma_start(t2_scales[32 * q:32 * q + 4, :].bitcast(I32),
+                              tab2_scales[0, 4 * q:4 * q + 4, :].bitcast(I32))
+        for u in range(1, 4):
+            load_ws(u)
+        t1s_v = tab_scales.rearrange("a (q r) c -> r q a c", r=4)
+        for r in range(4):
+            nc.sync.dma_start(t1_scales[r:P:16, :].bitcast(I32), t1s_v[r].bitcast(I32))
+        nc.sync.dma_start(t1_words[0][:], tab_words[0].rearrange("p t i -> p (t i)").bitcast(I32))
+        scale_rows(wf_sraw, wf_scales)
+        nc.sync.dma_start(t1_words[1][:], tab_words[1].rearrange("p t i -> p (t i)").bitcast(I32))
+
+        g_all = g[:, :, 0:4]
+        g_neg = held([P, 2, 4], F32, "g_neg")
+        g_safe = held([P, 2, 4], F32, "g_safe")
+        g_inv = held([P, 2, 4], F32, "g_inv")
+        nc.vector.tensor_scalar(g_neg[:], g_all, -1.0, None, ALU.mult)
+        nc.vector.scalar_tensor_tensor(g_safe[:], g_all, 0.0, g_all, ALU.is_equal, ALU.add)
         nc.vector.reciprocal(g_inv[:], g_safe[:])
 
         g2_w = [held([P, HALF], U16, "g2_w%d" % jh) for jh in range(2)]
@@ -100,8 +108,9 @@ def tile_list_transit_template_detrending_kernel(
         ws_sc = [held([P, HALF], U8, "ws_sc%d" % b) for b in range(2)]
         for b in range(2):
             ws_bf = work.tile([P, 4 * HALF], BF16, name="ws_bf", align_bytes=64)
-            nc.scalar.copy(ws_bf[:].rearrange("p (t m j) -> p m j t", t=4, j=4),
-                           ws_raw[b][:].rearrange("p j (m t) -> p m j t", t=4))
+            for u in range(2):
+                nc.scalar.copy(ws_bf[:].rearrange("p (t m j) -> p m j t", t=4, j=4)[:, 64 * u:64 * (u + 1)],
+                               ws_raw[2 * b + u][:].rearrange("p j (m t) -> p m j t", t=4))
             nc.vector.quantize_mx(ws_codes[b][:].bitcast(FP8X4), ws_sc[b][:], ws_bf[:])
 
         resid = [[held([P, 4, HALF], F32, "resid%d%d" % (jh, b)) for b in range(2)] for jh in range(2)]
@@ -116,17 +125,14 @@ def tile_list_transit_template_detrending_kernel(
 
         g1_s0 = held([P, S], U8, "g1_s0")
         nc.vector.tensor_copy(g1_s0[:], t1_scales[:].indirect(list1[:]))
-        nc.sync.dma_start(g1_s1[0:100, :].bitcast(I32), g1_s0[4:104, :].bitcast(I32))
+        nc.sync.dma_start(g1_s1[0:112, :].bitcast(I32), g1_s0[16:128, :].bitcast(I32))
         g1_s = (g1_s0, g1_s1)
 
+        wt_codes = held([P, 2, N], I32, "wt_codes", "mid")
         nc.sync.dma_start(wt_codes[:], wt_words.rearrange("a p c i -> p a (c i)").bitcast(I32))
-        for q in range(4):
-            nc.sync.dma_start(wt_sc[32 * q:32 * q + 4, :, :].bitcast(I32),
-                              wt_scales[:, 4 * q:4 * q + 4, :].rearrange("a r c -> r a c").bitcast(I32))
+        scale_rows(wt_sc, wt_scales)
         cat_v = cat.rearrange("(nt p) j -> p nt j", p=P)
         out_v = out.rearrange("(nt p) j -> p nt j", p=P)
-        for jh in range(2):
-            nc.sync.dma_start(cat_sb[jh][:], cat_v[:, :, jh * HALF:(jh + 1) * HALF])
 
         wf_codes = held([P, 2, H], U16, "wf_codes")
         wf_sc = held([P, 2, H], U8, "wf_sc")
@@ -136,10 +142,16 @@ def tile_list_transit_template_detrending_kernel(
                               wf_sraw[:].rearrange("p a (b m t) -> p (a b) m t", b=2, t=4))
 
         g1_w = [[held([P, HALF], U32, "g1_w%d%d" % (a, jh)) for jh in range(2)] for a in range(2)]
-        for a in range(2):
-            for jh in range(2):
-                cols = list1[:, jh * LIST_COLS:(jh + 1) * LIST_COLS]
-                nc.vector.tensor_copy(g1_w[a][jh][:], t1_words[a][:].bitcast(U32).indirect(cols))
+
+        def gather_pixels(a, jh):
+            cols = list1[:, jh * LIST_COLS:(jh + 1) * LIST_COLS]
+            nc.vector.tensor_copy(g1_w[a][jh][:], t1_words[a][:].bitcast(U32).indirect(cols))
+
+        cat_sb = []
+
+        def load_cat(jh):
+            cat_sb.append(held([P, 4, HALF], F32, "cat%d" % jh, "big%d" % jh))
+            nc.sync.dma_start(cat_sb[jh][:], cat_v[:, :, jh * HALF:(jh + 1) * HALF])
 
         h_codes = [[held([P, HALF], U32, "h_codes%d%d" % (jh, b)) for b in range(2)] for jh in range(2)]
         h_sc = [[held([P, HALF], U8, "h_sc%d%d" % (jh, b)) for b in range(2)] for jh in range(2)]
@@ -154,14 +166,14 @@ def tile_list_transit_template_detrending_kernel(
                                         rhs=g1_w[a][jh][:].bitcast(FP8X4), rhs_scale=g1_s[a][:, js],
                                         start=(a == 0), stop=(a == 1))
                 r = resid[jh][b][:, t, :]
-                nc.vector.scalar_tensor_tensor(r, acc[:], g_neg[:, 4 * b + t:4 * b + t + 1], r, ALU.mult, ALU.add)
+                nc.vector.scalar_tensor_tensor(r, acc[:], g_neg[:, b, t:t + 1], r, ALU.mult, ALU.add)
 
         def damp(jh, b, c0, w):
             cs = slice(c0, c0 + w)
             x = work.tile([P, 4, w], F32, name="x", align_bytes=64, bufs=3)
             for t in range(4):
                 nc.scalar.activation(x[:, t, :], resid[jh][b][:, t, cs], ACT.Square,
-                                     scale=g_inv[:, 4 * b + t:4 * b + t + 1])
+                                     scale=g_inv[:, b, t:t + 1])
             for t in range(4):
                 nc.scalar.activation(x[:, t, :], x[:, t, :], ACT.Abs_reciprocal_sqrt, bias=1.0)
             for t in range(4):
@@ -187,8 +199,14 @@ def tile_list_transit_template_detrending_kernel(
                 nc.vector.tensor_tensor(o, acc[:], o, ALU.add)
             nc.sync.dma_start(out_v[:, :, jh * HALF + c0:jh * HALF + c0 + w], cat_sb[jh][:, :, cs])
 
+        gather_pixels(0, 0)
+        gather_pixels(0, 1)
+        load_cat(0)
+        gather_pixels(1, 0)
         flux(0, 0)
         flux(0, 1)
+        gather_pixels(1, 1)
+        load_cat(1)
         damp(0, 0, 0, HALF)
         flux(1, 0)
         damp(0, 1, 0, HALF)

@@ -109,8 +109,8 @@ def tile_list_transit_template_detrending_kernel(
         for b in range(2):
             ws_bf = work.tile([P, 4 * HALF], BF16, name="ws_bf", align_bytes=64)
             for u in range(2):
-                nc.scalar.copy(ws_bf[:].rearrange("p (t m j) -> p m j t", t=4, j=4)[:, 64 * u:64 * (u + 1)],
-                               ws_raw[2 * b + u][:].rearrange("p j (m t) -> p m j t", t=4))
+                nc.scalar.copy(ws_bf[:].rearrange("p (s e m j) -> p s m j e", s=2, e=2, j=4)[:, :, 64 * u:64 * (u + 1)],
+                               ws_raw[2 * b + u][:].rearrange("p j (m s e) -> p s m j e", s=2, e=2))
             nc.vector.quantize_mx(ws_codes[b][:].bitcast(FP8X4), ws_sc[b][:], ws_bf[:])
 
         resid = [[held([P, 4, HALF], F32, "resid%d%d" % (jh, b)) for b in range(2)] for jh in range(2)]
@@ -136,10 +136,10 @@ def tile_list_transit_template_detrending_kernel(
 
         wf_codes = held([P, 2, H], U16, "wf_codes")
         wf_sc = held([P, 2, H], U8, "wf_sc")
-        nc.vector.tensor_copy(wf_codes[:].rearrange("p a (b t m) -> p (a b) m t", b=2, t=4),
-                              wf_raw[:].rearrange("p a (b m t) -> p (a b) m t", b=2, t=4))
-        nc.vector.tensor_copy(wf_sc[:].rearrange("p a (b t m) -> p (a b) m t", b=2, t=4),
-                              wf_sraw[:].rearrange("p a (b m t) -> p (a b) m t", b=2, t=4))
+        nc.vector.tensor_copy(wf_codes[:].rearrange("p a (b t m) -> p (a b) t m", b=2, t=4),
+                              wf_raw[:].rearrange("p a (b m t) -> p (a b) t m", b=2, t=4))
+        nc.vector.tensor_copy(wf_sc[:].rearrange("p a (b t m) -> p (a b) t m", b=2, t=4),
+                              wf_sraw[:].rearrange("p a (b m t) -> p (a b) t m", b=2, t=4))
 
         g1_w = [[held([P, HALF], U32, "g1_w%d%d" % (a, jh)) for jh in range(2)] for a in range(2)]
 
@@ -179,9 +179,9 @@ def tile_list_transit_template_detrending_kernel(
             for t in range(4):
                 nc.scalar.activation(x[:, t, :], x[:, t, :], ACT.Square)
             h = work.tile([P, 4 * w], BF16, name="h", align_bytes=64)
-            nc.vector.tensor_tensor(h[:].rearrange("p (c i t) -> p c t i", i=4, t=4),
-                                    resid[jh][b][:, :, cs].rearrange("p t (c i) -> p c t i", i=4),
-                                    x[:].rearrange("p t (c i) -> p c t i", i=4), ALU.mult)
+            nc.vector.tensor_tensor(h[:].rearrange("p (c i t) -> p c t i", i=2, t=4),
+                                    resid[jh][b][:, :, cs].rearrange("p t (c i) -> p c t i", i=2),
+                                    x[:].rearrange("p t (c i) -> p c t i", i=2), ALU.mult)
             nc.vector.quantize_mx(h_codes[jh][b][:, cs].bitcast(FP8X4), h_sc[jh][b][:, cs], h[:])
 
         def project(jh, c0, w):

@@ -42,32 +42,29 @@ def tile_list_transit_template_detrending_kernel(
         t2_scales = held([P, T], U8, "t2_scales")
         t1_words = [held([P, T], I32, "t1_words%d" % a, "big%d" % a) for a in range(2)]
         t1_scales = held([P, T], U8, "t1_scales", "mid")
-        ws_raw = [held([P, 4, 256], F32, "ws_raw%d" % u) for u in range(4)]
+        ws_raw = [held([P, 4, HALF], F32, "ws_raw%d" % b) for b in range(2)]
         wf_raw = held([P, 2, H], U16, "wf_raw")
-        wf_sraw = held([P, 2, H], U8, "wf_sraw")
-        wt_sc = held([P, 2, N], U8, "wt_sc")
+        wf_sraw = held([P, 2 * H], U8, "wf_sraw")
+        wt_sc = held([P, 2 * N], U8, "wt_sc")
         g = held([P, 2, 8], F32, "g")
-        g1_s1 = held([P, S], U8, "g1_s1")
+        g1_s = held([P, 2, S], U8, "g1_s")
         warm = held([P, 16], F32, "warm")
 
         nc.vector.memset(t2_scales[:].bitcast(I32), 0)
         nc.vector.memset(warm[:], 1.0)
         nc.vector.memset(t1_scales[:].bitcast(I32), 0)
-        nc.vector.memset(wf_sraw[:].rearrange("p a c -> p (a c)").bitcast(I32), 0)
-        nc.vector.memset(wt_sc[:].rearrange("p a c -> p (a c)").bitcast(I32), 0)
-        nc.vector.memset(g1_s1[:].bitcast(I32), 0)
+        nc.vector.memset(wf_sraw[:].bitcast(I32), 0)
+        nc.vector.memset(wt_sc[:].bitcast(I32), 0)
+        nc.vector.memset(g1_s[:].rearrange("p a c -> p (a c)").bitcast(I32), 0)
         warm_out = held([P, 16], F32, "warm_out")
         nc.scalar.activation(warm_out[:], warm[:], ACT.Abs_reciprocal_sqrt)
 
         def scale_rows(tile, dram):
-            for q in range(4):
-                nc.sync.dma_start(tile[32 * q:32 * q + 4, :, :].bitcast(I32),
-                                  dram[:, 4 * q:4 * q + 4, :].rearrange("a r c -> r a c").bitcast(I32))
+            rows = dram.rearrange("a (q r) c -> r q a c", r=4)
+            for r in range(4):
+                nc.sync.dma_start(tile[r:P:32, :].bitcast(I32), rows[r].bitcast(I32))
 
         ws_v = ws.rearrange("(p j) c -> p j c", j=4)
-        def load_ws(u):
-            nc.sync.dma_start(ws_raw[u][:], ws_v[:, :, u * 256:(u + 1) * 256])
-
         nc.sync.dma_start(list2[:], offs2)
         for b in range(2):
             nc.sync.dma_start(g[:, b, 0:4], gain[b * HALF:(b + 1) * HALF].rearrange("(p t) -> p t", t=4))
@@ -75,16 +72,13 @@ def tile_list_transit_template_detrending_kernel(
         for u in range(2):
             nc.sync.dma_start(t2_words[:, u * 2048:(u + 1) * 2048].bitcast(I32),
                               tab2_words[0, :, u * 4096:(u + 1) * 4096].bitcast(I32))
+        nc.sync.dma_start(ws_raw[0][:], ws_v[:, :, 0:HALF])
         nc.sync.dma_start(wf_raw[:].bitcast(I32), wf_words.rearrange("a p c -> p a c").bitcast(I32))
-        load_ws(0)
-        for q in range(4):
-            nc.sync.dma_start(t2_scales[32 * q:32 * q + 4, :].bitcast(I32),
-                              tab2_scales[0, 4 * q:4 * q + 4, :].bitcast(I32))
-        for u in range(1, 4):
-            load_ws(u)
+        scale_rows(t2_scales, tab2_scales)
+        nc.sync.dma_start(ws_raw[1][:], ws_v[:, :, HALF:H])
         t1s_v = tab_scales.rearrange("a (q r) c -> r q a c", r=4)
         for r in range(4):
-            nc.sync.dma_start(t1_scales[r:P:16, :].bitcast(I32), t1s_v[r].bitcast(I32))
+            nc.gpsimd.dma_start(t1_scales[8 + r:P:16, :].bitcast(I32), t1s_v[r].bitcast(I32))
         nc.sync.dma_start(t1_words[0][:], tab_words[0].rearrange("p t i -> p (t i)").bitcast(I32))
         scale_rows(wf_sraw, wf_scales)
         nc.sync.dma_start(t1_words[1][:], tab_words[1].rearrange("p t i -> p (t i)").bitcast(I32))
@@ -108,9 +102,8 @@ def tile_list_transit_template_detrending_kernel(
         ws_sc = [held([P, HALF], U8, "ws_sc%d" % b) for b in range(2)]
         for b in range(2):
             ws_bf = work.tile([P, 4 * HALF], BF16, name="ws_bf", align_bytes=64)
-            for u in range(2):
-                nc.scalar.copy(ws_bf[:].rearrange("p (s e m j) -> p s m j e", s=2, e=2, j=4)[:, :, 64 * u:64 * (u + 1)],
-                               ws_raw[2 * b + u][:].rearrange("p j (m s e) -> p s m j e", s=2, e=2))
+            nc.scalar.copy(ws_bf[:].rearrange("p (s e m j) -> p s m j e", s=2, e=2, j=4),
+                           ws_raw[b][:].rearrange("p j (m s e) -> p s m j e", s=2, e=2))
             nc.vector.quantize_mx(ws_codes[b][:].bitcast(FP8X4), ws_sc[b][:], ws_bf[:])
 
         resid = [[held([P, 4, HALF], F32, "resid%d%d" % (jh, b)) for b in range(2)] for jh in range(2)]
@@ -123,10 +116,11 @@ def tile_list_transit_template_detrending_kernel(
                                         rhs=g2_w[jh][:].bitcast(FP4X4), rhs_scale=g2_s[jh][:], start=True, stop=True)
                     nc.scalar.activation(resid[jh][b][:, t, :], acc[:], ACT.Copy, scale=g[:, b, t:t + 1])
 
-        g1_s0 = held([P, S], U8, "g1_s0")
-        nc.vector.tensor_copy(g1_s0[:], t1_scales[:].indirect(list1[:]))
-        nc.sync.dma_start(g1_s1[0:112, :].bitcast(I32), g1_s0[16:128, :].bitcast(I32))
-        g1_s = (g1_s0, g1_s1)
+        g1_picked = held([P, S], U8, "g1_picked")
+        nc.vector.tensor_copy(g1_picked[:], t1_scales[:].indirect(list1[:]))
+        for a in range(2):
+            first = 8 + 16 * a
+            nc.gpsimd.dma_start(g1_s[0:104, a, :].bitcast(I32), g1_picked[first:first + 104, :].bitcast(I32))
 
         wt_codes = held([P, 2, N], I32, "wt_codes", "mid")
         nc.sync.dma_start(wt_codes[:], wt_words.rearrange("a p c i -> p a (c i)").bitcast(I32))
@@ -139,7 +133,7 @@ def tile_list_transit_template_detrending_kernel(
         nc.vector.tensor_copy(wf_codes[:].rearrange("p a (b t m) -> p (a b) t m", b=2, t=4),
                               wf_raw[:].rearrange("p a (b m t) -> p (a b) t m", b=2, t=4))
         nc.vector.tensor_copy(wf_sc[:].rearrange("p a (b t m) -> p (a b) t m", b=2, t=4),
-                              wf_sraw[:].rearrange("p a (b m t) -> p (a b) t m", b=2, t=4))
+                              wf_sraw[:].rearrange("p (ab m t) -> p ab t m", ab=4, t=4))
 
         g1_w = [[held([P, HALF], U32, "g1_w%d%d" % (a, jh)) for jh in range(2)] for a in range(2)]
 
@@ -163,7 +157,7 @@ def tile_list_transit_template_detrending_kernel(
                 m = slice(b * HALF + t * P, b * HALF + (t + 1) * P)
                 for a in range(2):
                     nc.tensor.matmul_mx(acc[:], lhsT=wf_codes[:, a, m].bitcast(FP4X4), lhsT_scale=wf_sc[:, a, m],
-                                        rhs=g1_w[a][jh][:].bitcast(FP8X4), rhs_scale=g1_s[a][:, js],
+                                        rhs=g1_w[a][jh][:].bitcast(FP8X4), rhs_scale=g1_s[:, a, js],
                                         start=(a == 0), stop=(a == 1))
                 r = resid[jh][b][:, t, :]
                 nc.vector.scalar_tensor_tensor(r, acc[:], g_neg[:, b, t:t + 1], r, ALU.mult, ALU.add)
@@ -192,7 +186,7 @@ def tile_list_transit_template_detrending_kernel(
                 for k in range(per_bank):
                     m = slice((n0 + k) * P, (n0 + k + 1) * P)
                     for b in range(2):
-                        nc.tensor.matmul_mx(acc[:, k, :], lhsT=wt_codes[:, b, m].bitcast(FP8X4), lhsT_scale=wt_sc[:, b, m],
+                        nc.tensor.matmul_mx(acc[:, k, :], lhsT=wt_codes[:, b, m].bitcast(FP8X4), lhsT_scale=wt_sc[:, b * N + (n0 + k) * P:b * N + (n0 + k + 1) * P],
                                             rhs=h_codes[jh][b][:, cs].bitcast(FP8X4), rhs_scale=h_sc[jh][b][:, cs],
                                             start=(b == 0), stop=(b == 1))
                 o = cat_sb[jh][:, n0:n0 + per_bank, cs]

@@ -17,9 +17,12 @@ ALU = mybir.AluOpType
 ACT = mybir.ActivationFunctionType
 
 P = 128
+PACK = 4
 HALF = 512
 LIST_COLS = HALF // 16
-LAST_PIECES = ((0, 256), (256, 128), (384, 128))
+SECOND = 16
+PIECES = ((0, 256), (256, 128))
+LAST_PIECE = (384, 128)
 
 
 def tile_list_transit_template_detrending_kernel(
@@ -30,183 +33,227 @@ def tile_list_transit_template_detrending_kernel(
     with ExitStack() as ctx:
         keep = ctx.enter_context(tc.tile_pool(name="keep", bufs=1))
         work = ctx.enter_context(tc.tile_pool(name="work", bufs=2))
-        ps1 = ctx.enter_context(tc.psum_pool(name="ps1", bufs=4))
-        ps2 = ctx.enter_context(tc.psum_pool(name="ps2", bufs=4))
+        banks_a = ctx.enter_context(tc.psum_pool(name="banks_a", bufs=4))
+        banks_b = ctx.enter_context(tc.psum_pool(name="banks_b", bufs=4))
 
         def held(shape, dtype, name, tag=""):
             return keep.tile(shape, dtype, name=name, tag=tag, align_bytes=64)
 
-        list1 = keep.tile([P, S // 16], U16, name="list1")
-        list2 = keep.tile([P, S // 16], U16, name="list2")
-        t2_words = held([P, T], U16, "t2_words")
-        t2_scales = held([P, T], U8, "t2_scales")
-        t1_words = [held([P, T], I32, "t1_words%d" % a, "big%d" % a) for a in range(2)]
-        t1_scales = held([P, T], U8, "t1_scales", "mid")
-        ws_raw = [held([P, 4, HALF], F32, "ws_raw%d" % b) for b in range(2)]
+        pix_list = keep.tile([P, S // 16], U16, name="pix_list")
+        eng_list = keep.tile([P, S // 16], U16, name="eng_list")
+        eng_words = held([P, T], U16, "eng_words")
+        eng_scales = held([P, T], U8, "eng_scales")
+        pix_words = [held([P, T], I32, "pix_words%d" % a, "table%d" % a) for a in range(2)]
+        pix_scales = held([P, T], U8, "pix_scales")
+        ws_raw = [held([P, PACK, HALF], F32, "ws_raw%d" % b) for b in range(2)]
         wf_raw = held([P, 2, H], U16, "wf_raw")
-        wf_sraw = held([P, 2 * H], U8, "wf_sraw")
-        wt_sc = held([P, 2 * N], U8, "wt_sc")
-        g = held([P, 2, 8], F32, "g")
-        g1_s = held([P, 2, S], U8, "g1_s")
-        warm = held([P, 16], F32, "warm")
+        wf_raw_scales = held([P, H], U8, "wf_raw_scales", "weight_scales")
+        gain_sb = held([P, 2, 8], F32, "gain_sb")
+        pix_picked_scales1 = held([P, S], U8, "pix_picked_scales1")
+        wf_scales1 = held([P, H], U8, "wf_scales1")
+        warm_in = held([P, 16], F32, "warm_in")
 
-        nc.vector.memset(t2_scales[:].bitcast(I32), 0)
-        nc.vector.memset(warm[:], 1.0)
-        nc.vector.memset(t1_scales[:].bitcast(I32), 0)
-        nc.vector.memset(wf_sraw[:].bitcast(I32), 0)
-        nc.vector.memset(wt_sc[:].bitcast(I32), 0)
-        nc.vector.memset(g1_s[:].rearrange("p a c -> p (a c)").bitcast(I32), 0)
+        nc.vector.memset(eng_scales[:].bitcast(I32), 0)
+        nc.vector.memset(warm_in[:], 1.0)
+        nc.vector.memset(pix_scales[:].bitcast(I32), 0)
+        nc.vector.memset(wf_raw_scales[:].bitcast(I32), 0)
+        nc.vector.memset(pix_picked_scales1[:].bitcast(I32), 0)
+        nc.vector.memset(wf_scales1[:].bitcast(I32), 0)
         warm_out = held([P, 16], F32, "warm_out")
-        nc.scalar.activation(warm_out[:], warm[:], ACT.Abs_reciprocal_sqrt)
+        nc.scalar.activation(warm_out[:], warm_in[:], ACT.Abs_reciprocal_sqrt)
 
-        def scale_rows(tile, dram):
-            rows = dram.rearrange("a (q r) c -> r q a c", r=4)
-            for r in range(4):
-                nc.sync.dma_start(tile[r:P:32, :].bitcast(I32), rows[r].bitcast(I32))
+        def load_scale_rows(tile, dram):
+            passes = dram.shape[0]
+            rows = dram.rearrange("a (q s) c -> s q a c", s=4)
+            for s in range(4):
+                nc.sync.dma_start(tile[s:P:32 // passes, :].bitcast(I32), rows[s].bitcast(I32))
 
-        ws_v = ws.rearrange("(p j) c -> p j c", j=4)
-        nc.sync.dma_start(list2[:], offs2)
+        def move_second_pass_rows(dst, src):
+            nc.sync.dma_start(dst[0:P - SECOND, :].bitcast(I32), src[SECOND:P, :].bitcast(I32))
+
+        def load_engineering(c0, c1):
+            nc.sync.dma_start(eng_words[:, c0:c1].bitcast(I32), tab2_words[0, :, 2 * c0:2 * c1].bitcast(I32))
+
+        def load_pixels(a):
+            nc.sync.dma_start(pix_words[a][:], tab_words[a].rearrange("p t i -> p (t i)").bitcast(I32))
+
+        ws_rows = ws.rearrange("(p i) c -> p i c", i=PACK)
+        nc.sync.dma_start(eng_list[:], offs2)
+        nc.sync.dma_start(pix_list[:], offs)
         for b in range(2):
-            nc.sync.dma_start(g[:, b, 0:4], gain[b * HALF:(b + 1) * HALF].rearrange("(p t) -> p t", t=4))
-        nc.sync.dma_start(list1[:], offs)
-        for u in range(2):
-            nc.sync.dma_start(t2_words[:, u * 2048:(u + 1) * 2048].bitcast(I32),
-                              tab2_words[0, :, u * 4096:(u + 1) * 4096].bitcast(I32))
-        nc.sync.dma_start(ws_raw[0][:], ws_v[:, :, 0:HALF])
+            nc.sync.dma_start(gain_sb[:, b, 0:PACK], gain[b * HALF:(b + 1) * HALF].rearrange("(p t) -> p t", t=PACK))
+        load_engineering(0, T // 4)
+        load_engineering(T // 4, T // 2)
+        load_engineering(T // 2, T)
+        nc.sync.dma_start(ws_raw[0][:], ws_rows[:, :, 0:HALF])
+        load_scale_rows(eng_scales, tab2_scales)
+        nc.sync.dma_start(ws_raw[1][:], ws_rows[:, :, HALF:H])
         nc.sync.dma_start(wf_raw[:].bitcast(I32), wf_words.rearrange("a p c -> p a c").bitcast(I32))
-        scale_rows(t2_scales, tab2_scales)
-        nc.sync.dma_start(ws_raw[1][:], ws_v[:, :, HALF:H])
-        t1s_v = tab_scales.rearrange("a (q r) c -> r q a c", r=4)
-        for r in range(4):
-            nc.gpsimd.dma_start(t1_scales[8 + r:P:16, :].bitcast(I32), t1s_v[r].bitcast(I32))
-        nc.sync.dma_start(t1_words[0][:], tab_words[0].rearrange("p t i -> p (t i)").bitcast(I32))
-        scale_rows(wf_sraw, wf_scales)
-        nc.sync.dma_start(t1_words[1][:], tab_words[1].rearrange("p t i -> p (t i)").bitcast(I32))
+        load_scale_rows(pix_scales, tab_scales)
+        load_pixels(0)
+        load_scale_rows(wf_raw_scales, wf_scales)
+        load_pixels(1)
 
-        g_all = g[:, :, 0:4]
-        g_neg = held([P, 2, 4], F32, "g_neg")
-        g_safe = held([P, 2, 4], F32, "g_safe")
-        g_inv = held([P, 2, 4], F32, "g_inv")
-        nc.vector.tensor_scalar(g_neg[:], g_all, -1.0, None, ALU.mult)
-        nc.vector.scalar_tensor_tensor(g_safe[:], g_all, 0.0, g_all, ALU.is_equal, ALU.add)
-        nc.vector.reciprocal(g_inv[:], g_safe[:])
-
-        g2_w = [held([P, HALF], U16, "g2_w%d" % jh) for jh in range(2)]
-        g2_s = [held([P, HALF], U8, "g2_s%d" % jh) for jh in range(2)]
-        for jh in range(2):
-            cols = list2[:, jh * LIST_COLS:(jh + 1) * LIST_COLS]
-            nc.vector.tensor_copy(g2_w[jh][:], t2_words[:].indirect(cols))
-            nc.vector.tensor_copy(g2_s[jh][:], t2_scales[:].indirect(cols))
+        gain_all = gain_sb[:, :, 0:PACK]
+        gain_neg = held([P, 2, PACK], F32, "gain_neg")
+        gain_safe = held([P, 2, PACK], F32, "gain_safe")
+        gain_inv = held([P, 2, PACK], F32, "gain_inv")
+        nc.vector.tensor_scalar(gain_neg[:], gain_all, -1.0, None, ALU.mult)
+        nc.vector.scalar_tensor_tensor(gain_safe[:], gain_all, 0.0, gain_all, ALU.is_equal, ALU.add)
+        nc.vector.reciprocal(gain_inv[:], gain_safe[:])
 
         ws_codes = [held([P, HALF], U32, "ws_codes%d" % b) for b in range(2)]
-        ws_sc = [held([P, HALF], U8, "ws_sc%d" % b) for b in range(2)]
-        for b in range(2):
-            ws_bf = work.tile([P, 4 * HALF], BF16, name="ws_bf", align_bytes=64)
-            nc.scalar.copy(ws_bf[:].rearrange("p (s e m j) -> p s m j e", s=2, e=2, j=4),
-                           ws_raw[b][:].rearrange("p j (m s e) -> p s m j e", s=2, e=2))
-            nc.vector.quantize_mx(ws_codes[b][:].bitcast(FP8X4), ws_sc[b][:], ws_bf[:])
+        ws_scales = [held([P, HALF], U8, "ws_scales%d" % b) for b in range(2)]
+        eng_picked = [held([P, HALF], U16, "eng_picked%d" % jh) for jh in range(2)]
+        eng_picked_scales = [held([P, HALF], U8, "eng_picked_scales%d" % jh) for jh in range(2)]
+        resid = [[held([P, PACK, HALF], F32, "resid%d%d" % (jh, b)) for b in range(2)] for jh in range(2)]
 
-        resid = [[held([P, 4, HALF], F32, "resid%d%d" % (jh, b)) for b in range(2)] for jh in range(2)]
-        for b in range(2):
+        def quantise_ws(b, copy):
+            ws_bf = work.tile([P, PACK * HALF], BF16, name="ws_bf", align_bytes=64)
+            copy(ws_bf[:].rearrange("p (u e m i) -> p u m i e", u=2, e=2, i=PACK),
+                 ws_raw[b][:].rearrange("p i (m u e) -> p u m i e", u=2, e=2))
+            nc.vector.quantize_mx(ws_codes[b][:].bitcast(FP8X4), ws_scales[b][:], ws_bf[:])
+
+        def systematics(b):
             for jh in range(2):
-                for t in range(4):
-                    acc = ps1.tile([P, HALF], F32, name="acc1")
-                    m = slice(t * P, (t + 1) * P)
-                    nc.tensor.matmul_mx(acc[:], lhsT=ws_codes[b][:, m].bitcast(FP8X4), lhsT_scale=ws_sc[b][:, m],
-                                        rhs=g2_w[jh][:].bitcast(FP4X4), rhs_scale=g2_s[jh][:], start=True, stop=True)
-                    nc.scalar.activation(resid[jh][b][:, t, :], acc[:], ACT.Copy, scale=g[:, b, t:t + 1])
+                for t in range(PACK):
+                    acc = banks_a.tile([P, HALF], F32, name="acc_a")
+                    cols = slice(t * P, (t + 1) * P)
+                    nc.tensor.matmul_mx(acc[:], lhsT=ws_codes[b][:, cols].bitcast(FP8X4),
+                                        lhsT_scale=ws_scales[b][:, cols],
+                                        rhs=eng_picked[jh][:].bitcast(FP4X4), rhs_scale=eng_picked_scales[jh][:],
+                                        start=True, stop=True)
+                    nc.scalar.activation(resid[jh][b][:, t, :], acc[:], ACT.Copy, scale=gain_sb[:, b, t:t + 1])
 
-        g1_picked = held([P, S], U8, "g1_picked")
-        nc.vector.tensor_copy(g1_picked[:], t1_scales[:].indirect(list1[:]))
-        for a in range(2):
-            first = 8 + 16 * a
-            nc.gpsimd.dma_start(g1_s[0:104, a, :].bitcast(I32), g1_picked[first:first + 104, :].bitcast(I32))
+        quantise_ws(0, nc.scalar.copy)
+        for jh in range(2):
+            entries = eng_list[:, jh * LIST_COLS:(jh + 1) * LIST_COLS]
+            nc.vector.tensor_copy(eng_picked[jh][:], eng_words[:].indirect(entries))
+            nc.vector.tensor_copy(eng_picked_scales[jh][:], eng_scales[:].indirect(entries))
+        systematics(0)
+        quantise_ws(1, nc.vector.tensor_copy)
+        systematics(1)
 
-        wt_codes = held([P, 2, N], I32, "wt_codes", "mid")
-        nc.sync.dma_start(wt_codes[:], wt_words.rearrange("a p c i -> p a (c i)").bitcast(I32))
-        scale_rows(wt_sc, wt_scales)
-        cat_v = cat.rearrange("(nt p) j -> p nt j", p=P)
-        out_v = out.rearrange("(nt p) j -> p nt j", p=P)
+        pix_picked_scales0 = held([P, S], U8, "pix_picked_scales0")
+        nc.vector.tensor_copy(pix_picked_scales0[:], pix_scales[:].indirect(pix_list[:]))
+        move_second_pass_rows(pix_picked_scales1, pix_picked_scales0)
+        pix_picked_scales = (pix_picked_scales0, pix_picked_scales1)
 
         wf_codes = held([P, 2, H], U16, "wf_codes")
-        wf_sc = held([P, 2, H], U8, "wf_sc")
-        nc.vector.tensor_copy(wf_codes[:].rearrange("p a (b t m) -> p (a b) t m", b=2, t=4),
-                              wf_raw[:].rearrange("p a (b m t) -> p (a b) t m", b=2, t=4))
-        nc.vector.tensor_copy(wf_sc[:].rearrange("p a (b t m) -> p (a b) t m", b=2, t=4),
-                              wf_sraw[:].rearrange("p (ab m t) -> p ab t m", ab=4, t=4))
+        wf_scales0 = held([P, H], U8, "wf_scales0")
+        nc.vector.tensor_copy(wf_codes[:].rearrange("p a (b t m) -> p (a b) t m", b=2, t=PACK),
+                              wf_raw[:].rearrange("p a (b m t) -> p (a b) t m", b=2, t=PACK))
+        nc.vector.tensor_copy(wf_scales0[:].rearrange("p (b t m) -> p b t m", b=2, t=PACK),
+                              wf_raw_scales[:].rearrange("p (b m t) -> p b t m", b=2, t=PACK))
+        move_second_pass_rows(wf_scales1, wf_scales0)
+        wf_scales_sb = (wf_scales0, wf_scales1)
 
-        g1_w = [[held([P, HALF], U32, "g1_w%d%d" % (a, jh)) for jh in range(2)] for a in range(2)]
+        wt_scales_sb = held([P, 2 * N], U8, "wt_scales_sb", "weight_scales")
+        nc.vector.memset(wt_scales_sb[:].bitcast(I32), 0)
+        for q in range(4):
+            nc.sync.dma_start(wt_scales_sb[32 * q:32 * q + 4, :].rearrange("s (b c) -> s b c", b=2).bitcast(I32),
+                              wt_scales[:, 4 * q:4 * q + 4, :].rearrange("b s c -> s b c").bitcast(I32))
+
+        pix_picked = [[held([P, HALF], U32, "pix_picked%d%d" % (a, jh)) for jh in range(2)] for a in range(2)]
+        h_codes = [[held([P, HALF], U32, "h_codes%d%d" % (jh, b)) for b in range(2)] for jh in range(2)]
+        h_scales = [[held([P, HALF], U8, "h_scales%d%d" % (jh, b)) for b in range(2)] for jh in range(2)]
+        out_rows = out.rearrange("(nt p) j -> p nt j", p=P)
 
         def gather_pixels(a, jh):
-            cols = list1[:, jh * LIST_COLS:(jh + 1) * LIST_COLS]
-            nc.vector.tensor_copy(g1_w[a][jh][:], t1_words[a][:].bitcast(U32).indirect(cols))
+            entries = pix_list[:, jh * LIST_COLS:(jh + 1) * LIST_COLS]
+            nc.vector.tensor_copy(pix_picked[a][jh][:], pix_words[a][:].bitcast(U32).indirect(entries))
 
-        cat_sb = []
+        def flux_pass(acc, jh, b, t, a):
+            cols = slice(b * HALF + t * P, b * HALF + (t + 1) * P)
+            nc.tensor.matmul_mx(acc[:], lhsT=wf_codes[:, a, cols].bitcast(FP4X4), lhsT_scale=wf_scales_sb[a][:, cols],
+                                rhs=pix_picked[a][jh][:].bitcast(FP8X4),
+                                rhs_scale=pix_picked_scales[a][:, jh * HALF:(jh + 1) * HALF],
+                                start=(a == 0), stop=(a == 1))
 
-        def load_cat(jh):
-            cat_sb.append(held([P, 4, HALF], F32, "cat%d" % jh, "big%d" % jh))
-            nc.sync.dma_start(cat_sb[jh][:], cat_v[:, :, jh * HALF:(jh + 1) * HALF])
-
-        h_codes = [[held([P, HALF], U32, "h_codes%d%d" % (jh, b)) for b in range(2)] for jh in range(2)]
-        h_sc = [[held([P, HALF], U8, "h_sc%d%d" % (jh, b)) for b in range(2)] for jh in range(2)]
+        def subtract_flux(acc, jh, b, t):
+            tile = resid[jh][b][:, t, :]
+            nc.vector.scalar_tensor_tensor(tile, acc[:], gain_neg[:, b, t:t + 1], tile, ALU.mult, ALU.add)
 
         def flux(jh, b):
-            js = slice(jh * HALF, (jh + 1) * HALF)
-            for t in range(4):
-                acc = ps1.tile([P, HALF], F32, name="acc1")
-                m = slice(b * HALF + t * P, b * HALF + (t + 1) * P)
+            for t in range(PACK):
+                acc = banks_a.tile([P, HALF], F32, name="acc_a")
                 for a in range(2):
-                    nc.tensor.matmul_mx(acc[:], lhsT=wf_codes[:, a, m].bitcast(FP4X4), lhsT_scale=wf_sc[:, a, m],
-                                        rhs=g1_w[a][jh][:].bitcast(FP8X4), rhs_scale=g1_s[:, a, js],
-                                        start=(a == 0), stop=(a == 1))
-                r = resid[jh][b][:, t, :]
-                nc.vector.scalar_tensor_tensor(r, acc[:], g_neg[:, b, t:t + 1], r, ALU.mult, ALU.add)
+                    flux_pass(acc, jh, b, t, a)
+                subtract_flux(acc, jh, b, t)
 
-        def damp(jh, b, c0, w):
-            cs = slice(c0, c0 + w)
-            x = work.tile([P, 4, w], F32, name="x", align_bytes=64, bufs=3)
-            for t in range(4):
-                nc.scalar.activation(x[:, t, :], resid[jh][b][:, t, cs], ACT.Square,
-                                     scale=g_inv[:, b, t:t + 1])
-            for t in range(4):
-                nc.scalar.activation(x[:, t, :], x[:, t, :], ACT.Abs_reciprocal_sqrt, bias=1.0)
-            for t in range(4):
-                nc.scalar.activation(x[:, t, :], x[:, t, :], ACT.Square)
-            h = work.tile([P, 4 * w], BF16, name="h", align_bytes=64)
-            nc.vector.tensor_tensor(h[:].rearrange("p (c i t) -> p c t i", i=2, t=4),
-                                    resid[jh][b][:, :, cs].rearrange("p t (c i) -> p c t i", i=2),
-                                    x[:].rearrange("p t (c i) -> p c t i", i=2), ALU.mult)
-            nc.vector.quantize_mx(h_codes[jh][b][:, cs].bitcast(FP8X4), h_sc[jh][b][:, cs], h[:])
+        def damp(jh, b, c0, width):
+            cols = slice(c0, c0 + width)
+            weight = work.tile([P, PACK, width], F32, name="weight", align_bytes=64, bufs=3)
+            for t in range(PACK):
+                nc.scalar.activation(weight[:, t, :], resid[jh][b][:, t, cols], ACT.Square,
+                                     scale=gain_inv[:, b, t:t + 1])
+            for t in (0, 2):
+                nc.scalar.activation(weight[:, t:t + 2, :], weight[:, t:t + 2, :], ACT.Abs_reciprocal_sqrt, bias=1.0)
+            for t in (0, 2):
+                nc.scalar.activation(weight[:, t:t + 2, :], weight[:, t:t + 2, :], ACT.Square)
+            h = work.tile([P, PACK * width], BF16, name="h", align_bytes=64)
+            nc.vector.tensor_tensor(h[:].rearrange("p (c e t) -> p c t e", e=2, t=PACK),
+                                    resid[jh][b][:, :, cols].rearrange("p t (c e) -> p c t e", e=2),
+                                    weight[:].rearrange("p t (c e) -> p c t e", e=2), ALU.mult)
+            nc.vector.quantize_mx(h_codes[jh][b][:, cols].bitcast(FP8X4), h_scales[jh][b][:, cols], h[:])
 
-        def project(jh, c0, w):
-            cs = slice(c0, c0 + w)
-            per_bank = HALF // w
-            for n0 in range(0, 4, per_bank):
-                acc = ps2.tile([P, per_bank, w], F32, name="acc2")
+        def template_pass(acc, jh, c0, width, nt, b):
+            cols = slice(c0, c0 + width)
+            nc.tensor.matmul_mx(acc, lhsT=wt_codes[:, b, nt * P:(nt + 1) * P].bitcast(FP8X4),
+                                lhsT_scale=wt_scales_sb[:, b * N + nt * P:b * N + (nt + 1) * P],
+                                rhs=h_codes[jh][b][:, cols].bitcast(FP8X4), rhs_scale=h_scales[jh][b][:, cols],
+                                start=(b == 0), stop=(b == 1))
+
+        def add_catalogue(acc, jh, c0, width, nt0, nt1):
+            scores = cat_sb[:, nt0:nt1, jh * HALF + c0:jh * HALF + c0 + width]
+            nc.vector.tensor_tensor(scores, acc, scores, ALU.add)
+
+        def store(jh, c0, width):
+            entries = slice(jh * HALF + c0, jh * HALF + c0 + width)
+            nc.sync.dma_start(out_rows[:, :, entries], cat_sb[:, :, entries])
+
+        def project(jh, c0, width):
+            per_bank = HALF // width
+            for nt0 in range(0, N // P, per_bank):
+                acc = banks_b.tile([P, per_bank, width], F32, name="acc_b")
                 for k in range(per_bank):
-                    m = slice((n0 + k) * P, (n0 + k + 1) * P)
                     for b in range(2):
-                        nc.tensor.matmul_mx(acc[:, k, :], lhsT=wt_codes[:, b, m].bitcast(FP8X4), lhsT_scale=wt_sc[:, b * N + (n0 + k) * P:b * N + (n0 + k + 1) * P],
-                                            rhs=h_codes[jh][b][:, cs].bitcast(FP8X4), rhs_scale=h_sc[jh][b][:, cs],
-                                            start=(b == 0), stop=(b == 1))
-                o = cat_sb[jh][:, n0:n0 + per_bank, cs]
-                nc.vector.tensor_tensor(o, acc[:], o, ALU.add)
-            nc.sync.dma_start(out_v[:, :, jh * HALF + c0:jh * HALF + c0 + w], cat_sb[jh][:, :, cs])
+                        template_pass(acc[:, k, :], jh, c0, width, nt0 + k, b)
+                add_catalogue(acc[:], jh, c0, width, nt0, nt0 + per_bank)
+            store(jh, c0, width)
 
+        first = [banks_b.tile([P, HALF], F32, name="acc_b") for t in range(PACK)]
         gather_pixels(0, 0)
-        gather_pixels(0, 1)
-        load_cat(0)
+        for t in range(PACK):
+            flux_pass(first[t], 0, 0, t, 0)
         gather_pixels(1, 0)
-        flux(0, 0)
+        for t in range(PACK):
+            flux_pass(first[t], 0, 0, t, 1)
+            subtract_flux(first[t], 0, 0, t)
+        gather_pixels(0, 1)
+        wt_codes = held([P, 2, N], I32, "wt_codes", "table0")
+        nc.sync.dma_start(wt_codes[:], wt_words.rearrange("b p c i -> p b (c i)").bitcast(I32))
         flux(0, 1)
         gather_pixels(1, 1)
-        load_cat(1)
+        cat_sb = held([P, N // P, S], F32, "cat_sb", "table1")
+        nc.sync.dma_start(cat_sb[:], cat.rearrange("(nt p) j -> p nt j", p=P))
         damp(0, 0, 0, HALF)
         flux(1, 0)
         damp(0, 1, 0, HALF)
         flux(1, 1)
         project(0, 0, HALF)
-        damp(1, 0, 0, HALF)
-        for c0, w in LAST_PIECES:
-            damp(1, 1, c0, w)
-            project(1, c0, w)
+        for c0, width in PIECES:
+            damp(1, 0, c0, width)
+            damp(1, 1, c0, width)
+            project(1, c0, width)
+
+        c0, width = LAST_PIECE
+        last = [banks_a.tile([P, 1, width], F32, name="acc_a") for nt in range(N // P)]
+        damp(1, 0, c0, width)
+        for nt in range(N // P):
+            template_pass(last[nt][:, 0, :], 1, c0, width, nt, 0)
+        damp(1, 1, c0, width)
+        for nt in range(N // P):
+            template_pass(last[nt][:, 0, :], 1, c0, width, nt, 1)
+            add_catalogue(last[nt][:], 1, c0, width, nt, nt + 1)
+        store(1, c0, width)

@@ -33,8 +33,10 @@ def tile_list_transit_template_detrending_kernel(
     with ExitStack() as ctx:
         keep = ctx.enter_context(tc.tile_pool(name="keep", bufs=1))
         work = ctx.enter_context(tc.tile_pool(name="work", bufs=2))
-        banks_a = ctx.enter_context(tc.psum_pool(name="banks_a", bufs=4))
-        banks_b = ctx.enter_context(tc.psum_pool(name="banks_b", bufs=4))
+        banks = ctx.enter_context(tc.psum_pool(name="banks", bufs=1))
+
+        def bank(k, shape):
+            return banks.tile(shape, F32, name="bank%d" % k)
 
         def held(shape, dtype, name, tag=""):
             return keep.tile(shape, dtype, name=name, tag=tag, align_bytes=64)
@@ -88,8 +90,8 @@ def tile_list_transit_template_detrending_kernel(
         nc.sync.dma_start(ws_raw[0][:], ws_rows[:, :, 0:HALF])
         load_scale_rows(eng_scales, tab2_scales)
         nc.sync.dma_start(ws_raw[1][:], ws_rows[:, :, HALF:H])
-        nc.sync.dma_start(wf_raw[:].bitcast(I32), wf_words.rearrange("a p c -> p a c").bitcast(I32))
         load_scale_rows(pix_scales, tab_scales)
+        nc.sync.dma_start(wf_raw[:].bitcast(I32), wf_words.rearrange("a p c -> p a c").bitcast(I32))
         load_pixels(0)
         load_scale_rows(wf_raw_scales, wf_scales)
         load_pixels(1)
@@ -108,16 +110,23 @@ def tile_list_transit_template_detrending_kernel(
         eng_picked_scales = [held([P, HALF], U8, "eng_picked_scales%d" % jh) for jh in range(2)]
         resid = [[held([P, PACK, HALF], F32, "resid%d%d" % (jh, b)) for b in range(2)] for jh in range(2)]
 
-        def quantise_ws(b, copy):
+        def round_on_scalar(ws_bf, raw):
+            nc.scalar.copy(ws_bf.rearrange("p (u e m i) -> p u m i e", u=2, e=2, i=PACK),
+                           raw.rearrange("p i (m u e) -> p u m i e", u=2, e=2))
+
+        def round_on_gpsimd(ws_bf, raw):
+            nc.gpsimd.tensor_scalar(ws_bf.rearrange("p (t m i) -> p t m i", t=PACK, i=PACK),
+                                    raw.rearrange("p i (m t) -> p t m i", t=PACK), 1.0, 0.0, ALU.mult, ALU.add)
+
+        def quantise_ws(b, round_ws):
             ws_bf = work.tile([P, PACK * HALF], BF16, name="ws_bf", align_bytes=64)
-            copy(ws_bf[:].rearrange("p (u e m i) -> p u m i e", u=2, e=2, i=PACK),
-                 ws_raw[b][:].rearrange("p i (m u e) -> p u m i e", u=2, e=2))
+            round_ws(ws_bf[:], ws_raw[b][:])
             nc.vector.quantize_mx(ws_codes[b][:].bitcast(FP8X4), ws_scales[b][:], ws_bf[:])
 
         def systematics(b):
             for jh in range(2):
                 for t in range(PACK):
-                    acc = banks_a.tile([P, HALF], F32, name="acc_a")
+                    acc = bank(jh * PACK + t, [P, HALF])
                     cols = slice(t * P, (t + 1) * P)
                     nc.tensor.matmul_mx(acc[:], lhsT=ws_codes[b][:, cols].bitcast(FP8X4),
                                         lhsT_scale=ws_scales[b][:, cols],
@@ -125,13 +134,13 @@ def tile_list_transit_template_detrending_kernel(
                                         start=True, stop=True)
                     nc.scalar.activation(resid[jh][b][:, t, :], acc[:], ACT.Copy, scale=gain_sb[:, b, t:t + 1])
 
-        quantise_ws(0, nc.scalar.copy)
+        quantise_ws(0, round_on_scalar)
         for jh in range(2):
             entries = eng_list[:, jh * LIST_COLS:(jh + 1) * LIST_COLS]
             nc.vector.tensor_copy(eng_picked[jh][:], eng_words[:].indirect(entries))
             nc.vector.tensor_copy(eng_picked_scales[jh][:], eng_scales[:].indirect(entries))
         systematics(0)
-        quantise_ws(1, nc.vector.tensor_copy)
+        quantise_ws(1, round_on_gpsimd)
         systematics(1)
 
         pix_picked_scales0 = held([P, S], U8, "pix_picked_scales0")
@@ -176,7 +185,7 @@ def tile_list_transit_template_detrending_kernel(
 
         def flux(jh, b):
             for t in range(PACK):
-                acc = banks_a.tile([P, HALF], F32, name="acc_a")
+                acc = bank(b * PACK + t, [P, HALF])
                 for a in range(2):
                     flux_pass(acc, jh, b, t, a)
                 subtract_flux(acc, jh, b, t)
@@ -197,12 +206,12 @@ def tile_list_transit_template_detrending_kernel(
                                     weight[:].rearrange("p t (c e) -> p c t e", e=2), ALU.mult)
             nc.vector.quantize_mx(h_codes[jh][b][:, cols].bitcast(FP8X4), h_scales[jh][b][:, cols], h[:])
 
-        def template_pass(acc, jh, c0, width, nt, b):
+        def template_pass(acc, jh, c0, width, nt, b, start, stop):
             cols = slice(c0, c0 + width)
             nc.tensor.matmul_mx(acc, lhsT=wt_codes[:, b, nt * P:(nt + 1) * P].bitcast(FP8X4),
                                 lhsT_scale=wt_scales_sb[:, b * N + nt * P:b * N + (nt + 1) * P],
                                 rhs=h_codes[jh][b][:, cols].bitcast(FP8X4), rhs_scale=h_scales[jh][b][:, cols],
-                                start=(b == 0), stop=(b == 1))
+                                start=start, stop=stop)
 
         def add_catalogue(acc, jh, c0, width, nt0, nt1):
             scores = cat_sb[:, nt0:nt1, jh * HALF + c0:jh * HALF + c0 + width]
@@ -212,17 +221,17 @@ def tile_list_transit_template_detrending_kernel(
             entries = slice(jh * HALF + c0, jh * HALF + c0 + width)
             nc.sync.dma_start(out_rows[:, :, entries], cat_sb[:, :, entries])
 
-        def project(jh, c0, width):
+        def project(jh, c0, width, bank0):
             per_bank = HALF // width
             for nt0 in range(0, N // P, per_bank):
-                acc = banks_b.tile([P, per_bank, width], F32, name="acc_b")
+                acc = bank(bank0 + nt0 // per_bank, [P, per_bank, width])
                 for k in range(per_bank):
                     for b in range(2):
-                        template_pass(acc[:, k, :], jh, c0, width, nt0 + k, b)
+                        template_pass(acc[:, k, :], jh, c0, width, nt0 + k, b, b == 0, b == 1)
                 add_catalogue(acc[:], jh, c0, width, nt0, nt0 + per_bank)
             store(jh, c0, width)
 
-        first = [banks_b.tile([P, HALF], F32, name="acc_b") for t in range(PACK)]
+        first = [bank(t, [P, HALF]) for t in range(PACK)]
         gather_pixels(0, 0)
         for t in range(PACK):
             flux_pass(first[t], 0, 0, t, 0)
@@ -241,19 +250,17 @@ def tile_list_transit_template_detrending_kernel(
         flux(1, 0)
         damp(0, 1, 0, HALF)
         flux(1, 1)
-        project(0, 0, HALF)
+        project(0, 0, HALF, 0)
         for c0, width in PIECES:
             damp(1, 0, c0, width)
             damp(1, 1, c0, width)
-            project(1, c0, width)
+            project(1, c0, width, PACK + c0 // P)
 
         c0, width = LAST_PIECE
-        last = [banks_a.tile([P, 1, width], F32, name="acc_a") for nt in range(N // P)]
-        damp(1, 0, c0, width)
-        for nt in range(N // P):
-            template_pass(last[nt][:, 0, :], 1, c0, width, nt, 0)
-        damp(1, 1, c0, width)
-        for nt in range(N // P):
-            template_pass(last[nt][:, 0, :], 1, c0, width, nt, 1)
-            add_catalogue(last[nt][:], 1, c0, width, nt, nt + 1)
+        last = bank(PACK + c0 // P, [P, N // P, width])
+        for b in range(2):
+            damp(1, b, c0, width)
+            for nt in range(N // P):
+                template_pass(last[:, nt, :], 1, c0, width, nt, b, b == 0 and nt == 0, b == 1 and nt == N // P - 1)
+        add_catalogue(last[:], 1, c0, width, 0, N // P)
         store(1, c0, width)

@@ -190,17 +190,26 @@ def tile_list_transit_template_detrending_kernel(
                     flux_pass(acc, jh, b, t, a)
                 subtract_flux(acc, jh, b, t)
 
-        def damp(jh, b, c0, width):
+        def square_on_scalar(x):
+            nc.scalar.activation(x, x, ACT.Square)
+
+        def square_on_vector(x):
+            nc.vector.tensor_tensor(x, x, x, ALU.mult)
+
+        def square_on_gpsimd(x):
+            nc.gpsimd.tensor_tensor(x, x, x, ALU.mult)
+
+        def damp(jh, b, c0, width, squares):
             cols = slice(c0, c0 + width)
-            weight = work.tile([P, PACK, width], F32, name="weight", align_bytes=64, bufs=3)
+            weight = held([P, PACK, width], F32, "weight%d%d_%d" % (jh, b, c0))
             for t in range(PACK):
                 nc.scalar.activation(weight[:, t, :], resid[jh][b][:, t, cols], ACT.Square,
                                      scale=gain_inv[:, b, t:t + 1])
             for t in (0, 2):
                 nc.scalar.activation(weight[:, t:t + 2, :], weight[:, t:t + 2, :], ACT.Abs_reciprocal_sqrt, bias=1.0)
-            for t in (0, 2):
-                nc.scalar.activation(weight[:, t:t + 2, :], weight[:, t:t + 2, :], ACT.Square)
-            h = work.tile([P, PACK * width], BF16, name="h", align_bytes=64)
+            for u in range(2):
+                squares[u](weight[:, 2 * u:2 * u + 2, :])
+            h = work.tile([P, PACK * width], BF16, name="h", align_bytes=64, bufs=3)
             nc.vector.tensor_tensor(h[:].rearrange("p (c e t) -> p c t e", e=2, t=PACK),
                                     resid[jh][b][:, :, cols].rearrange("p t (c e) -> p c t e", e=2),
                                     weight[:].rearrange("p t (c e) -> p c t e", e=2), ALU.mult)
@@ -246,20 +255,21 @@ def tile_list_transit_template_detrending_kernel(
         gather_pixels(1, 1)
         cat_sb = held([P, N // P, S], F32, "cat_sb", "table1")
         nc.sync.dma_start(cat_sb[:], cat.rearrange("(nt p) j -> p nt j", p=P))
-        damp(0, 0, 0, HALF)
+        damp(0, 0, 0, HALF, (square_on_gpsimd, square_on_gpsimd))
         flux(1, 0)
-        damp(0, 1, 0, HALF)
+        damp(0, 1, 0, HALF, (square_on_scalar, square_on_scalar))
         flux(1, 1)
         project(0, 0, HALF, 0)
         for c0, width in PIECES:
-            damp(1, 0, c0, width)
-            damp(1, 1, c0, width)
+            squares = (square_on_vector if width > P else square_on_scalar, square_on_scalar)
+            damp(1, 0, c0, width, squares)
+            damp(1, 1, c0, width, squares)
             project(1, c0, width, PACK + c0 // P)
 
         c0, width = LAST_PIECE
         last = bank(PACK + c0 // P, [P, N // P, width])
         for b in range(2):
-            damp(1, b, c0, width)
+            damp(1, b, c0, width, (square_on_scalar, square_on_scalar))
             for nt in range(N // P):
                 template_pass(last[:, nt, :], 1, c0, width, nt, b, b == 0 and nt == 0, b == 1 and nt == N // P - 1)
         add_catalogue(last[:], 1, c0, width, 0, N // P)

@@ -21,8 +21,7 @@ PACK = 4
 HALF = 512
 LIST_COLS = HALF // 16
 SECOND = 16
-PIECES = ((0, 256), (256, 128))
-LAST_PIECE = (384, 128)
+PIECES = ((0, 256), (256, 128), (384, 128))
 
 
 def tile_list_transit_template_detrending_kernel(
@@ -49,10 +48,9 @@ def tile_list_transit_template_detrending_kernel(
         pix_scales = held([P, T], U8, "pix_scales")
         ws_raw = [held([P, PACK, HALF], F32, "ws_raw%d" % b) for b in range(2)]
         wf_raw = held([P, 2, H], U16, "wf_raw")
-        wf_raw_scales = held([P, H], U8, "wf_raw_scales", "weight_scales")
+        wf_raw_scales = held([P, 2 * H], U8, "wf_raw_scales", "weight_scales")
         gain_sb = held([P, 2, 8], F32, "gain_sb")
         pix_picked_scales1 = held([P, S], U8, "pix_picked_scales1")
-        wf_scales1 = held([P, H], U8, "wf_scales1")
         warm_in = held([P, 16], F32, "warm_in")
 
         nc.vector.memset(eng_scales[:].bitcast(I32), 0)
@@ -60,7 +58,6 @@ def tile_list_transit_template_detrending_kernel(
         nc.vector.memset(pix_scales[:].bitcast(I32), 0)
         nc.vector.memset(wf_raw_scales[:].bitcast(I32), 0)
         nc.vector.memset(pix_picked_scales1[:].bitcast(I32), 0)
-        nc.vector.memset(wf_scales1[:].bitcast(I32), 0)
         warm_out = held([P, 16], F32, "warm_out")
         nc.scalar.activation(warm_out[:], warm_in[:], ACT.Abs_reciprocal_sqrt)
 
@@ -76,8 +73,8 @@ def tile_list_transit_template_detrending_kernel(
         def load_engineering(c0, c1):
             nc.sync.dma_start(eng_words[:, c0:c1].bitcast(I32), tab2_words[0, :, 2 * c0:2 * c1].bitcast(I32))
 
-        def load_pixels(a):
-            nc.sync.dma_start(pix_words[a][:], tab_words[a].rearrange("p t i -> p (t i)").bitcast(I32))
+        def load_pixels(a, c0, c1):
+            nc.sync.dma_start(pix_words[a][:, c0:c1], tab_words[a, :, c0:c1].rearrange("p t i -> p (t i)").bitcast(I32))
 
         ws_rows = ws.rearrange("(p i) c -> p i c", i=PACK)
         nc.sync.dma_start(eng_list[:], offs2)
@@ -92,9 +89,13 @@ def tile_list_transit_template_detrending_kernel(
         nc.sync.dma_start(ws_raw[1][:], ws_rows[:, :, HALF:H])
         load_scale_rows(pix_scales, tab_scales)
         nc.sync.dma_start(wf_raw[:].bitcast(I32), wf_words.rearrange("a p c -> p a c").bitcast(I32))
-        load_pixels(0)
-        load_scale_rows(wf_raw_scales, wf_scales)
-        load_pixels(1)
+        load_pixels(0, 0, T // 2)
+        wf_scale_rows = wf_scales.rearrange("a (q s) c -> s q a c", s=4)
+        for s in range(4):
+            nc.sync.dma_start(wf_raw_scales[s:P:32, :].rearrange("q (a c) -> q a c", a=2).bitcast(I32),
+                              wf_scale_rows[s].bitcast(I32))
+        load_pixels(0, T // 2, T)
+        load_pixels(1, 0, T)
 
         gain_all = gain_sb[:, :, 0:PACK]
         gain_neg = held([P, 2, PACK], F32, "gain_neg")
@@ -111,16 +112,17 @@ def tile_list_transit_template_detrending_kernel(
         resid = [[held([P, PACK, HALF], F32, "resid%d%d" % (jh, b)) for b in range(2)] for jh in range(2)]
 
         def round_on_scalar(ws_bf, raw):
-            nc.scalar.copy(ws_bf.rearrange("p (u e m i) -> p u m i e", u=2, e=2, i=PACK),
-                           raw.rearrange("p i (m u e) -> p u m i e", u=2, e=2))
+            nc.scalar.copy(ws_bf.rearrange("p (e m i) -> p m i e", e=2, i=PACK), raw.rearrange("p i m e -> p m i e"))
 
         def round_on_gpsimd(ws_bf, raw):
-            nc.gpsimd.tensor_scalar(ws_bf.rearrange("p (t m i) -> p t m i", t=PACK, i=PACK),
-                                    raw.rearrange("p i (m t) -> p t m i", t=PACK), 1.0, 0.0, ALU.mult, ALU.add)
+            nc.gpsimd.tensor_scalar(ws_bf.rearrange("p (e m i) -> p e m i", e=2, i=PACK),
+                                    raw.rearrange("p i m e -> p e m i"), 1.0, 0.0, ALU.mult, ALU.add)
 
-        def quantise_ws(b, round_ws):
+        def quantise_ws(b, rounds):
             ws_bf = work.tile([P, PACK * HALF], BF16, name="ws_bf", align_bytes=64)
-            round_ws(ws_bf[:], ws_raw[b][:])
+            for u in range(2):
+                rounds[u](ws_bf[:, u * 2 * HALF:(u + 1) * 2 * HALF],
+                          ws_raw[b][:].rearrange("p i (m t) -> p i m t", t=PACK)[:, :, :, 2 * u:2 * u + 2])
             nc.vector.quantize_mx(ws_codes[b][:].bitcast(FP8X4), ws_scales[b][:], ws_bf[:])
 
         def systematics(b):
@@ -134,13 +136,13 @@ def tile_list_transit_template_detrending_kernel(
                                         start=True, stop=True)
                     nc.scalar.activation(resid[jh][b][:, t, :], acc[:], ACT.Copy, scale=gain_sb[:, b, t:t + 1])
 
-        quantise_ws(0, round_on_scalar)
+        quantise_ws(0, (round_on_scalar, round_on_gpsimd))
         for jh in range(2):
             entries = eng_list[:, jh * LIST_COLS:(jh + 1) * LIST_COLS]
             nc.vector.tensor_copy(eng_picked[jh][:], eng_words[:].indirect(entries))
             nc.vector.tensor_copy(eng_picked_scales[jh][:], eng_scales[:].indirect(entries))
         systematics(0)
-        quantise_ws(1, round_on_gpsimd)
+        quantise_ws(1, (round_on_gpsimd, round_on_gpsimd))
         systematics(1)
 
         pix_picked_scales0 = held([P, S], U8, "pix_picked_scales0")
@@ -149,13 +151,11 @@ def tile_list_transit_template_detrending_kernel(
         pix_picked_scales = (pix_picked_scales0, pix_picked_scales1)
 
         wf_codes = held([P, 2, H], U16, "wf_codes")
-        wf_scales0 = held([P, H], U8, "wf_scales0")
+        wf_scales_sb = held([P, 2, H], U8, "wf_scales_sb")
         nc.vector.tensor_copy(wf_codes[:].rearrange("p a (b t m) -> p (a b) t m", b=2, t=PACK),
                               wf_raw[:].rearrange("p a (b m t) -> p (a b) t m", b=2, t=PACK))
-        nc.vector.tensor_copy(wf_scales0[:].rearrange("p (b t m) -> p b t m", b=2, t=PACK),
-                              wf_raw_scales[:].rearrange("p (b m t) -> p b t m", b=2, t=PACK))
-        move_second_pass_rows(wf_scales1, wf_scales0)
-        wf_scales_sb = (wf_scales0, wf_scales1)
+        nc.vector.tensor_copy(wf_scales_sb[:].rearrange("p a (b t m) -> p (a b) t m", b=2, t=PACK),
+                              wf_raw_scales[:].rearrange("p (ab m t) -> p ab t m", ab=4, t=PACK))
 
         wt_scales_sb = held([P, 2 * N], U8, "wt_scales_sb", "weight_scales")
         nc.vector.memset(wt_scales_sb[:].bitcast(I32), 0)
@@ -174,7 +174,7 @@ def tile_list_transit_template_detrending_kernel(
 
         def flux_pass(acc, jh, b, t, a):
             cols = slice(b * HALF + t * P, b * HALF + (t + 1) * P)
-            nc.tensor.matmul_mx(acc[:], lhsT=wf_codes[:, a, cols].bitcast(FP4X4), lhsT_scale=wf_scales_sb[a][:, cols],
+            nc.tensor.matmul_mx(acc[:], lhsT=wf_codes[:, a, cols].bitcast(FP4X4), lhsT_scale=wf_scales_sb[:, a, cols],
                                 rhs=pix_picked[a][jh][:].bitcast(FP8X4),
                                 rhs_scale=pix_picked_scales[a][:, jh * HALF:(jh + 1) * HALF],
                                 start=(a == 0), stop=(a == 1))
@@ -193,13 +193,10 @@ def tile_list_transit_template_detrending_kernel(
         def square_on_scalar(x):
             nc.scalar.activation(x, x, ACT.Square)
 
-        def square_on_vector(x):
-            nc.vector.tensor_tensor(x, x, x, ALU.mult)
-
         def square_on_gpsimd(x):
             nc.gpsimd.tensor_tensor(x, x, x, ALU.mult)
 
-        def damp(jh, b, c0, width, squares):
+        def damp(jh, b, c0, width, squares, h_tag=""):
             cols = slice(c0, c0 + width)
             weight = held([P, PACK, width], F32, "weight%d%d_%d" % (jh, b, c0))
             for t in range(PACK):
@@ -209,7 +206,8 @@ def tile_list_transit_template_detrending_kernel(
                 nc.scalar.activation(weight[:, t:t + 2, :], weight[:, t:t + 2, :], ACT.Abs_reciprocal_sqrt, bias=1.0)
             for u in range(2):
                 squares[u](weight[:, 2 * u:2 * u + 2, :])
-            h = work.tile([P, PACK * width], BF16, name="h", align_bytes=64, bufs=3)
+            h = (held([P, PACK * width], BF16, "h_last", h_tag) if h_tag
+                 else work.tile([P, PACK * width], BF16, name="h", align_bytes=64, bufs=3))
             nc.vector.tensor_tensor(h[:].rearrange("p (c e t) -> p c t e", e=2, t=PACK),
                                     resid[jh][b][:, :, cols].rearrange("p t (c e) -> p c t e", e=2),
                                     weight[:].rearrange("p t (c e) -> p c t e", e=2), ALU.mult)
@@ -230,14 +228,21 @@ def tile_list_transit_template_detrending_kernel(
             entries = slice(jh * HALF + c0, jh * HALF + c0 + width)
             nc.sync.dma_start(out_rows[:, :, entries], cat_sb[:, :, entries])
 
-        def project(jh, c0, width, bank0):
+        def template_sums(jh, c0, width, bank0):
             per_bank = HALF // width
-            for nt0 in range(0, N // P, per_bank):
-                acc = bank(bank0 + nt0 // per_bank, [P, per_bank, width])
-                for k in range(per_bank):
-                    for b in range(2):
-                        template_pass(acc[:, k, :], jh, c0, width, nt0 + k, b, b == 0, b == 1)
-                add_catalogue(acc[:], jh, c0, width, nt0, nt0 + per_bank)
+            return [bank(bank0 + k, [P, per_bank, width]) for k in range(N // P // per_bank)]
+
+        def template_passes(sums, jh, c0, width, b):
+            per_bank = HALF // width
+            for nt in range(N // P):
+                k = nt % per_bank
+                template_pass(sums[nt // per_bank][:, k, :], jh, c0, width, nt, b,
+                              b == 0 and k == 0, b == 1 and k == per_bank - 1)
+
+        def finish(sums, jh, c0, width):
+            per_bank = HALF // width
+            for k, acc in enumerate(sums):
+                add_catalogue(acc[:], jh, c0, width, k * per_bank, (k + 1) * per_bank)
             store(jh, c0, width)
 
         first = [bank(t, [P, HALF]) for t in range(PACK)]
@@ -259,18 +264,22 @@ def tile_list_transit_template_detrending_kernel(
         flux(1, 0)
         damp(0, 1, 0, HALF, (square_on_scalar, square_on_scalar))
         flux(1, 1)
-        project(0, 0, HALF, 0)
-        for c0, width in PIECES:
-            squares = (square_on_vector if width > P else square_on_scalar, square_on_scalar)
-            damp(1, 0, c0, width, squares)
-            damp(1, 1, c0, width, squares)
-            project(1, c0, width, PACK + c0 // P)
-
-        c0, width = LAST_PIECE
-        last = bank(PACK + c0 // P, [P, N // P, width])
+        sums = template_sums(0, 0, HALF, 0)
         for b in range(2):
-            damp(1, b, c0, width, (square_on_scalar, square_on_scalar))
-            for nt in range(N // P):
-                template_pass(last[:, nt, :], 1, c0, width, nt, b, b == 0 and nt == 0, b == 1 and nt == N // P - 1)
-        add_catalogue(last[:], 1, c0, width, 0, N // P)
-        store(1, c0, width)
+            template_passes(sums, 0, 0, HALF, b)
+        finish(sums, 0, 0, HALF)
+        damp(1, 0, 0, HALF, (square_on_gpsimd, square_on_scalar))
+        piece_sums = [template_sums(1, c0, width, PACK + c0 // P) for c0, width in PIECES]
+        for sums, (c0, width) in zip(piece_sums, PIECES):
+            template_passes(sums, 1, c0, width, 0)
+        for k, (c0, width) in enumerate(PIECES):
+            damp(1, 1, c0, width, (square_on_scalar, square_on_scalar), "last" if k == 2 else "")
+            template_passes(piece_sums[k], 1, c0, width, 1)
+            if k == 0:
+                finish(piece_sums[k], 1, c0, width)
+        c0, width = PIECES[1]
+        staged = held([P, N // P, width], F32, "staged", "last")
+        entries = slice(HALF + c0, HALF + c0 + width)
+        nc.vector.tensor_tensor(staged[:], piece_sums[1][0][:], cat_sb[:, :, entries], ALU.add)
+        nc.sync.dma_start(out_rows[:, :, entries], staged[:])
+        finish(piece_sums[2], 1, *PIECES[2])

@@ -31,6 +31,7 @@ def tile_list_transit_template_detrending_kernel(
     nc = tc.nc
     with ExitStack() as ctx:
         keep = ctx.enter_context(tc.tile_pool(name="keep", bufs=1))
+        shared = ctx.enter_context(tc.tile_pool(name="shared", bufs=1))
         work = ctx.enter_context(tc.tile_pool(name="work", bufs=2))
         banks = ctx.enter_context(tc.psum_pool(name="banks", bufs=1))
 
@@ -46,10 +47,11 @@ def tile_list_transit_template_detrending_kernel(
         eng_scales = held([P, T], U8, "eng_scales")
         pix_words = [held([P, T], I32, "pix_words%d" % a, "table%d" % a) for a in range(2)]
         pix_scales = held([P, T], U8, "pix_scales")
-        ws_raw = [held([P, PACK, HALF], F32, "ws_raw%d" % b) for b in range(2)]
+        ws_raw = [held([P, PACK, HALF], F32, "ws_raw0"),
+                  shared.tile([P, PACK, HALF], F32, name="ws_raw1", offset=2 * PACK * HALF)]
         wf_raw = held([P, 2, H], U16, "wf_raw")
         wf_raw_scales = held([P, 2 * H], U8, "wf_raw_scales", "weight_scales")
-        gain_sb = held([P, 2, 8], F32, "gain_sb")
+        gain_sb = held([P, 2, PACK], F32, "gain_sb")
         pix_picked_scales1 = held([P, S], U8, "pix_picked_scales1")
         warm_in = held([P, 16], F32, "warm_in")
 
@@ -79,14 +81,13 @@ def tile_list_transit_template_detrending_kernel(
         ws_rows = ws.rearrange("(p i) c -> p i c", i=PACK)
         nc.sync.dma_start(eng_list[:], offs2)
         nc.sync.dma_start(pix_list[:], offs)
-        for b in range(2):
-            nc.sync.dma_start(gain_sb[:, b, 0:PACK], gain[b * HALF:(b + 1) * HALF].rearrange("(p t) -> p t", t=PACK))
-        load_engineering(0, T // 4)
-        load_engineering(T // 4, T // 2)
-        load_engineering(T // 2, T)
-        nc.sync.dma_start(ws_raw[0][:], ws_rows[:, :, 0:HALF])
+        for k in range(4):
+            load_engineering(k * T // 4, (k + 1) * T // 4)
+        for i in (0, 2):
+            nc.sync.dma_start(ws_raw[0][:, i:i + 2, :], ws_rows[:, i:i + 2, 0:HALF])
         load_scale_rows(eng_scales, tab2_scales)
         nc.sync.dma_start(ws_raw[1][:], ws_rows[:, :, HALF:H])
+        nc.sync.dma_start(gain_sb[:], gain.rearrange("(b p t) -> p b t", b=2, t=PACK))
         load_scale_rows(pix_scales, tab_scales)
         nc.sync.dma_start(wf_raw[:].bitcast(I32), wf_words.rearrange("a p c -> p a c").bitcast(I32))
         load_pixels(0, 0, T // 2)
@@ -107,22 +108,13 @@ def tile_list_transit_template_detrending_kernel(
 
         ws_codes = [held([P, HALF], U32, "ws_codes%d" % b) for b in range(2)]
         ws_scales = [held([P, HALF], U8, "ws_scales%d" % b) for b in range(2)]
-        eng_picked = [held([P, HALF], U16, "eng_picked%d" % jh) for jh in range(2)]
-        eng_picked_scales = [held([P, HALF], U8, "eng_picked_scales%d" % jh) for jh in range(2)]
-        resid = [[held([P, PACK, HALF], F32, "resid%d%d" % (jh, b)) for b in range(2)] for jh in range(2)]
+        eng_picked = held([P, S], U16, "eng_picked")
+        eng_picked_scales = held([P, S], U8, "eng_picked_scales")
 
-        def round_on_scalar(ws_bf, raw):
-            nc.scalar.copy(ws_bf.rearrange("p (e m i) -> p m i e", e=2, i=PACK), raw.rearrange("p i m e -> p m i e"))
-
-        def round_on_gpsimd(ws_bf, raw):
-            nc.gpsimd.tensor_scalar(ws_bf.rearrange("p (e m i) -> p e m i", e=2, i=PACK),
-                                    raw.rearrange("p i m e -> p e m i"), 1.0, 0.0, ALU.mult, ALU.add)
-
-        def quantise_ws(b, rounds):
+        def quantise_ws(b):
             ws_bf = work.tile([P, PACK * HALF], BF16, name="ws_bf", align_bytes=64)
-            for u in range(2):
-                rounds[u](ws_bf[:, u * 2 * HALF:(u + 1) * 2 * HALF],
-                          ws_raw[b][:].rearrange("p i (m t) -> p i m t", t=PACK)[:, :, :, 2 * u:2 * u + 2])
+            nc.scalar.copy(ws_bf[:].rearrange("p (u e m i) -> p u m i e", u=2, e=2, i=PACK),
+                           ws_raw[b][:].rearrange("p i (m u e) -> p u m i e", u=2, e=2))
             nc.vector.quantize_mx(ws_codes[b][:].bitcast(FP8X4), ws_scales[b][:], ws_bf[:])
 
         def systematics(b):
@@ -132,17 +124,18 @@ def tile_list_transit_template_detrending_kernel(
                     cols = slice(t * P, (t + 1) * P)
                     nc.tensor.matmul_mx(acc[:], lhsT=ws_codes[b][:, cols].bitcast(FP8X4),
                                         lhsT_scale=ws_scales[b][:, cols],
-                                        rhs=eng_picked[jh][:].bitcast(FP4X4), rhs_scale=eng_picked_scales[jh][:],
+                                        rhs=eng_picked[:, jh * HALF:(jh + 1) * HALF].bitcast(FP4X4),
+                                        rhs_scale=eng_picked_scales[:, jh * HALF:(jh + 1) * HALF],
                                         start=True, stop=True)
                     nc.scalar.activation(resid[jh][b][:, t, :], acc[:], ACT.Copy, scale=gain_sb[:, b, t:t + 1])
 
-        quantise_ws(0, (round_on_scalar, round_on_gpsimd))
-        for jh in range(2):
-            entries = eng_list[:, jh * LIST_COLS:(jh + 1) * LIST_COLS]
-            nc.vector.tensor_copy(eng_picked[jh][:], eng_words[:].indirect(entries))
-            nc.vector.tensor_copy(eng_picked_scales[jh][:], eng_scales[:].indirect(entries))
+        nc.vector.tensor_copy(eng_picked[:], eng_words[:].indirect(eng_list[:]))
+        nc.vector.tensor_copy(eng_picked_scales[:], eng_scales[:].indirect(eng_list[:]))
+        quantise_ws(0)
+        quantise_ws(1)
+        resid = [[shared.tile([P, PACK, HALF], F32, name="resid%d0" % jh, offset=jh * 4 * PACK * HALF),
+                  held([P, PACK, HALF], F32, "resid%d1" % jh)] for jh in range(2)]
         systematics(0)
-        quantise_ws(1, (round_on_gpsimd, round_on_gpsimd))
         systematics(1)
 
         pix_picked_scales0 = held([P, S], U8, "pix_picked_scales0")

@@ -81,10 +81,10 @@ def tile_list_transit_template_detrending_kernel(
         ws_rows = ws.rearrange("(p i) c -> p i c", i=PACK)
         nc.sync.dma_start(eng_list[:], offs2)
         nc.sync.dma_start(pix_list[:], offs)
-        for k in range(4):
-            load_engineering(k * T // 4, (k + 1) * T // 4)
-        for i in (0, 2):
-            nc.sync.dma_start(ws_raw[0][:, i:i + 2, :], ws_rows[:, i:i + 2, 0:HALF])
+        for k in range(2):
+            load_engineering(k * T // 2, (k + 1) * T // 2)
+        for i in range(PACK):
+            nc.sync.dma_start(ws_raw[0][:, i, :], ws_rows[:, i, 0:HALF])
         load_scale_rows(eng_scales, tab2_scales)
         nc.sync.dma_start(ws_raw[1][:], ws_rows[:, :, HALF:H])
         nc.sync.dma_start(gain_sb[:], gain.rearrange("(b p t) -> p b t", b=2, t=PACK))
@@ -189,7 +189,7 @@ def tile_list_transit_template_detrending_kernel(
         def square_on_gpsimd(x):
             nc.gpsimd.tensor_tensor(x, x, x, ALU.mult)
 
-        def damp(jh, b, c0, width, squares, h_tag=""):
+        def damp(jh, b, c0, width, squares, h_tag="", parts=1):
             cols = slice(c0, c0 + width)
             weight = held([P, PACK, width], F32, "weight%d%d_%d" % (jh, b, c0))
             for t in range(PACK):
@@ -201,10 +201,15 @@ def tile_list_transit_template_detrending_kernel(
                 squares[u](weight[:, 2 * u:2 * u + 2, :])
             h = (held([P, PACK * width], BF16, "h_last", h_tag) if h_tag
                  else work.tile([P, PACK * width], BF16, name="h", align_bytes=64, bufs=3))
-            nc.vector.tensor_tensor(h[:].rearrange("p (c e t) -> p c t e", e=2, t=PACK),
-                                    resid[jh][b][:, :, cols].rearrange("p t (c e) -> p c t e", e=2),
-                                    weight[:].rearrange("p t (c e) -> p c t e", e=2), ALU.mult)
-            nc.vector.quantize_mx(h_codes[jh][b][:, cols].bitcast(FP8X4), h_scales[jh][b][:, cols], h[:])
+            step = width // parts
+            for c in range(0, width, step):
+                nc.vector.tensor_tensor(h[:, PACK * c:PACK * (c + step)].rearrange("p (c e t) -> p c t e", e=2, t=PACK),
+                                        resid[jh][b][:, :, c0 + c:c0 + c + step].rearrange("p t (c e) -> p c t e", e=2),
+                                        weight[:, :, c:c + step].rearrange("p t (c e) -> p c t e", e=2), ALU.mult)
+            for c in range(0, width, step):
+                part = slice(c0 + c, c0 + c + step)
+                nc.vector.quantize_mx(h_codes[jh][b][:, part].bitcast(FP8X4), h_scales[jh][b][:, part],
+                                      h[:, PACK * c:PACK * (c + step)])
 
         def template_pass(acc, jh, c0, width, nt, b, start, stop):
             cols = slice(c0, c0 + width)
@@ -255,24 +260,40 @@ def tile_list_transit_template_detrending_kernel(
         nc.sync.dma_start(cat_sb[:], cat.rearrange("(nt p) j -> p nt j", p=P))
         damp(0, 0, 0, HALF, (square_on_gpsimd, square_on_gpsimd))
         flux(1, 0)
-        damp(0, 1, 0, HALF, (square_on_scalar, square_on_scalar))
+        damp(0, 1, 0, HALF, (square_on_scalar, square_on_scalar), "", 2)
         flux(1, 1)
-        sums = template_sums(0, 0, HALF, 0)
+        half_sums = [template_sums(0, c0, HALF // 2, c0 // P) for c0 in (0, HALF // 2)]
         for b in range(2):
-            template_passes(sums, 0, 0, HALF, b)
-        finish(sums, 0, 0, HALF)
+            for k in range(2):
+                template_passes(half_sums[k], 0, k * HALF // 2, HALF // 2, b)
+        for k in range(2):
+            finish(half_sums[k], 0, k * HALF // 2, HALF // 2)
         damp(1, 0, 0, HALF, (square_on_gpsimd, square_on_scalar))
-        piece_sums = [template_sums(1, c0, width, PACK + c0 // P) for c0, width in PIECES]
+        piece_sums = [template_sums(1, c0, width, PACK + c0 // P) for c0, width in PIECES[:2]]
+        last_sums = [bank(k, [P, 2, P]) for k in (7, 0)]
+
+        def last_passes(b):
+            for nt in range(N // P):
+                template_pass(last_sums[nt // 2][:, nt % 2, :], 1, PIECES[2][0], P, nt, b,
+                              b == 0 and nt % 2 == 0, b == 1 and nt % 2 == 1)
+
         for sums, (c0, width) in zip(piece_sums, PIECES):
             template_passes(sums, 1, c0, width, 0)
+        last_passes(0)
         for k, (c0, width) in enumerate(PIECES):
             damp(1, 1, c0, width, (square_on_scalar, square_on_scalar), "last" if k == 2 else "")
-            template_passes(piece_sums[k], 1, c0, width, 1)
+            if k < 2:
+                template_passes(piece_sums[k], 1, c0, width, 1)
             if k == 0:
                 finish(piece_sums[k], 1, c0, width)
+        last_passes(1)
         c0, width = PIECES[1]
         staged = held([P, N // P, width], F32, "staged", "last")
         entries = slice(HALF + c0, HALF + c0 + width)
         nc.vector.tensor_tensor(staged[:], piece_sums[1][0][:], cat_sb[:, :, entries], ALU.add)
         nc.sync.dma_start(out_rows[:, :, entries], staged[:])
-        finish(piece_sums[2], 1, *PIECES[2])
+        c0, width = PIECES[2]
+        entries = slice(HALF + c0, HALF + c0 + width)
+        for k in range(2):
+            add_catalogue(last_sums[k][:], 1, c0, width, 2 * k, 2 * k + 2)
+            nc.sync.dma_start(out_rows[:, 2 * k:2 * k + 2, entries], cat_sb[:, 2 * k:2 * k + 2, entries])

@@ -20,7 +20,7 @@ P = 128
 PACK = 4
 HALF = 512
 LIST_COLS = HALF // 16
-SECOND = 16
+SPREAD = 8
 PIECES = ((0, 256), (256, 128), (384, 128))
 
 
@@ -44,33 +44,32 @@ def tile_list_transit_template_detrending_kernel(
         pix_list = keep.tile([P, S // 16], U16, name="pix_list")
         eng_list = keep.tile([P, S // 16], U16, name="eng_list")
         eng_words = held([P, T], U16, "eng_words")
-        eng_scales = held([P, T], U8, "eng_scales")
-        pix_words = [held([P, T], I32, "pix_words%d" % a, "table%d" % a) for a in range(2)]
-        pix_scales = held([P, T], U8, "pix_scales")
+        eng_scales = held([P, T], U8, "eng_scales", "table0")
+        pix_scales = held([P, T], U8, "pix_scales", "table1")
         ws_raw = [held([P, PACK, HALF], F32, "ws_raw0"),
                   shared.tile([P, PACK, HALF], F32, name="ws_raw1", offset=2 * PACK * HALF)]
         wf_raw = held([P, 2, H], U16, "wf_raw")
         wf_raw_scales = held([P, 2 * H], U8, "wf_raw_scales", "weight_scales")
         gain_sb = held([P, 2, PACK], F32, "gain_sb")
-        pix_picked_scales1 = held([P, S], U8, "pix_picked_scales1")
+        eng_plane = held([P, S], U8, "eng_plane")
+        pix_planes = held([P, 2 * S], U8, "pix_planes")
         warm_in = held([P, 16], F32, "warm_in")
 
         nc.vector.memset(eng_scales[:].bitcast(I32), 0)
         nc.vector.memset(warm_in[:], 1.0)
         nc.vector.memset(pix_scales[:].bitcast(I32), 0)
         nc.vector.memset(wf_raw_scales[:].bitcast(I32), 0)
-        nc.vector.memset(pix_picked_scales1[:].bitcast(I32), 0)
+        nc.vector.memset(eng_plane[:].bitcast(I32), 0)
+        nc.vector.memset(pix_planes[:].bitcast(I32), 0)
         warm_out = held([P, 16], F32, "warm_out")
         nc.scalar.activation(warm_out[:], warm_in[:], ACT.Abs_reciprocal_sqrt)
 
-        def load_scale_rows(tile, dram):
-            passes = dram.shape[0]
-            rows = dram.rearrange("a (q s) c -> s q a c", s=4)
-            for s in range(4):
-                nc.sync.dma_start(tile[s:P:32 // passes, :].bitcast(I32), rows[s].bitcast(I32))
+        def load_scale_rows(tile, dram, a):
+            nc.sync.dma_start(tile[4 + a:P:SPREAD, :].bitcast(I32), dram[a].bitcast(I32))
 
-        def move_second_pass_rows(dst, src):
-            nc.sync.dma_start(dst[0:P - SECOND, :].bitcast(I32), src[SECOND:P, :].bitcast(I32))
+        def move_picked_rows(plane, picked, a):
+            for s in range(4):
+                nc.sync.dma_start(plane[s:P:32, :].bitcast(I32), picked[SPREAD * s + 4 + a:P:32, :].bitcast(I32))
 
         def load_engineering(c0, c1):
             nc.sync.dma_start(eng_words[:, c0:c1].bitcast(I32), tab2_words[0, :, 2 * c0:2 * c1].bitcast(I32))
@@ -83,20 +82,18 @@ def tile_list_transit_template_detrending_kernel(
         nc.sync.dma_start(pix_list[:], offs)
         for k in range(2):
             load_engineering(k * T // 2, (k + 1) * T // 2)
+        load_scale_rows(eng_scales, tab2_scales, 0)
         for i in range(PACK):
             nc.sync.dma_start(ws_raw[0][:, i, :], ws_rows[:, i, 0:HALF])
-        load_scale_rows(eng_scales, tab2_scales)
+        for a in range(2):
+            load_scale_rows(pix_scales, tab_scales, a)
         nc.sync.dma_start(ws_raw[1][:], ws_rows[:, :, HALF:H])
         nc.sync.dma_start(gain_sb[:], gain.rearrange("(b p t) -> p b t", b=2, t=PACK))
-        load_scale_rows(pix_scales, tab_scales)
         nc.sync.dma_start(wf_raw[:].bitcast(I32), wf_words.rearrange("a p c -> p a c").bitcast(I32))
-        load_pixels(0, 0, T // 2)
         wf_scale_rows = wf_scales.rearrange("a (q s) c -> s q a c", s=4)
         for s in range(4):
             nc.sync.dma_start(wf_raw_scales[s:P:32, :].rearrange("q (a c) -> q a c", a=2).bitcast(I32),
                               wf_scale_rows[s].bitcast(I32))
-        load_pixels(0, T // 2, T)
-        load_pixels(1, 0, T)
 
         gain_all = gain_sb[:, :, 0:PACK]
         gain_neg = held([P, 2, PACK], F32, "gain_neg")
@@ -125,23 +122,28 @@ def tile_list_transit_template_detrending_kernel(
                     nc.tensor.matmul_mx(acc[:], lhsT=ws_codes[b][:, cols].bitcast(FP8X4),
                                         lhsT_scale=ws_scales[b][:, cols],
                                         rhs=eng_picked[:, jh * HALF:(jh + 1) * HALF].bitcast(FP4X4),
-                                        rhs_scale=eng_picked_scales[:, jh * HALF:(jh + 1) * HALF],
+                                        rhs_scale=eng_plane[:, jh * HALF:(jh + 1) * HALF],
                                         start=True, stop=True)
                     nc.scalar.activation(resid[jh][b][:, t, :], acc[:], ACT.Copy, scale=gain_sb[:, b, t:t + 1])
 
-        nc.vector.tensor_copy(eng_picked[:], eng_words[:].indirect(eng_list[:]))
         nc.vector.tensor_copy(eng_picked_scales[:], eng_scales[:].indirect(eng_list[:]))
+        move_picked_rows(eng_plane[:], eng_picked_scales, 0)
+        pix_words = [held([P, T], I32, "pix_words0", "table0")]
+        load_pixels(0, 0, T // 2)
+        load_pixels(0, T // 2, T)
+        nc.vector.tensor_copy(eng_picked[:], eng_words[:].indirect(eng_list[:]))
         quantise_ws(0)
+        pix_picked_scales = held([P, S], U8, "pix_picked_scales")
+        nc.vector.tensor_copy(pix_picked_scales[:], pix_scales[:].indirect(pix_list[:]))
+        pix_words.append(held([P, T], I32, "pix_words1", "table1"))
+        for a in range(2):
+            move_picked_rows(pix_planes[:, a * S:(a + 1) * S], pix_picked_scales, a)
+            load_pixels(1, a * T // 2, (a + 1) * T // 2)
         quantise_ws(1)
         resid = [[shared.tile([P, PACK, HALF], F32, name="resid%d0" % jh, offset=jh * 4 * PACK * HALF),
                   held([P, PACK, HALF], F32, "resid%d1" % jh)] for jh in range(2)]
         systematics(0)
         systematics(1)
-
-        pix_picked_scales0 = held([P, S], U8, "pix_picked_scales0")
-        nc.vector.tensor_copy(pix_picked_scales0[:], pix_scales[:].indirect(pix_list[:]))
-        move_second_pass_rows(pix_picked_scales1, pix_picked_scales0)
-        pix_picked_scales = (pix_picked_scales0, pix_picked_scales1)
 
         wf_codes = held([P, 2, H], U16, "wf_codes")
         wf_scales_sb = held([P, 2, H], U8, "wf_scales_sb")
@@ -169,7 +171,7 @@ def tile_list_transit_template_detrending_kernel(
             cols = slice(b * HALF + t * P, b * HALF + (t + 1) * P)
             nc.tensor.matmul_mx(acc[:], lhsT=wf_codes[:, a, cols].bitcast(FP4X4), lhsT_scale=wf_scales_sb[:, a, cols],
                                 rhs=pix_picked[a][jh][:].bitcast(FP8X4),
-                                rhs_scale=pix_picked_scales[a][:, jh * HALF:(jh + 1) * HALF],
+                                rhs_scale=pix_planes[:, a * S + jh * HALF:a * S + (jh + 1) * HALF],
                                 start=(a == 0), stop=(a == 1))
 
         def subtract_flux(acc, jh, b, t):

@@ -31,7 +31,6 @@ def tile_list_transit_template_detrending_kernel(
     nc = tc.nc
     with ExitStack() as ctx:
         keep = ctx.enter_context(tc.tile_pool(name="keep", bufs=1))
-        shared = ctx.enter_context(tc.tile_pool(name="shared", bufs=1))
         work = ctx.enter_context(tc.tile_pool(name="work", bufs=2))
         banks = ctx.enter_context(tc.psum_pool(name="banks", bufs=1))
 
@@ -46,11 +45,10 @@ def tile_list_transit_template_detrending_kernel(
         eng_words = held([P, T], U16, "eng_words")
         eng_scales = held([P, T], U8, "eng_scales", "table0")
         pix_scales = held([P, T], U8, "pix_scales", "table1")
-        ws_raw = [held([P, PACK, HALF], F32, "ws_raw0"),
-                  shared.tile([P, PACK, HALF], F32, name="ws_raw1", offset=2 * PACK * HALF)]
+        ws_raw = [held([P, PACK, HALF], F32, "ws_raw%d" % b) for b in range(2)]
         wf_raw = held([P, 2, H], U16, "wf_raw")
         wf_raw_scales = held([P, 2 * H], U8, "wf_raw_scales", "weight_scales")
-        gain_sb = held([P, 2, PACK], F32, "gain_sb")
+        gain_sb = held([P, 2, 2 * PACK], F32, "gain_sb")
         eng_plane = held([P, S], U8, "eng_plane")
         pix_planes = held([P, 2 * S], U8, "pix_planes")
         warm_in = held([P, 16], F32, "warm_in")
@@ -80,20 +78,21 @@ def tile_list_transit_template_detrending_kernel(
         ws_rows = ws.rearrange("(p i) c -> p i c", i=PACK)
         nc.sync.dma_start(eng_list[:], offs2)
         nc.sync.dma_start(pix_list[:], offs)
-        for k in range(2):
-            load_engineering(k * T // 2, (k + 1) * T // 2)
-        load_scale_rows(eng_scales, tab2_scales, 0)
+        for b in range(2):
+            nc.sync.dma_start(gain_sb[:, b, 0:PACK], gain.rearrange("(b p t) -> b p t", b=2, t=PACK)[b])
         for i in range(PACK):
             nc.sync.dma_start(ws_raw[0][:, i, :], ws_rows[:, i, 0:HALF])
+        load_scale_rows(eng_scales, tab2_scales, 0)
         for a in range(2):
             load_scale_rows(pix_scales, tab_scales, a)
-        nc.sync.dma_start(ws_raw[1][:], ws_rows[:, :, HALF:H])
-        nc.sync.dma_start(gain_sb[:], gain.rearrange("(b p t) -> p b t", b=2, t=PACK))
+        for k in range(2):
+            load_engineering(k * T // 2, (k + 1) * T // 2)
         nc.sync.dma_start(wf_raw[:].bitcast(I32), wf_words.rearrange("a p c -> p a c").bitcast(I32))
         wf_scale_rows = wf_scales.rearrange("a (q s) c -> s q a c", s=4)
         for s in range(4):
             nc.sync.dma_start(wf_raw_scales[s:P:32, :].rearrange("q (a c) -> q a c", a=2).bitcast(I32),
                               wf_scale_rows[s].bitcast(I32))
+        nc.sync.dma_start(ws_raw[1][:], ws_rows[:, :, HALF:H])
 
         gain_all = gain_sb[:, :, 0:PACK]
         gain_neg = held([P, 2, PACK], F32, "gain_neg")
@@ -108,11 +107,12 @@ def tile_list_transit_template_detrending_kernel(
         eng_picked = held([P, S], U16, "eng_picked")
         eng_picked_scales = held([P, S], U8, "eng_picked_scales")
 
-        def quantise_ws(b):
-            ws_bf = work.tile([P, PACK * HALF], BF16, name="ws_bf", align_bytes=64)
-            nc.scalar.copy(ws_bf[:].rearrange("p (u e m i) -> p u m i e", u=2, e=2, i=PACK),
-                           ws_raw[b][:].rearrange("p i (m u e) -> p u m i e", u=2, e=2))
-            nc.vector.quantize_mx(ws_codes[b][:].bitcast(FP8X4), ws_scales[b][:], ws_bf[:])
+        def quantise_ws(b, copies):
+            ws_bf = work.tile([P, 2, PACK * HALF // 2], BF16, name="ws_bf", align_bytes=64)
+            for u in range(2):
+                copies[u](ws_bf[:, u, :].rearrange("p (e m i) -> p m i e", e=2, i=PACK),
+                          ws_raw[b][:].rearrange("p i (m u e) -> p u m i e", u=2, e=2)[:, u])
+            nc.vector.quantize_mx(ws_codes[b][:].bitcast(FP8X4), ws_scales[b][:], ws_bf[:].rearrange("p u c -> p (u c)"))
 
         def systematics(b):
             for jh in range(2):
@@ -131,17 +131,18 @@ def tile_list_transit_template_detrending_kernel(
         pix_words = [held([P, T], I32, "pix_words0", "table0")]
         load_pixels(0, 0, T // 2)
         load_pixels(0, T // 2, T)
-        nc.vector.tensor_copy(eng_picked[:], eng_words[:].indirect(eng_list[:]))
-        quantise_ws(0)
+        quantise_ws(0, (nc.scalar.copy, nc.scalar.copy))
+        for jh in range(2):
+            nc.vector.tensor_copy(eng_picked[:, jh * HALF:(jh + 1) * HALF],
+                                  eng_words[:].indirect(eng_list[:, jh * LIST_COLS:(jh + 1) * LIST_COLS]))
         pix_picked_scales = held([P, S], U8, "pix_picked_scales")
         nc.vector.tensor_copy(pix_picked_scales[:], pix_scales[:].indirect(pix_list[:]))
         pix_words.append(held([P, T], I32, "pix_words1", "table1"))
-        for a in range(2):
-            move_picked_rows(pix_planes[:, a * S:(a + 1) * S], pix_picked_scales, a)
-            load_pixels(1, a * T // 2, (a + 1) * T // 2)
-        quantise_ws(1)
-        resid = [[shared.tile([P, PACK, HALF], F32, name="resid%d0" % jh, offset=jh * 4 * PACK * HALF),
-                  held([P, PACK, HALF], F32, "resid%d1" % jh)] for jh in range(2)]
+        move_picked_rows(pix_planes[:, 0:S], pix_picked_scales, 0)
+        load_pixels(1, 0, T)
+        move_picked_rows(pix_planes[:, S:2 * S], pix_picked_scales, 1)
+        quantise_ws(1, (nc.scalar.copy, nc.vector.tensor_copy))
+        resid = [[held([P, PACK, HALF], F32, "resid%d%d" % (jh, b)) for b in range(2)] for jh in range(2)]
         systematics(0)
         systematics(1)
 
@@ -178,6 +179,17 @@ def tile_list_transit_template_detrending_kernel(
             tile = resid[jh][b][:, t, :]
             nc.vector.scalar_tensor_tensor(tile, acc[:], gain_neg[:, b, t:t + 1], tile, ALU.mult, ALU.add)
 
+        def open_flux(jh, b):
+            sums = [bank(b * PACK + t, [P, HALF]) for t in range(PACK)]
+            for t in range(PACK):
+                flux_pass(sums[t], jh, b, t, 0)
+            return sums
+
+        def close_flux(sums, jh, b):
+            for t in range(PACK):
+                flux_pass(sums[t], jh, b, t, 1)
+                subtract_flux(sums[t], jh, b, t)
+
         def flux(jh, b):
             for t in range(PACK):
                 acc = bank(b * PACK + t, [P, HALF])
@@ -185,33 +197,41 @@ def tile_list_transit_template_detrending_kernel(
                     flux_pass(acc, jh, b, t, a)
                 subtract_flux(acc, jh, b, t)
 
-        def square_on_scalar(x):
-            nc.scalar.activation(x, x, ACT.Square)
+        def square_on_scalar(y, x):
+            nc.scalar.activation(y, x, ACT.Square)
 
-        def square_on_gpsimd(x):
-            nc.gpsimd.tensor_tensor(x, x, x, ALU.mult)
+        def square_on_gpsimd(y, x):
+            nc.gpsimd.tensor_tensor(y, x, x, ALU.mult)
 
-        def damp(jh, b, c0, width, squares, h_tag="", parts=1):
-            cols = slice(c0, c0 + width)
-            weight = held([P, PACK, width], F32, "weight%d%d_%d" % (jh, b, c0))
-            for t in range(PACK):
-                nc.scalar.activation(weight[:, t, :], resid[jh][b][:, t, cols], ACT.Square,
-                                     scale=gain_inv[:, b, t:t + 1])
-            for t in (0, 2):
-                nc.scalar.activation(weight[:, t:t + 2, :], weight[:, t:t + 2, :], ACT.Abs_reciprocal_sqrt, bias=1.0)
+        def square_residual(jh, b, t, weight):
+            nc.scalar.activation(weight[:, t, :], resid[jh][b][:, t, :], ACT.Square, scale=gain_inv[:, b, t:t + 1])
+
+        def inverse_root(x):
+            nc.scalar.activation(x, x, ACT.Abs_reciprocal_sqrt, bias=1.0)
+
+        def multiply(h, jh, b, weight, cols):
+            nc.vector.tensor_tensor(h.rearrange("p (c e t) -> p c t e", e=2, t=PACK),
+                                    resid[jh][b][:, :, cols].rearrange("p t (c e) -> p c t e", e=2),
+                                    weight[:, :, cols].rearrange("p t (c e) -> p c t e", e=2), ALU.mult)
+
+        def quantise_h(h, jh, b, cols):
+            nc.vector.quantize_mx(h_codes[jh][b][:, cols].bitcast(FP8X4), h_scales[jh][b][:, cols], h)
+
+        def damp(jh, b, squares, h_tag, weight_tag=""):
+            root = held([P, PACK, HALF], F32, "root%d%d" % (jh, b))
             for u in range(2):
-                squares[u](weight[:, 2 * u:2 * u + 2, :])
-            h = (held([P, PACK * width], BF16, "h_last", h_tag) if h_tag
-                 else work.tile([P, PACK * width], BF16, name="h", align_bytes=64, bufs=3))
-            step = width // parts
-            for c in range(0, width, step):
-                nc.vector.tensor_tensor(h[:, PACK * c:PACK * (c + step)].rearrange("p (c e t) -> p c t e", e=2, t=PACK),
-                                        resid[jh][b][:, :, c0 + c:c0 + c + step].rearrange("p t (c e) -> p c t e", e=2),
-                                        weight[:, :, c:c + step].rearrange("p t (c e) -> p c t e", e=2), ALU.mult)
-            for c in range(0, width, step):
-                part = slice(c0 + c, c0 + c + step)
-                nc.vector.quantize_mx(h_codes[jh][b][:, part].bitcast(FP8X4), h_scales[jh][b][:, part],
-                                      h[:, PACK * c:PACK * (c + step)])
+                for t in (2 * u, 2 * u + 1):
+                    square_residual(jh, b, t, root)
+                inverse_root(root[:, 2 * u:2 * u + 2, :])
+            weight = held([P, PACK, HALF], F32, "weight%d%d" % (jh, b), weight_tag) if weight_tag else root
+            for u in range(2):
+                squares[u](weight[:, 2 * u:2 * u + 2, :], root[:, 2 * u:2 * u + 2, :])
+            h = held([P, PACK * HALF], BF16, "h%d%d" % (jh, b), h_tag)
+            halves = [slice(c, c + HALF // 2) for c in (0, HALF // 2)]
+            for cols in halves:
+                multiply(h[:, PACK * cols.start:PACK * cols.stop], jh, b, weight, cols)
+            for cols in halves:
+                quantise_h(h[:, PACK * cols.start:PACK * cols.stop], jh, b, cols)
 
         def template_pass(acc, jh, c0, width, nt, b, start, stop):
             cols = slice(c0, c0 + width)
@@ -245,32 +265,28 @@ def tile_list_transit_template_detrending_kernel(
                 add_catalogue(acc[:], jh, c0, width, k * per_bank, (k + 1) * per_bank)
             store(jh, c0, width)
 
-        first = [bank(t, [P, HALF]) for t in range(PACK)]
-        gather_pixels(0, 0)
-        for t in range(PACK):
-            flux_pass(first[t], 0, 0, t, 0)
-        gather_pixels(1, 0)
-        for t in range(PACK):
-            flux_pass(first[t], 0, 0, t, 1)
-            subtract_flux(first[t], 0, 0, t)
-        gather_pixels(0, 1)
+        for jh in range(2):
+            gather_pixels(0, jh)
         wt_codes = held([P, 2, N], I32, "wt_codes", "table0")
         nc.sync.dma_start(wt_codes[:], wt_words.rearrange("b p c i -> p b (c i)").bitcast(I32))
+        opened = open_flux(0, 0)
+        gather_pixels(1, 0)
+        close_flux(opened, 0, 0)
         flux(0, 1)
         gather_pixels(1, 1)
         cat_sb = held([P, N // P, S], F32, "cat_sb", "table1")
         nc.sync.dma_start(cat_sb[:], cat.rearrange("(nt p) j -> p nt j", p=P))
-        damp(0, 0, 0, HALF, (square_on_gpsimd, square_on_gpsimd))
-        flux(1, 0)
-        damp(0, 1, 0, HALF, (square_on_scalar, square_on_scalar), "", 2)
-        flux(1, 1)
+        for b in range(2):
+            flux(1, b)
+        damp(0, 0, (square_on_gpsimd, square_on_gpsimd), "h_a")
+        damp(0, 1, (square_on_gpsimd, square_on_scalar), "h_b")
         half_sums = [template_sums(0, c0, HALF // 2, c0 // P) for c0 in (0, HALF // 2)]
         for b in range(2):
             for k in range(2):
                 template_passes(half_sums[k], 0, k * HALF // 2, HALF // 2, b)
         for k in range(2):
             finish(half_sums[k], 0, k * HALF // 2, HALF // 2)
-        damp(1, 0, 0, HALF, (square_on_gpsimd, square_on_scalar))
+        damp(1, 0, (square_on_gpsimd, square_on_scalar), "h_a", "h_b")
         piece_sums = [template_sums(1, c0, width, PACK + c0 // P) for c0, width in PIECES[:2]]
         last_sums = [bank(k, [P, 2, P]) for k in (7, 0)]
 
@@ -282,8 +298,16 @@ def tile_list_transit_template_detrending_kernel(
         for sums, (c0, width) in zip(piece_sums, PIECES):
             template_passes(sums, 1, c0, width, 0)
         last_passes(0)
+        weight = held([P, PACK, HALF], F32, "weight11")
+        for t in range(PACK):
+            square_residual(1, 1, t, weight)
         for k, (c0, width) in enumerate(PIECES):
-            damp(1, 1, c0, width, (square_on_scalar, square_on_scalar), "last" if k == 2 else "")
+            cols = slice(c0, c0 + width)
+            inverse_root(weight[:, :, cols])
+            square_on_scalar(weight[:, :, cols], weight[:, :, cols])
+            h = held([P, PACK * width], BF16, "h11_%d" % k, "last" if k == 2 else "")
+            multiply(h[:], 1, 1, weight, cols)
+            quantise_h(h[:], 1, 1, cols)
             if k < 2:
                 template_passes(piece_sums[k], 1, c0, width, 1)
             if k == 0:

@@ -20,6 +20,9 @@ P = 128
 PACK = 4
 HALF = 512
 LIST_COLS = HALF // 16
+REGION = (0, T + 4 * T)
+PICKED = 2 * REGION[1] + 2 * T
+ENG = 2 * REGION[1]
 SPREAD = 8
 PIECES = ((0, 256), (256, 128), (384, 128))
 
@@ -31,6 +34,7 @@ def tile_list_transit_template_detrending_kernel(
     nc = tc.nc
     with ExitStack() as ctx:
         keep = ctx.enter_context(tc.tile_pool(name="keep", bufs=1))
+        shared = ctx.enter_context(tc.tile_pool(name="shared", bufs=1))
         work = ctx.enter_context(tc.tile_pool(name="work", bufs=2))
         banks = ctx.enter_context(tc.psum_pool(name="banks", bufs=1))
 
@@ -40,13 +44,16 @@ def tile_list_transit_template_detrending_kernel(
         def held(shape, dtype, name, tag=""):
             return keep.tile(shape, dtype, name=name, tag=tag, align_bytes=64)
 
+        def placed(shape, dtype, name, offset):
+            return shared.tile(shape, dtype, name=name, offset=offset, align_bytes=64)
+
         pix_list = keep.tile([P, S // 16], U16, name="pix_list")
         eng_list = keep.tile([P, S // 16], U16, name="eng_list")
-        eng_words = held([P, T], U16, "eng_words")
-        eng_scales = held([P, T], U8, "eng_scales", "table0")
-        pix_scales = held([P, T], U8, "pix_scales", "table1")
+        eng_words = placed([P, T], U16, "eng_words", ENG)
+        eng_scales = placed([P, T], U8, "eng_scales", REGION[0])
+        pix_scales = placed([P, T], U8, "pix_scales", REGION[1])
         ws_raw = [held([P, PACK, HALF], F32, "ws_raw%d" % b) for b in range(2)]
-        wf_raw = held([P, 2, H], U16, "wf_raw")
+        wf_raw = [held([P, 2, HALF], U16, "wf_raw0")]
         wf_raw_scales = held([P, 2 * H], U8, "wf_raw_scales", "weight_scales")
         gain_sb = held([P, 2, 2 * PACK], F32, "gain_sb")
         eng_plane = held([P, S], U8, "eng_plane")
@@ -72,27 +79,32 @@ def tile_list_transit_template_detrending_kernel(
         def load_engineering(c0, c1):
             nc.sync.dma_start(eng_words[:, c0:c1].bitcast(I32), tab2_words[0, :, 2 * c0:2 * c1].bitcast(I32))
 
+        def load_flux_weights(b):
+            words = wf_words[:, :, 2 * b * HALF:2 * (b + 1) * HALF].rearrange("a p c -> p a c")
+            nc.sync.dma_start(wf_raw[b][:].bitcast(I32), words.bitcast(I32))
+
         def load_pixels(a, c0, c1):
             nc.sync.dma_start(pix_words[a][:, c0:c1], tab_words[a, :, c0:c1].rearrange("p t i -> p (t i)").bitcast(I32))
 
         ws_rows = ws.rearrange("(p i) c -> p i c", i=PACK)
+        nc.sync.dma_start(ws_raw[0][:, 0, :], ws_rows[:, 0, 0:HALF])
         nc.sync.dma_start(eng_list[:], offs2)
         nc.sync.dma_start(pix_list[:], offs)
         for b in range(2):
             nc.sync.dma_start(gain_sb[:, b, 0:PACK], gain.rearrange("(b p t) -> b p t", b=2, t=PACK)[b])
-        for i in range(PACK):
+        for i in range(1, PACK):
             nc.sync.dma_start(ws_raw[0][:, i, :], ws_rows[:, i, 0:HALF])
         load_scale_rows(eng_scales, tab2_scales, 0)
         for a in range(2):
             load_scale_rows(pix_scales, tab_scales, a)
-        for k in range(2):
-            load_engineering(k * T // 2, (k + 1) * T // 2)
-        nc.sync.dma_start(wf_raw[:].bitcast(I32), wf_words.rearrange("a p c -> p a c").bitcast(I32))
+        nc.sync.dma_start(ws_raw[1][:], ws_rows[:, :, HALF:H])
+        load_engineering(0, T // 2)
         wf_scale_rows = wf_scales.rearrange("a (q s) c -> s q a c", s=4)
         for s in range(4):
             nc.sync.dma_start(wf_raw_scales[s:P:32, :].rearrange("q (a c) -> q a c", a=2).bitcast(I32),
                               wf_scale_rows[s].bitcast(I32))
-        nc.sync.dma_start(ws_raw[1][:], ws_rows[:, :, HALF:H])
+        load_engineering(T // 2, T)
+        load_flux_weights(0)
 
         gain_all = gain_sb[:, :, 0:PACK]
         gain_neg = held([P, 2, PACK], F32, "gain_neg")
@@ -101,9 +113,11 @@ def tile_list_transit_template_detrending_kernel(
         nc.vector.tensor_scalar(gain_neg[:], gain_all, -1.0, None, ALU.mult)
         nc.vector.scalar_tensor_tensor(gain_safe[:], gain_all, 0.0, gain_all, ALU.is_equal, ALU.add)
         nc.vector.reciprocal(gain_inv[:], gain_safe[:])
+        gain_inv_sq = held([P, 1], F32, "gain_inv_sq")
+        nc.vector.tensor_tensor(gain_inv_sq[:], gain_inv[:, 0, 3:4], gain_inv[:, 0, 3:4], ALU.mult)
 
-        ws_codes = [held([P, HALF], U32, "ws_codes%d" % b) for b in range(2)]
-        ws_scales = [held([P, HALF], U8, "ws_scales%d" % b) for b in range(2)]
+        ws_codes = [held([P, HALF], U32, "ws_codes0")]
+        ws_scales = []
         eng_picked = held([P, S], U16, "eng_picked")
         eng_picked_scales = held([P, S], U8, "eng_picked_scales")
 
@@ -128,28 +142,37 @@ def tile_list_transit_template_detrending_kernel(
 
         nc.vector.tensor_copy(eng_picked_scales[:], eng_scales[:].indirect(eng_list[:]))
         move_picked_rows(eng_plane[:], eng_picked_scales, 0)
-        pix_words = [held([P, T], I32, "pix_words0", "table0")]
+        pix_words = [placed([P, T], I32, "pix_words0", REGION[0] + T // 2)]
         load_pixels(0, 0, T // 2)
         load_pixels(0, T // 2, T)
+        pix_picked_scales = placed([P, S], U8, "pix_picked_scales", REGION[0])
+        nc.vector.tensor_copy(pix_picked_scales[:], pix_scales[:].indirect(pix_list[:]))
+        pix_words.append(placed([P, T], I32, "pix_words1", REGION[1] + T // 2))
+        move_picked_rows(pix_planes[:, 0:S], pix_picked_scales, 0)
+        load_pixels(1, 0, T)
+        move_picked_rows(pix_planes[:, S:2 * S], pix_picked_scales, 1)
+        wf_raw.append(placed([P, 2, HALF], U16, "wf_raw1", REGION[1] - T // 4))
+        load_flux_weights(1)
+        ws_scales.append(placed([P, HALF], U8, "ws_scales0", REGION[1] + T // 4))
         quantise_ws(0, (nc.scalar.copy, nc.scalar.copy))
         for jh in range(2):
             nc.vector.tensor_copy(eng_picked[:, jh * HALF:(jh + 1) * HALF],
                                   eng_words[:].indirect(eng_list[:, jh * LIST_COLS:(jh + 1) * LIST_COLS]))
-        pix_picked_scales = held([P, S], U8, "pix_picked_scales")
-        nc.vector.tensor_copy(pix_picked_scales[:], pix_scales[:].indirect(pix_list[:]))
-        pix_words.append(held([P, T], I32, "pix_words1", "table1"))
-        move_picked_rows(pix_planes[:, 0:S], pix_picked_scales, 0)
-        load_pixels(1, 0, T)
-        move_picked_rows(pix_planes[:, S:2 * S], pix_picked_scales, 1)
-        quantise_ws(1, (nc.scalar.copy, nc.vector.tensor_copy))
+        ws_codes.append(placed([P, HALF], U32, "ws_codes1", ENG))
+        ws_scales.append(held([P, HALF], U8, "ws_scales1"))
+        quantise_ws(1, (nc.scalar.copy, nc.scalar.copy))
         resid = [[held([P, PACK, HALF], F32, "resid%d%d" % (jh, b)) for b in range(2)] for jh in range(2)]
         systematics(0)
         systematics(1)
 
-        wf_codes = held([P, 2, H], U16, "wf_codes")
-        wf_scales_sb = held([P, 2, H], U8, "wf_scales_sb")
-        nc.vector.tensor_copy(wf_codes[:].rearrange("p a (b t m) -> p (a b) t m", b=2, t=PACK),
-                              wf_raw[:].rearrange("p a (b m t) -> p (a b) t m", b=2, t=PACK))
+        wf_codes = [placed([P, 2, HALF], U16, "wf_codes%d" % b, ENG + (b + 1) * 4 * HALF) for b in range(2)]
+
+        def deal_flux_weights(b):
+            nc.vector.tensor_copy(wf_codes[b][:].rearrange("p a (t m) -> p a t m", t=PACK),
+                                  wf_raw[b][:].rearrange("p a (m t) -> p a t m", t=PACK))
+
+        wf_scales_sb = placed([P, 2, H], U8, "wf_scales_sb", ENG + 4 * HALF + 4 * H)
+        deal_flux_weights(0)
         nc.vector.tensor_copy(wf_scales_sb[:].rearrange("p a (b t m) -> p (a b) t m", b=2, t=PACK),
                               wf_raw_scales[:].rearrange("p (ab m t) -> p ab t m", ab=4, t=PACK))
 
@@ -159,36 +182,26 @@ def tile_list_transit_template_detrending_kernel(
             nc.sync.dma_start(wt_scales_sb[32 * q:32 * q + 4, :].rearrange("s (b c) -> s b c", b=2).bitcast(I32),
                               wt_scales[:, 4 * q:4 * q + 4, :].rearrange("b s c -> s b c").bitcast(I32))
 
-        pix_picked = [[held([P, HALF], U32, "pix_picked%d%d" % (a, jh)) for jh in range(2)] for a in range(2)]
+        pix_picked = {}
         h_codes = [[held([P, HALF], U32, "h_codes%d%d" % (jh, b)) for b in range(2)] for jh in range(2)]
         h_scales = [[held([P, HALF], U8, "h_scales%d%d" % (jh, b)) for b in range(2)] for jh in range(2)]
         out_rows = out.rearrange("(nt p) j -> p nt j", p=P)
 
-        def gather_pixels(a, jh):
+        def gather_pixels(a, jh, slot):
+            pix_picked[a, jh] = placed([P, HALF], U32, "pix_picked%d%d" % (a, jh), PICKED + slot * 4 * HALF)
             entries = pix_list[:, jh * LIST_COLS:(jh + 1) * LIST_COLS]
-            nc.vector.tensor_copy(pix_picked[a][jh][:], pix_words[a][:].bitcast(U32).indirect(entries))
+            nc.vector.tensor_copy(pix_picked[a, jh][:], pix_words[a][:].bitcast(U32).indirect(entries))
 
         def flux_pass(acc, jh, b, t, a):
             cols = slice(b * HALF + t * P, b * HALF + (t + 1) * P)
-            nc.tensor.matmul_mx(acc[:], lhsT=wf_codes[:, a, cols].bitcast(FP4X4), lhsT_scale=wf_scales_sb[:, a, cols],
-                                rhs=pix_picked[a][jh][:].bitcast(FP8X4),
+            nc.tensor.matmul_mx(acc[:], lhsT=wf_codes[b][:, a, t * P:(t + 1) * P].bitcast(FP4X4), lhsT_scale=wf_scales_sb[:, a, cols],
+                                rhs=pix_picked[a, jh][:].bitcast(FP8X4),
                                 rhs_scale=pix_planes[:, a * S + jh * HALF:a * S + (jh + 1) * HALF],
                                 start=(a == 0), stop=(a == 1))
 
         def subtract_flux(acc, jh, b, t):
             tile = resid[jh][b][:, t, :]
             nc.vector.scalar_tensor_tensor(tile, acc[:], gain_neg[:, b, t:t + 1], tile, ALU.mult, ALU.add)
-
-        def open_flux(jh, b):
-            sums = [bank(b * PACK + t, [P, HALF]) for t in range(PACK)]
-            for t in range(PACK):
-                flux_pass(sums[t], jh, b, t, 0)
-            return sums
-
-        def close_flux(sums, jh, b):
-            for t in range(PACK):
-                flux_pass(sums[t], jh, b, t, 1)
-                subtract_flux(sums[t], jh, b, t)
 
         def flux(jh, b):
             for t in range(PACK):
@@ -203,33 +216,37 @@ def tile_list_transit_template_detrending_kernel(
         def square_on_gpsimd(y, x):
             nc.gpsimd.tensor_tensor(y, x, x, ALU.mult)
 
-        def square_residual(jh, b, t, weight):
-            nc.scalar.activation(weight[:, t, :], resid[jh][b][:, t, :], ACT.Square, scale=gain_inv[:, b, t:t + 1])
+        def square_residual(jh, b, t, weight, cols):
+            nc.scalar.activation(weight[:, t, cols], resid[jh][b][:, t, cols], ACT.Square, scale=gain_inv[:, b, t:t + 1])
 
-        def inverse_root(x):
-            nc.scalar.activation(x, x, ACT.Abs_reciprocal_sqrt, bias=1.0)
+        def inverse_root(y, x):
+            nc.scalar.activation(y, x, ACT.Abs_reciprocal_sqrt, bias=1.0)
 
-        def multiply(h, jh, b, weight, cols):
+        def multiply(h, jh, b, cols, weight):
             nc.vector.tensor_tensor(h.rearrange("p (c e t) -> p c t e", e=2, t=PACK),
                                     resid[jh][b][:, :, cols].rearrange("p t (c e) -> p c t e", e=2),
-                                    weight[:, :, cols].rearrange("p t (c e) -> p c t e", e=2), ALU.mult)
+                                    weight.rearrange("p t (c e) -> p c t e", e=2), ALU.mult)
 
         def quantise_h(h, jh, b, cols):
             nc.vector.quantize_mx(h_codes[jh][b][:, cols].bitcast(FP8X4), h_scales[jh][b][:, cols], h)
 
-        def damp(jh, b, squares, h_tag, weight_tag=""):
+        def roots(jh, b):
             root = held([P, PACK, HALF], F32, "root%d%d" % (jh, b))
             for u in range(2):
                 for t in (2 * u, 2 * u + 1):
-                    square_residual(jh, b, t, root)
-                inverse_root(root[:, 2 * u:2 * u + 2, :])
+                    square_residual(jh, b, t, root, slice(0, HALF))
+                inverse_root(root[:, 2 * u:2 * u + 2, :], root[:, 2 * u:2 * u + 2, :])
+            return root
+
+        def damp(jh, b, root, squares, h_tag, weight_tag=""):
             weight = held([P, PACK, HALF], F32, "weight%d%d" % (jh, b), weight_tag) if weight_tag else root
-            for u in range(2):
-                squares[u](weight[:, 2 * u:2 * u + 2, :], root[:, 2 * u:2 * u + 2, :])
-            h = held([P, PACK * HALF], BF16, "h%d%d" % (jh, b), h_tag)
+            for square, t0, t1 in squares:
+                square(weight[:, t0:t1, :], root[:, t0:t1, :])
+            h = (held([P, PACK * HALF], BF16, "h%d%d" % (jh, b), h_tag) if h_tag
+                 else placed([P, PACK * HALF], BF16, "h%d%d" % (jh, b), PICKED))
             halves = [slice(c, c + HALF // 2) for c in (0, HALF // 2)]
             for cols in halves:
-                multiply(h[:, PACK * cols.start:PACK * cols.stop], jh, b, weight, cols)
+                multiply(h[:, PACK * cols.start:PACK * cols.stop], jh, b, cols, weight[:, :, cols])
             for cols in halves:
                 quantise_h(h[:, PACK * cols.start:PACK * cols.stop], jh, b, cols)
 
@@ -265,28 +282,51 @@ def tile_list_transit_template_detrending_kernel(
                 add_catalogue(acc[:], jh, c0, width, k * per_bank, (k + 1) * per_bank)
             store(jh, c0, width)
 
-        for jh in range(2):
-            gather_pixels(0, jh)
-        wt_codes = held([P, 2, N], I32, "wt_codes", "table0")
+        gather_pixels(0, 0, 1)
+        gather_pixels(0, 1, 0)
+        wt_codes = placed([P, 2, N], I32, "wt_codes", REGION[0] + T // 2)
         nc.sync.dma_start(wt_codes[:], wt_words.rearrange("b p c i -> p b (c i)").bitcast(I32))
-        opened = open_flux(0, 0)
-        gather_pixels(1, 0)
-        close_flux(opened, 0, 0)
-        flux(0, 1)
-        gather_pixels(1, 1)
-        cat_sb = held([P, N // P, S], F32, "cat_sb", "table1")
+        sums = [bank(t, [P, HALF]) for t in range(PACK)]
+        for t in range(PACK):
+            flux_pass(sums[t], 0, 0, t, 0)
+        gather_pixels(1, 0, 2)
+        deal_flux_weights(1)
+        root = held([P, PACK, HALF], F32, "root00")
+        for t in (0, 3, 1, 2):
+            flux_pass(sums[t], 0, 0, t, 1)
+            if t == 3:
+                tile = resid[0][0][:, t, :]
+                nc.scalar.activation(root[:, t, :], sums[t][:], ACT.Copy, scale=gain_neg[:, 0, t:t + 1])
+                nc.gpsimd.tensor_tensor(tile, tile, root[:, t, :], ALU.add)
+                square_on_gpsimd(root[:, t, :], tile)
+            else:
+                subtract_flux(sums[t], 0, 0, t)
+        sums = [bank(PACK + t, [P, HALF]) for t in range(PACK)]
+        for t in range(PACK):
+            for a in range(2):
+                flux_pass(sums[t], 0, 1, t, a)
+        gather_pixels(1, 1, 1)
+        for t in range(PACK):
+            subtract_flux(sums[t], 0, 1, t)
+        cat_sb = placed([P, N // P, S], F32, "cat_sb", REGION[1] + T // 2)
         nc.sync.dma_start(cat_sb[:], cat.rearrange("(nt p) j -> p nt j", p=P))
         for b in range(2):
             flux(1, b)
-        damp(0, 0, (square_on_gpsimd, square_on_gpsimd), "h_a")
-        damp(0, 1, (square_on_gpsimd, square_on_scalar), "h_b")
+        for t in range(3):
+            square_residual(0, 0, t, root, slice(0, HALF))
+            if t == 1:
+                inverse_root(root[:, 0:2, :], root[:, 0:2, :])
+        inverse_root(root[:, 2, :], root[:, 2, :])
+        nc.scalar.activation(root[:, 3, :], root[:, 3, :], ACT.Abs_reciprocal_sqrt, bias=1.0, scale=gain_inv_sq[:])
+        damp(0, 0, root, ((square_on_gpsimd, 0, 2), (square_on_gpsimd, 2, 4)), "")
+        damp(0, 1, roots(0, 1), ((square_on_gpsimd, 0, 2), (square_on_scalar, 2, 4)), "h_b")
         half_sums = [template_sums(0, c0, HALF // 2, c0 // P) for c0 in (0, HALF // 2)]
         for b in range(2):
             for k in range(2):
                 template_passes(half_sums[k], 0, k * HALF // 2, HALF // 2, b)
         for k in range(2):
             finish(half_sums[k], 0, k * HALF // 2, HALF // 2)
-        damp(1, 0, (square_on_gpsimd, square_on_scalar), "h_a", "h_b")
+        damp(1, 0, roots(1, 0), ((square_on_gpsimd, 0, 2), (square_on_scalar, 2, 4)), "", "h_b")
         piece_sums = [template_sums(1, c0, width, PACK + c0 // P) for c0, width in PIECES[:2]]
         last_sums = [bank(k, [P, 2, P]) for k in (7, 0)]
 
@@ -298,15 +338,16 @@ def tile_list_transit_template_detrending_kernel(
         for sums, (c0, width) in zip(piece_sums, PIECES):
             template_passes(sums, 1, c0, width, 0)
         last_passes(0)
-        weight = held([P, PACK, HALF], F32, "weight11")
+        squared = held([P, PACK, HALF], F32, "squared11")
         for t in range(PACK):
-            square_residual(1, 1, t, weight)
+            square_residual(1, 1, t, squared, slice(0, HALF))
         for k, (c0, width) in enumerate(PIECES):
             cols = slice(c0, c0 + width)
-            inverse_root(weight[:, :, cols])
-            square_on_scalar(weight[:, :, cols], weight[:, :, cols])
-            h = held([P, PACK * width], BF16, "h11_%d" % k, "last" if k == 2 else "")
-            multiply(h[:], 1, 1, weight, cols)
+            weight = held([P, PACK, width], F32, "weight11_%d" % k)
+            inverse_root(weight[:], squared[:, :, cols])
+            square_on_scalar(weight[:], weight[:])
+            h = held([P, PACK * width], BF16, "h11_%d" % k, ("h_b", "", "last")[k])
+            multiply(h[:], 1, 1, cols, weight[:])
             quantise_h(h[:], 1, 1, cols)
             if k < 2:
                 template_passes(piece_sums[k], 1, c0, width, 1)

@@ -53,7 +53,7 @@ def tile_list_transit_template_detrending_kernel(
         eng_scales = placed([P, T], U8, "eng_scales", REGION[0])
         pix_scales = placed([P, T], U8, "pix_scales", REGION[1])
         ws_raw = [held([P, PACK, HALF], F32, "ws_raw%d" % b) for b in range(2)]
-        wf_raw = [held([P, 2, HALF], U16, "wf_raw0")]
+        wf_raw = []
         wf_raw_scales = held([P, 2 * H], U8, "wf_raw_scales", "weight_scales")
         gain_sb = held([P, 2, 2 * PACK], F32, "gain_sb")
         eng_plane = held([P, S], U8, "eng_plane")
@@ -98,13 +98,12 @@ def tile_list_transit_template_detrending_kernel(
         for a in range(2):
             load_scale_rows(pix_scales, tab_scales, a)
         nc.sync.dma_start(ws_raw[1][:], ws_rows[:, :, HALF:H])
-        load_engineering(0, T // 2)
         wf_scale_rows = wf_scales.rearrange("a (q s) c -> s q a c", s=4)
         for s in range(4):
             nc.sync.dma_start(wf_raw_scales[s:P:32, :].rearrange("q (a c) -> q a c", a=2).bitcast(I32),
                               wf_scale_rows[s].bitcast(I32))
-        load_engineering(T // 2, T)
-        load_flux_weights(0)
+        for k in range(2):
+            load_engineering(k * T // 2, (k + 1) * T // 2)
 
         gain_all = gain_sb[:, :, 0:PACK]
         gain_neg = held([P, 2, PACK], F32, "gain_neg")
@@ -138,22 +137,27 @@ def tile_list_transit_template_detrending_kernel(
                                         rhs=eng_picked[:, jh * HALF:(jh + 1) * HALF].bitcast(FP4X4),
                                         rhs_scale=eng_plane[:, jh * HALF:(jh + 1) * HALF],
                                         start=True, stop=True)
-                    nc.scalar.activation(resid[jh][b][:, t, :], acc[:], ACT.Copy, scale=gain_sb[:, b, t:t + 1])
+                    if (b, jh) == (0, 1) and t >= 2:
+                        nc.vector.tensor_scalar(resid[jh][b][:, t, :], acc[:], gain_sb[:, b, t:t + 1], None, ALU.mult)
+                    else:
+                        nc.scalar.activation(resid[jh][b][:, t, :], acc[:], ACT.Copy, scale=gain_sb[:, b, t:t + 1])
 
         nc.vector.tensor_copy(eng_picked_scales[:], eng_scales[:].indirect(eng_list[:]))
         move_picked_rows(eng_plane[:], eng_picked_scales, 0)
-        pix_words = [placed([P, T], I32, "pix_words0", REGION[0] + T // 2)]
+        wf_raw.append(placed([P, 2, HALF], U16, "wf_raw0", REGION[0] + T // 4))
+        load_flux_weights(0)
+        pix_words = [placed([P, T], I32, "pix_words0", REGION[0] + 3 * T // 4)]
         load_pixels(0, 0, T // 2)
         load_pixels(0, T // 2, T)
         pix_picked_scales = placed([P, S], U8, "pix_picked_scales", REGION[0])
         nc.vector.tensor_copy(pix_picked_scales[:], pix_scales[:].indirect(pix_list[:]))
-        pix_words.append(placed([P, T], I32, "pix_words1", REGION[1] + T // 2))
+        pix_words.append(placed([P, T], I32, "pix_words1", REGION[1] + 3 * T // 4))
         move_picked_rows(pix_planes[:, 0:S], pix_picked_scales, 0)
         load_pixels(1, 0, T)
         move_picked_rows(pix_planes[:, S:2 * S], pix_picked_scales, 1)
-        wf_raw.append(placed([P, 2, HALF], U16, "wf_raw1", REGION[1] - T // 4))
+        wf_raw.append(placed([P, 2, HALF], U16, "wf_raw1", REGION[1]))
         load_flux_weights(1)
-        ws_scales.append(placed([P, HALF], U8, "ws_scales0", REGION[1] + T // 4))
+        ws_scales.append(placed([P, HALF], U8, "ws_scales0", REGION[1] + T // 2))
         quantise_ws(0, (nc.scalar.copy, nc.scalar.copy))
         for jh in range(2):
             nc.vector.tensor_copy(eng_picked[:, jh * HALF:(jh + 1) * HALF],
@@ -284,7 +288,7 @@ def tile_list_transit_template_detrending_kernel(
 
         gather_pixels(0, 0, 1)
         gather_pixels(0, 1, 0)
-        wt_codes = placed([P, 2, N], I32, "wt_codes", REGION[0] + T // 2)
+        wt_codes = placed([P, 2, N], I32, "wt_codes", REGION[0] + 3 * T // 4)
         nc.sync.dma_start(wt_codes[:], wt_words.rearrange("b p c i -> p b (c i)").bitcast(I32))
         sums = [bank(t, [P, HALF]) for t in range(PACK)]
         for t in range(PACK):
@@ -308,7 +312,7 @@ def tile_list_transit_template_detrending_kernel(
         gather_pixels(1, 1, 1)
         for t in range(PACK):
             subtract_flux(sums[t], 0, 1, t)
-        cat_sb = placed([P, N // P, S], F32, "cat_sb", REGION[1] + T // 2)
+        cat_sb = placed([P, N // P, S], F32, "cat_sb", REGION[1] + 3 * T // 4)
         nc.sync.dma_start(cat_sb[:], cat.rearrange("(nt p) j -> p nt j", p=P))
         for b in range(2):
             flux(1, b)

@@ -20,11 +20,19 @@ P = 128
 PACK = 4
 HALF = 512
 LIST_COLS = HALF // 16
-REGION = (0, T + 4 * T)
-PICKED = 2 * REGION[1] + 2 * T
-ENG = 2 * REGION[1]
-SPREAD = 8
+LAP = 64
+WS_RAW1 = 0
+ENG_SCALES = WS_RAW1 + 16 * HALF - LAP
+PIX0 = ENG_SCALES + T - LAP
+WS_BF1 = PIX0 + 4 * T
+PIX_SCALES = WS_BF1 + 8 * HALF - LAP
+PIX1 = PIX_SCALES + T - LAP
+ENG_WORDS = PIX1 + 4 * T
+WS_BF0 = ENG_WORDS + 2 * T
+WF_RAW = WS_BF0 + 8 * HALF
+PICKED1 = WF_RAW + 4 * H
 PIECES = ((0, 256), (256, 128), (384, 128))
+EARLY = {(0, 0): (1, 3), (0, 1): (0,), (1, 0): (0, 1, 2), (1, 1): ()}
 
 
 def tile_list_transit_template_detrending_kernel(
@@ -35,7 +43,6 @@ def tile_list_transit_template_detrending_kernel(
     with ExitStack() as ctx:
         keep = ctx.enter_context(tc.tile_pool(name="keep", bufs=1))
         shared = ctx.enter_context(tc.tile_pool(name="shared", bufs=1))
-        work = ctx.enter_context(tc.tile_pool(name="work", bufs=2))
         banks = ctx.enter_context(tc.psum_pool(name="banks", bufs=1))
 
         def bank(k, shape):
@@ -49,83 +56,85 @@ def tile_list_transit_template_detrending_kernel(
 
         pix_list = keep.tile([P, S // 16], U16, name="pix_list")
         eng_list = keep.tile([P, S // 16], U16, name="eng_list")
-        eng_words = placed([P, T], U16, "eng_words", ENG)
-        eng_scales = placed([P, T], U8, "eng_scales", REGION[0])
-        pix_scales = placed([P, T], U8, "pix_scales", REGION[1])
-        ws_raw = [held([P, PACK, HALF], F32, "ws_raw%d" % b) for b in range(2)]
-        wf_raw = []
-        wf_raw_scales = held([P, 2 * H], U8, "wf_raw_scales", "weight_scales")
+        eng_words = placed([P, T], U16, "eng_words", ENG_WORDS)
+        eng_scales = placed([P, T], U8, "eng_scales", ENG_SCALES)
+        pix_scales = placed([P, T], U8, "pix_scales", PIX_SCALES)
+        ws_raw = [held([P, PACK, HALF], F32, "ws_raw0")]
         gain_sb = held([P, 2, 2 * PACK], F32, "gain_sb")
         eng_plane = held([P, S], U8, "eng_plane")
         pix_planes = held([P, 2 * S], U8, "pix_planes")
         warm_in = held([P, 16], F32, "warm_in")
 
-        nc.vector.memset(eng_scales[:].bitcast(I32), 0)
         nc.vector.memset(warm_in[:], 1.0)
+        nc.vector.memset(eng_scales[:].bitcast(I32), 0)
         nc.vector.memset(pix_scales[:].bitcast(I32), 0)
-        nc.vector.memset(wf_raw_scales[:].bitcast(I32), 0)
         nc.vector.memset(eng_plane[:].bitcast(I32), 0)
         nc.vector.memset(pix_planes[:].bitcast(I32), 0)
-        warm_out = held([P, 16], F32, "warm_out")
-        nc.scalar.activation(warm_out[:], warm_in[:], ACT.Abs_reciprocal_sqrt)
 
-        def load_scale_rows(tile, dram, a):
-            nc.sync.dma_start(tile[4 + a:P:SPREAD, :].bitcast(I32), dram[a].bitcast(I32))
+        def load_scale_rows(tile, dram, first, spread):
+            nc.scalar.dma_start(tile[first:P:spread, :].bitcast(I32), dram.rearrange("a q c -> (a q) c").bitcast(I32))
 
-        def move_picked_rows(plane, picked, a):
+        def move_picked_rows(plane, picked, first, spread):
             for s in range(4):
-                nc.sync.dma_start(plane[s:P:32, :].bitcast(I32), picked[SPREAD * s + 4 + a:P:32, :].bitcast(I32))
-
-        def load_engineering(c0, c1):
-            nc.sync.dma_start(eng_words[:, c0:c1].bitcast(I32), tab2_words[0, :, 2 * c0:2 * c1].bitcast(I32))
-
-        def load_flux_weights(b):
-            words = wf_words[:, :, 2 * b * HALF:2 * (b + 1) * HALF].rearrange("a p c -> p a c")
-            nc.sync.dma_start(wf_raw[b][:].bitcast(I32), words.bitcast(I32))
+                rows = slice(first + spread * s, first + spread * (12 + s) + 1, 4 * spread)
+                nc.sync.dma_start(plane[s:P:32, :].bitcast(I32), picked[rows, :].bitcast(I32))
 
         def load_pixels(a, c0, c1):
             nc.sync.dma_start(pix_words[a][:, c0:c1], tab_words[a, :, c0:c1].rearrange("p t i -> p (t i)").bitcast(I32))
 
         ws_rows = ws.rearrange("(p i) c -> p i c", i=PACK)
-        nc.sync.dma_start(ws_raw[0][:, 0, :], ws_rows[:, 0, 0:HALF])
         nc.sync.dma_start(eng_list[:], offs2)
+        nc.scalar.dma_start(gain_sb[:, :, 0:PACK], gain.rearrange("(b p t) -> p b t", b=2, t=PACK))
         nc.sync.dma_start(pix_list[:], offs)
-        for b in range(2):
-            nc.sync.dma_start(gain_sb[:, b, 0:PACK], gain.rearrange("(b p t) -> b p t", b=2, t=PACK)[b])
-        for i in range(1, PACK):
-            nc.sync.dma_start(ws_raw[0][:, i, :], ws_rows[:, i, 0:HALF])
-        load_scale_rows(eng_scales, tab2_scales, 0)
-        for a in range(2):
-            load_scale_rows(pix_scales, tab_scales, a)
-        nc.sync.dma_start(ws_raw[1][:], ws_rows[:, :, HALF:H])
-        wf_scale_rows = wf_scales.rearrange("a (q s) c -> s q a c", s=4)
-        for s in range(4):
-            nc.sync.dma_start(wf_raw_scales[s:P:32, :].rearrange("q (a c) -> q a c", a=2).bitcast(I32),
-                              wf_scale_rows[s].bitcast(I32))
-        for k in range(2):
-            load_engineering(k * T // 2, (k + 1) * T // 2)
+        nc.sync.dma_start(ws_raw[0][:], ws_rows[:, :, 0:HALF])
+        nc.sync.dma_start(eng_words[:].bitcast(I32), tab2_words[0].bitcast(I32))
+        wf_raw = placed([P, 2, H], U16, "wf_raw", WF_RAW)
+        nc.sync.dma_start(wf_raw[:].bitcast(I32), wf_words.rearrange("a p c -> p a c").bitcast(I32))
+        warm_out = held([P, 16], F32, "warm_out")
+        nc.scalar.activation(warm_out[:], warm_in[:], ACT.Abs_reciprocal_sqrt)
+        load_scale_rows(eng_scales, tab2_scales, 4, 8)
+        load_scale_rows(pix_scales, tab_scales, 0, 4)
 
         gain_all = gain_sb[:, :, 0:PACK]
         gain_neg = held([P, 2, PACK], F32, "gain_neg")
         gain_safe = held([P, 2, PACK], F32, "gain_safe")
         gain_inv = held([P, 2, PACK], F32, "gain_inv")
-        nc.vector.tensor_scalar(gain_neg[:], gain_all, -1.0, None, ALU.mult)
+        gain_inv_sq = held([P, 2, PACK], F32, "gain_inv_sq")
         nc.vector.scalar_tensor_tensor(gain_safe[:], gain_all, 0.0, gain_all, ALU.is_equal, ALU.add)
+        nc.vector.tensor_scalar(gain_neg[:], gain_all, -1.0, None, ALU.mult)
         nc.vector.reciprocal(gain_inv[:], gain_safe[:])
-        gain_inv_sq = held([P, 1], F32, "gain_inv_sq")
-        nc.vector.tensor_tensor(gain_inv_sq[:], gain_inv[:, 0, 3:4], gain_inv[:, 0, 3:4], ALU.mult)
+        nc.vector.tensor_tensor(gain_inv_sq[:], gain_inv[:], gain_inv[:], ALU.mult)
 
-        ws_codes = [held([P, HALF], U32, "ws_codes0")]
-        ws_scales = []
-        eng_picked = held([P, S], U16, "eng_picked")
+        ws_codes = [held([P, HALF], U32, "ws_codes%d" % b) for b in range(2)]
         eng_picked_scales = held([P, S], U8, "eng_picked_scales")
+        nc.vector.tensor_copy(eng_picked_scales[:], eng_scales[:].indirect(eng_list[:]))
+        move_picked_rows(eng_plane[:], eng_picked_scales, 4, 8)
+        ws_raw.append(placed([P, PACK, HALF], F32, "ws_raw1", WS_RAW1))
+        nc.sync.dma_start(ws_raw[1][:], ws_rows[:, :, HALF:H])
+        wf_raw_scales = placed([P, 2 * H], U8, "wf_raw_scales", ENG_SCALES + 1600)
+        nc.vector.memset(wf_raw_scales[:].bitcast(I32), 0)
+        wf_scale_rows = wf_scales.rearrange("a (q s) c -> s q a c", s=4)
+        for s in range(4):
+            nc.sync.dma_start(wf_raw_scales[s:P:32, :].rearrange("q (a c) -> q a c", a=2).bitcast(I32),
+                              wf_scale_rows[s].bitcast(I32))
+        pix_words = [placed([P, T], I32, "pix_words0", PIX0)]
+        load_pixels(0, 0, T)
 
-        def quantise_ws(b, copies):
-            ws_bf = work.tile([P, 2, PACK * HALF // 2], BF16, name="ws_bf", align_bytes=64)
+        def round_ws(b, ws_bf, copy):
             for u in range(2):
-                copies[u](ws_bf[:, u, :].rearrange("p (e m i) -> p m i e", e=2, i=PACK),
-                          ws_raw[b][:].rearrange("p i (m u e) -> p u m i e", u=2, e=2)[:, u])
+                copy(ws_bf[:, u, :].rearrange("p (e m i) -> p m i e", e=2, i=PACK),
+                     ws_raw[b][:].rearrange("p i (m u e) -> p u m i e", u=2, e=2)[:, u])
+
+        def quantise_ws(b, ws_bf):
             nc.vector.quantize_mx(ws_codes[b][:].bitcast(FP8X4), ws_scales[b][:], ws_bf[:].rearrange("p u c -> p (u c)"))
+
+        def gather_engineering(jh, offset):
+            eng_picked.append(placed([P, HALF], U16, "eng_picked%d" % jh, offset))
+            nc.vector.tensor_copy(eng_picked[jh][:], eng_words[:].indirect(eng_list[:, jh * LIST_COLS:(jh + 1) * LIST_COLS]))
+
+        def deal_flux_weights(b, copy):
+            copy(wf_codes[b][:].rearrange("p a (t m) -> p a t m", t=PACK),
+                 wf_raw[:, :, b * HALF:(b + 1) * HALF].rearrange("p a (m t) -> p a t m", t=PACK))
 
         def systematics(b):
             for jh in range(2):
@@ -134,53 +143,41 @@ def tile_list_transit_template_detrending_kernel(
                     cols = slice(t * P, (t + 1) * P)
                     nc.tensor.matmul_mx(acc[:], lhsT=ws_codes[b][:, cols].bitcast(FP8X4),
                                         lhsT_scale=ws_scales[b][:, cols],
-                                        rhs=eng_picked[:, jh * HALF:(jh + 1) * HALF].bitcast(FP4X4),
+                                        rhs=eng_picked[jh][:].bitcast(FP4X4),
                                         rhs_scale=eng_plane[:, jh * HALF:(jh + 1) * HALF],
                                         start=True, stop=True)
-                    if (b, jh) == (0, 1) and t >= 2:
-                        nc.vector.tensor_scalar(resid[jh][b][:, t, :], acc[:], gain_sb[:, b, t:t + 1], None, ALU.mult)
-                    else:
-                        nc.scalar.activation(resid[jh][b][:, t, :], acc[:], ACT.Copy, scale=gain_sb[:, b, t:t + 1])
+                    nc.scalar.activation(resid[jh][b][:, t, :], acc[:], ACT.Copy, scale=gain_sb[:, b, t:t + 1])
 
-        nc.vector.tensor_copy(eng_picked_scales[:], eng_scales[:].indirect(eng_list[:]))
-        move_picked_rows(eng_plane[:], eng_picked_scales, 0)
-        wf_raw.append(placed([P, 2, HALF], U16, "wf_raw0", REGION[0] + T // 4))
-        load_flux_weights(0)
-        pix_words = [placed([P, T], I32, "pix_words0", REGION[0] + 3 * T // 4)]
-        load_pixels(0, 0, T // 2)
-        load_pixels(0, T // 2, T)
-        pix_picked_scales = placed([P, S], U8, "pix_picked_scales", REGION[0])
-        nc.vector.tensor_copy(pix_picked_scales[:], pix_scales[:].indirect(pix_list[:]))
-        pix_words.append(placed([P, T], I32, "pix_words1", REGION[1] + 3 * T // 4))
-        move_picked_rows(pix_planes[:, 0:S], pix_picked_scales, 0)
-        load_pixels(1, 0, T)
-        move_picked_rows(pix_planes[:, S:2 * S], pix_picked_scales, 1)
-        wf_raw.append(placed([P, 2, HALF], U16, "wf_raw1", REGION[1]))
-        load_flux_weights(1)
-        ws_scales.append(placed([P, HALF], U8, "ws_scales0", REGION[1] + T // 2))
-        quantise_ws(0, (nc.scalar.copy, nc.scalar.copy))
-        for jh in range(2):
-            nc.vector.tensor_copy(eng_picked[:, jh * HALF:(jh + 1) * HALF],
-                                  eng_words[:].indirect(eng_list[:, jh * LIST_COLS:(jh + 1) * LIST_COLS]))
-        ws_codes.append(placed([P, HALF], U32, "ws_codes1", ENG))
-        ws_scales.append(held([P, HALF], U8, "ws_scales1"))
-        quantise_ws(1, (nc.scalar.copy, nc.scalar.copy))
         resid = [[held([P, PACK, HALF], F32, "resid%d%d" % (jh, b)) for b in range(2)] for jh in range(2)]
+        eng_picked = []
+        ws_scales = [placed([P, HALF], U8, "ws_scales0", ENG_SCALES + LAP), held([P, HALF], U8, "ws_scales1")]
+        ws_bf0 = placed([P, 2, PACK * HALF // 2], BF16, "ws_bf0", WS_BF0)
+        round_ws(0, ws_bf0, nc.scalar.copy)
+        wf_codes = [held([P, 2, HALF], U16, "wf_codes0")]
+        deal_flux_weights(0, nc.scalar.copy)
+        gather_engineering(0, ENG_SCALES + 576)
+        quantise_ws(0, ws_bf0)
+        gather_engineering(1, WS_BF0)
         systematics(0)
-        systematics(1)
 
-        wf_codes = [placed([P, 2, HALF], U16, "wf_codes%d" % b, ENG + (b + 1) * 4 * HALF) for b in range(2)]
+        pix_picked_scales = placed([P, S], U8, "pix_picked_scales", ENG_WORDS)
+        nc.vector.tensor_copy(pix_picked_scales[:], pix_scales[:].indirect(pix_list[:]))
+        pix_words.append(placed([P, T], I32, "pix_words1", PIX1))
+        move_picked_rows(pix_planes[:, 0:S], pix_picked_scales, 0, 4)
+        load_pixels(1, 0, T)
+        move_picked_rows(pix_planes[:, S:2 * S], pix_picked_scales, 64, 4)
 
-        def deal_flux_weights(b):
-            nc.vector.tensor_copy(wf_codes[b][:].rearrange("p a (t m) -> p a t m", t=PACK),
-                                  wf_raw[b][:].rearrange("p a (m t) -> p a t m", t=PACK))
-
-        wf_scales_sb = placed([P, 2, H], U8, "wf_scales_sb", ENG + 4 * HALF + 4 * H)
-        deal_flux_weights(0)
+        ws_bf1 = placed([P, 2, PACK * HALF // 2], BF16, "ws_bf1", WS_BF1)
+        round_ws(1, ws_bf1, nc.vector.tensor_copy)
+        wf_scales_sb = placed([P, 2, H], U8, "wf_scales_sb", WS_RAW1)
         nc.vector.tensor_copy(wf_scales_sb[:].rearrange("p a (b t m) -> p (a b) t m", b=2, t=PACK),
                               wf_raw_scales[:].rearrange("p (ab m t) -> p ab t m", ab=4, t=PACK))
+        quantise_ws(1, ws_bf1)
+        systematics(1)
+        wf_codes.append(placed([P, 2, HALF], U16, "wf_codes1", WS_BF1))
+        deal_flux_weights(1, nc.vector.tensor_copy)
 
-        wt_scales_sb = held([P, 2 * N], U8, "wt_scales_sb", "weight_scales")
+        wt_scales_sb = placed([P, 2 * N], U8, "wt_scales_sb", ENG_SCALES + 1600)
         nc.vector.memset(wt_scales_sb[:].bitcast(I32), 0)
         for q in range(4):
             nc.sync.dma_start(wt_scales_sb[32 * q:32 * q + 4, :].rearrange("s (b c) -> s b c", b=2).bitcast(I32),
@@ -191,8 +188,8 @@ def tile_list_transit_template_detrending_kernel(
         h_scales = [[held([P, HALF], U8, "h_scales%d%d" % (jh, b)) for b in range(2)] for jh in range(2)]
         out_rows = out.rearrange("(nt p) j -> p nt j", p=P)
 
-        def gather_pixels(a, jh, slot):
-            pix_picked[a, jh] = placed([P, HALF], U32, "pix_picked%d%d" % (a, jh), PICKED + slot * 4 * HALF)
+        def gather_pixels(a, jh, offset):
+            pix_picked[a, jh] = placed([P, HALF], U32, "pix_picked%d%d" % (a, jh), offset)
             entries = pix_list[:, jh * LIST_COLS:(jh + 1) * LIST_COLS]
             nc.vector.tensor_copy(pix_picked[a, jh][:], pix_words[a][:].bitcast(U32).indirect(entries))
 
@@ -203,51 +200,47 @@ def tile_list_transit_template_detrending_kernel(
                                 rhs_scale=pix_planes[:, a * S + jh * HALF:a * S + (jh + 1) * HALF],
                                 start=(a == 0), stop=(a == 1))
 
-        def subtract_flux(acc, jh, b, t):
-            tile = resid[jh][b][:, t, :]
-            nc.vector.scalar_tensor_tensor(tile, acc[:], gain_neg[:, b, t:t + 1], tile, ALU.mult, ALU.add)
+        root = [[held([P, PACK, HALF], F32, "root%d%d" % (jh, b)) for b in range(2)] for jh in range(2)]
 
-        def flux(jh, b):
-            for t in range(PACK):
-                acc = bank(b * PACK + t, [P, HALF])
-                for a in range(2):
-                    flux_pass(acc, jh, b, t, a)
-                subtract_flux(acc, jh, b, t)
+        def flux(jh):
+            sums = [[bank(b * PACK + t, [P, HALF]) for t in range(PACK)] for b in range(2)]
+            for b in range(2):
+                for t in range(PACK):
+                    flux_pass(sums[b][t], jh, b, t, 0)
+            gather_pixels(1, jh, PICKED1)
+            for b in range(2):
+                for t in range(PACK):
+                    flux_pass(sums[b][t], jh, b, t, 1)
+                    tile = resid[jh][b][:, t, :]
+                    nc.vector.scalar_tensor_tensor(tile, sums[b][t][:], gain_neg[:, b, t:t + 1], tile, ALU.mult, ALU.add)
+                    if t in EARLY[jh, b]:
+                        nc.gpsimd.tensor_tensor(root[jh][b][:, t, :], tile, tile, ALU.mult)
 
-        def square_on_scalar(y, x):
-            nc.scalar.activation(y, x, ACT.Square)
-
-        def square_on_gpsimd(y, x):
-            nc.gpsimd.tensor_tensor(y, x, x, ALU.mult)
-
-        def square_residual(jh, b, t, weight, cols):
-            nc.scalar.activation(weight[:, t, cols], resid[jh][b][:, t, cols], ACT.Square, scale=gain_inv[:, b, t:t + 1])
+        def square_residual(jh, b, t):
+            nc.scalar.activation(root[jh][b][:, t, :], resid[jh][b][:, t, :], ACT.Square, scale=gain_inv[:, b, t:t + 1])
 
         def inverse_root(y, x):
             nc.scalar.activation(y, x, ACT.Abs_reciprocal_sqrt, bias=1.0)
 
-        def multiply(h, jh, b, cols, weight):
+        def roots(jh, b, rest):
+            tile = root[jh][b]
+            for t in range(PACK)[rest]:
+                square_residual(jh, b, t)
+            for t in EARLY[jh, b]:
+                nc.scalar.activation(tile[:, t, :], tile[:, t, :], ACT.Abs_reciprocal_sqrt, bias=1.0,
+                                     scale=gain_inv_sq[:, b, t:t + 1])
+            inverse_root(tile[:, rest, :], tile[:, rest, :])
+
+        def multiply(h, jh, b, cols, weights):
             nc.vector.tensor_tensor(h.rearrange("p (c e t) -> p c t e", e=2, t=PACK),
                                     resid[jh][b][:, :, cols].rearrange("p t (c e) -> p c t e", e=2),
-                                    weight.rearrange("p t (c e) -> p c t e", e=2), ALU.mult)
+                                    weights.rearrange("p t (c e) -> p c t e", e=2), ALU.mult)
 
         def quantise_h(h, jh, b, cols):
             nc.vector.quantize_mx(h_codes[jh][b][:, cols].bitcast(FP8X4), h_scales[jh][b][:, cols], h)
 
-        def roots(jh, b):
-            root = held([P, PACK, HALF], F32, "root%d%d" % (jh, b))
-            for u in range(2):
-                for t in (2 * u, 2 * u + 1):
-                    square_residual(jh, b, t, root, slice(0, HALF))
-                inverse_root(root[:, 2 * u:2 * u + 2, :], root[:, 2 * u:2 * u + 2, :])
-            return root
-
-        def damp(jh, b, root, squares, h_tag, weight_tag=""):
-            weight = held([P, PACK, HALF], F32, "weight%d%d" % (jh, b), weight_tag) if weight_tag else root
-            for square, t0, t1 in squares:
-                square(weight[:, t0:t1, :], root[:, t0:t1, :])
-            h = (held([P, PACK * HALF], BF16, "h%d%d" % (jh, b), h_tag) if h_tag
-                 else placed([P, PACK * HALF], BF16, "h%d%d" % (jh, b), PICKED))
+        def damp(jh, b, weight, h_tag):
+            h = held([P, PACK * HALF], BF16, "h%d%d" % (jh, b), h_tag)
             halves = [slice(c, c + HALF // 2) for c in (0, HALF // 2)]
             for cols in halves:
                 multiply(h[:, PACK * cols.start:PACK * cols.stop], jh, b, cols, weight[:, :, cols])
@@ -286,51 +279,30 @@ def tile_list_transit_template_detrending_kernel(
                 add_catalogue(acc[:], jh, c0, width, k * per_bank, (k + 1) * per_bank)
             store(jh, c0, width)
 
-        gather_pixels(0, 0, 1)
-        gather_pixels(0, 1, 0)
-        wt_codes = placed([P, 2, N], I32, "wt_codes", REGION[0] + 3 * T // 4)
+        for jh in range(2):
+            gather_pixels(0, jh, WF_RAW + jh * 4 * HALF)
+        wt_codes = placed([P, 2, N], I32, "wt_codes", PIX0)
         nc.sync.dma_start(wt_codes[:], wt_words.rearrange("b p c i -> p b (c i)").bitcast(I32))
-        sums = [bank(t, [P, HALF]) for t in range(PACK)]
-        for t in range(PACK):
-            flux_pass(sums[t], 0, 0, t, 0)
-        gather_pixels(1, 0, 2)
-        deal_flux_weights(1)
-        root = held([P, PACK, HALF], F32, "root00")
-        for t in (0, 3, 1, 2):
-            flux_pass(sums[t], 0, 0, t, 1)
-            if t == 3:
-                tile = resid[0][0][:, t, :]
-                nc.scalar.activation(root[:, t, :], sums[t][:], ACT.Copy, scale=gain_neg[:, 0, t:t + 1])
-                nc.gpsimd.tensor_tensor(tile, tile, root[:, t, :], ALU.add)
-                square_on_gpsimd(root[:, t, :], tile)
-            else:
-                subtract_flux(sums[t], 0, 0, t)
-        sums = [bank(PACK + t, [P, HALF]) for t in range(PACK)]
-        for t in range(PACK):
-            for a in range(2):
-                flux_pass(sums[t], 0, 1, t, a)
-        gather_pixels(1, 1, 1)
-        for t in range(PACK):
-            subtract_flux(sums[t], 0, 1, t)
-        cat_sb = placed([P, N // P, S], F32, "cat_sb", REGION[1] + 3 * T // 4)
+        for jh in range(2):
+            flux(jh)
+        cat_sb = placed([P, N // P, S], F32, "cat_sb", PIX1)
         nc.sync.dma_start(cat_sb[:], cat.rearrange("(nt p) j -> p nt j", p=P))
-        for b in range(2):
-            flux(1, b)
-        for t in range(3):
-            square_residual(0, 0, t, root, slice(0, HALF))
-            if t == 1:
-                inverse_root(root[:, 0:2, :], root[:, 0:2, :])
-        inverse_root(root[:, 2, :], root[:, 2, :])
-        nc.scalar.activation(root[:, 3, :], root[:, 3, :], ACT.Abs_reciprocal_sqrt, bias=1.0, scale=gain_inv_sq[:])
-        damp(0, 0, root, ((square_on_gpsimd, 0, 2), (square_on_gpsimd, 2, 4)), "")
-        damp(0, 1, roots(0, 1), ((square_on_gpsimd, 0, 2), (square_on_scalar, 2, 4)), "h_b")
+
+        for b, rest in enumerate((slice(0, PACK, 2), slice(1, PACK))):
+            roots(0, b, rest)
+            nc.scalar.activation(root[0][b][:], root[0][b][:], ACT.Square)
+            damp(0, b, root[0][b], "h_%d" % b)
         half_sums = [template_sums(0, c0, HALF // 2, c0 // P) for c0 in (0, HALF // 2)]
         for b in range(2):
             for k in range(2):
                 template_passes(half_sums[k], 0, k * HALF // 2, HALF // 2, b)
         for k in range(2):
             finish(half_sums[k], 0, k * HALF // 2, HALF // 2)
-        damp(1, 0, roots(1, 0), ((square_on_gpsimd, 0, 2), (square_on_scalar, 2, 4)), "", "h_b")
+        roots(1, 0, slice(3, PACK))
+        weight = held([P, PACK, HALF], F32, "weight10", "h_1")
+        nc.gpsimd.tensor_tensor(weight[:, 0:2, :], root[1][0][:, 0:2, :], root[1][0][:, 0:2, :], ALU.mult)
+        nc.scalar.activation(weight[:, 2:4, :], root[1][0][:, 2:4, :], ACT.Square)
+        damp(1, 0, weight, "h_0")
         piece_sums = [template_sums(1, c0, width, PACK + c0 // P) for c0, width in PIECES[:2]]
         last_sums = [bank(k, [P, 2, P]) for k in (7, 0)]
 
@@ -342,15 +314,14 @@ def tile_list_transit_template_detrending_kernel(
         for sums, (c0, width) in zip(piece_sums, PIECES):
             template_passes(sums, 1, c0, width, 0)
         last_passes(0)
-        squared = held([P, PACK, HALF], F32, "squared11")
         for t in range(PACK):
-            square_residual(1, 1, t, squared, slice(0, HALF))
+            square_residual(1, 1, t)
         for k, (c0, width) in enumerate(PIECES):
             cols = slice(c0, c0 + width)
             weight = held([P, PACK, width], F32, "weight11_%d" % k)
-            inverse_root(weight[:], squared[:, :, cols])
-            square_on_scalar(weight[:], weight[:])
-            h = held([P, PACK * width], BF16, "h11_%d" % k, ("h_b", "", "last")[k])
+            inverse_root(weight[:], root[1][1][:, :, cols])
+            nc.scalar.activation(weight[:], weight[:], ACT.Square)
+            h = held([P, PACK * width], BF16, "h11_%d" % k, ("h_1", "", "last")[k])
             multiply(h[:], 1, 1, cols, weight[:])
             quantise_h(h[:], 1, 1, cols)
             if k < 2:

@@ -20,19 +20,18 @@ P = 128
 PACK = 4
 HALF = 512
 LIST_COLS = HALF // 16
+ENG_ROW, PIX_ROW = P - 16, P - 32
 LAP = 64
 WS_RAW1 = 0
 ENG_SCALES = WS_RAW1 + 16 * HALF - LAP
-PIX0 = ENG_SCALES + T - LAP
-WS_BF1 = PIX0 + 4 * T
-PIX_SCALES = WS_BF1 + 8 * HALF - LAP
+PIX0 = ENG_SCALES + T
+PIX_SCALES = PIX0 + 4 * T - LAP
 PIX1 = PIX_SCALES + T - LAP
-ENG_WORDS = PIX1 + 4 * T
-WS_BF0 = ENG_WORDS + 2 * T
-WF_RAW = WS_BF0 + 8 * HALF
-PICKED1 = WF_RAW + 4 * H
+WS_BF1 = PIX1 + 4 * T
+WS_BF0 = WS_BF1 + 8 * HALF
+PICKED1 = WS_BF0 + 8 * HALF
 PIECES = ((0, 256), (256, 128), (384, 128))
-EARLY = {(0, 0): (1, 3), (0, 1): (0,), (1, 0): (0, 1, 2), (1, 1): ()}
+EARLY = {(0, 0): (0, 2), (0, 1): (0, 3), (1, 0): (0, 1, 2), (1, 1): ()}
 
 
 def tile_list_transit_template_detrending_kernel(
@@ -56,7 +55,7 @@ def tile_list_transit_template_detrending_kernel(
 
         pix_list = keep.tile([P, S // 16], U16, name="pix_list")
         eng_list = keep.tile([P, S // 16], U16, name="eng_list")
-        eng_words = placed([P, T], U16, "eng_words", ENG_WORDS)
+        eng_words = held([P, T], U16, "eng_words")
         eng_scales = placed([P, T], U8, "eng_scales", ENG_SCALES)
         pix_scales = placed([P, T], U8, "pix_scales", PIX_SCALES)
         ws_raw = [held([P, PACK, HALF], F32, "ws_raw0")]
@@ -66,34 +65,38 @@ def tile_list_transit_template_detrending_kernel(
         warm_in = held([P, 16], F32, "warm_in")
 
         nc.vector.memset(warm_in[:], 1.0)
-        nc.vector.memset(eng_scales[:].bitcast(I32), 0)
-        nc.vector.memset(pix_scales[:].bitcast(I32), 0)
+        nc.vector.memset(eng_scales[0:ENG_ROW, :].bitcast(I32), 0)
+        nc.gpsimd.memset(pix_scales[0:PIX_ROW, :].bitcast(I32), 0)
         nc.vector.memset(eng_plane[:].bitcast(I32), 0)
         nc.vector.memset(pix_planes[:].bitcast(I32), 0)
 
-        def load_scale_rows(tile, dram, first, spread):
-            nc.scalar.dma_start(tile[first:P:spread, :].bitcast(I32), dram.rearrange("a q c -> (a q) c").bitcast(I32))
+        def load_scale_rows(tile, dram, first):
+            nc.sync.dma_start(tile[first:P, :].bitcast(I32), dram.rearrange("a q c -> (a q) c").bitcast(I32))
 
-        def move_picked_rows(plane, picked, first, spread):
+        def move_picked_rows(plane, picked, first):
             for s in range(4):
-                rows = slice(first + spread * s, first + spread * (12 + s) + 1, 4 * spread)
+                rows = slice(first + s, first + 16, 4)
                 nc.sync.dma_start(plane[s:P:32, :].bitcast(I32), picked[rows, :].bitcast(I32))
+
+        def load_flux_weights(b):
+            words = wf_words[:, :, 2 * b * HALF:2 * (b + 1) * HALF].rearrange("a p c -> p a c")
+            nc.sync.dma_start(wf_raw[b][:].bitcast(I32), words.bitcast(I32))
 
         def load_pixels(a, c0, c1):
             nc.sync.dma_start(pix_words[a][:, c0:c1], tab_words[a, :, c0:c1].rearrange("p t i -> p (t i)").bitcast(I32))
 
         ws_rows = ws.rearrange("(p i) c -> p i c", i=PACK)
         nc.sync.dma_start(eng_list[:], offs2)
-        nc.scalar.dma_start(gain_sb[:, :, 0:PACK], gain.rearrange("(b p t) -> p b t", b=2, t=PACK))
+        load_scale_rows(eng_scales, tab2_scales, ENG_ROW)
         nc.sync.dma_start(pix_list[:], offs)
+        load_scale_rows(pix_scales, tab_scales, PIX_ROW)
+        nc.sync.dma_start(gain_sb[:, :, 0:PACK], gain.rearrange("(b p t) -> p b t", b=2, t=PACK))
         nc.sync.dma_start(ws_raw[0][:], ws_rows[:, :, 0:HALF])
         nc.sync.dma_start(eng_words[:].bitcast(I32), tab2_words[0].bitcast(I32))
-        wf_raw = placed([P, 2, H], U16, "wf_raw", WF_RAW)
-        nc.sync.dma_start(wf_raw[:].bitcast(I32), wf_words.rearrange("a p c -> p a c").bitcast(I32))
+        wf_raw = [held([P, 2, HALF], U16, "wf_raw0")]
+        load_flux_weights(0)
         warm_out = held([P, 16], F32, "warm_out")
         nc.scalar.activation(warm_out[:], warm_in[:], ACT.Abs_reciprocal_sqrt)
-        load_scale_rows(eng_scales, tab2_scales, 4, 8)
-        load_scale_rows(pix_scales, tab_scales, 0, 4)
 
         gain_all = gain_sb[:, :, 0:PACK]
         gain_neg = held([P, 2, PACK], F32, "gain_neg")
@@ -108,17 +111,26 @@ def tile_list_transit_template_detrending_kernel(
         ws_codes = [held([P, HALF], U32, "ws_codes%d" % b) for b in range(2)]
         eng_picked_scales = held([P, S], U8, "eng_picked_scales")
         nc.vector.tensor_copy(eng_picked_scales[:], eng_scales[:].indirect(eng_list[:]))
-        move_picked_rows(eng_plane[:], eng_picked_scales, 4, 8)
+        move_picked_rows(eng_plane[:], eng_picked_scales, ENG_ROW)
         ws_raw.append(placed([P, PACK, HALF], F32, "ws_raw1", WS_RAW1))
         nc.sync.dma_start(ws_raw[1][:], ws_rows[:, :, HALF:H])
         wf_raw_scales = placed([P, 2 * H], U8, "wf_raw_scales", ENG_SCALES + 1600)
-        nc.vector.memset(wf_raw_scales[:].bitcast(I32), 0)
+        nc.gpsimd.memset(wf_raw_scales[:].bitcast(I32), 0)
         wf_scale_rows = wf_scales.rearrange("a (q s) c -> s q a c", s=4)
         for s in range(4):
             nc.sync.dma_start(wf_raw_scales[s:P:32, :].rearrange("q (a c) -> q a c", a=2).bitcast(I32),
                               wf_scale_rows[s].bitcast(I32))
-        pix_words = [placed([P, T], I32, "pix_words0", PIX0)]
-        load_pixels(0, 0, T)
+
+        pix_picked_scales = held([P, S], U8, "pix_picked_scales")
+        nc.vector.tensor_copy(pix_picked_scales[:], pix_scales[:].indirect(pix_list[:]))
+        pix_words = [placed([P, T], I32, "pix_words%d" % a, offset) for a, offset in enumerate((PIX0, PIX1))]
+        load_pixels(0, 0, T // 2)
+        move_picked_rows(pix_planes[:, 0:S], pix_picked_scales, PIX_ROW)
+        load_pixels(0, T // 2, T)
+        load_pixels(1, 0, T)
+        move_picked_rows(pix_planes[:, S:2 * S], pix_picked_scales, PIX_ROW + 16)
+        wf_raw.append(placed([P, 2, HALF], U16, "wf_raw1", PIX_SCALES + LAP))
+        load_flux_weights(1)
 
         def round_ws(b, ws_bf, copy):
             for u in range(2):
@@ -132,9 +144,9 @@ def tile_list_transit_template_detrending_kernel(
             eng_picked.append(placed([P, HALF], U16, "eng_picked%d" % jh, offset))
             nc.vector.tensor_copy(eng_picked[jh][:], eng_words[:].indirect(eng_list[:, jh * LIST_COLS:(jh + 1) * LIST_COLS]))
 
-        def deal_flux_weights(b, copy):
-            copy(wf_codes[b][:].rearrange("p a (t m) -> p a t m", t=PACK),
-                 wf_raw[:, :, b * HALF:(b + 1) * HALF].rearrange("p a (m t) -> p a t m", t=PACK))
+        def deal_flux_weights(b):
+            nc.scalar.copy(wf_codes[b][:].rearrange("p a (t m) -> p a t m", t=PACK),
+                 wf_raw[b][:].rearrange("p a (m t) -> p a t m", t=PACK))
 
         def systematics(b):
             for jh in range(2):
@@ -153,19 +165,12 @@ def tile_list_transit_template_detrending_kernel(
         ws_scales = [placed([P, HALF], U8, "ws_scales0", ENG_SCALES + LAP), held([P, HALF], U8, "ws_scales1")]
         ws_bf0 = placed([P, 2, PACK * HALF // 2], BF16, "ws_bf0", WS_BF0)
         round_ws(0, ws_bf0, nc.scalar.copy)
-        wf_codes = [held([P, 2, HALF], U16, "wf_codes0")]
-        deal_flux_weights(0, nc.scalar.copy)
+        wf_codes = [held([P, 2, HALF], U16, "wf_codes%d" % b) for b in range(2)]
+        deal_flux_weights(0)
         gather_engineering(0, ENG_SCALES + 576)
         quantise_ws(0, ws_bf0)
         gather_engineering(1, WS_BF0)
         systematics(0)
-
-        pix_picked_scales = placed([P, S], U8, "pix_picked_scales", ENG_WORDS)
-        nc.vector.tensor_copy(pix_picked_scales[:], pix_scales[:].indirect(pix_list[:]))
-        pix_words.append(placed([P, T], I32, "pix_words1", PIX1))
-        move_picked_rows(pix_planes[:, 0:S], pix_picked_scales, 0, 4)
-        load_pixels(1, 0, T)
-        move_picked_rows(pix_planes[:, S:2 * S], pix_picked_scales, 64, 4)
 
         ws_bf1 = placed([P, 2, PACK * HALF // 2], BF16, "ws_bf1", WS_BF1)
         round_ws(1, ws_bf1, nc.vector.tensor_copy)
@@ -174,11 +179,10 @@ def tile_list_transit_template_detrending_kernel(
                               wf_raw_scales[:].rearrange("p (ab m t) -> p ab t m", ab=4, t=PACK))
         quantise_ws(1, ws_bf1)
         systematics(1)
-        wf_codes.append(placed([P, 2, HALF], U16, "wf_codes1", WS_BF1))
-        deal_flux_weights(1, nc.vector.tensor_copy)
+        deal_flux_weights(1)
 
         wt_scales_sb = placed([P, 2 * N], U8, "wt_scales_sb", ENG_SCALES + 1600)
-        nc.vector.memset(wt_scales_sb[:].bitcast(I32), 0)
+        nc.gpsimd.memset(wt_scales_sb[:].bitcast(I32), 0)
         for q in range(4):
             nc.sync.dma_start(wt_scales_sb[32 * q:32 * q + 4, :].rearrange("s (b c) -> s b c", b=2).bitcast(I32),
                               wt_scales[:, 4 * q:4 * q + 4, :].rearrange("b s c -> s b c").bitcast(I32))
@@ -204,13 +208,13 @@ def tile_list_transit_template_detrending_kernel(
 
         def flux(jh):
             sums = [[bank(b * PACK + t, [P, HALF]) for t in range(PACK)] for b in range(2)]
-            for b in range(2):
-                for t in range(PACK):
-                    flux_pass(sums[b][t], jh, b, t, 0)
+            for t in range(PACK):
+                flux_pass(sums[0][t], jh, 0, t, 0)
             gather_pixels(1, jh, PICKED1)
             for b in range(2):
                 for t in range(PACK):
-                    flux_pass(sums[b][t], jh, b, t, 1)
+                    for a in range(1 - b, 2):
+                        flux_pass(sums[b][t], jh, b, t, a)
                     tile = resid[jh][b][:, t, :]
                     nc.vector.scalar_tensor_tensor(tile, sums[b][t][:], gain_neg[:, b, t:t + 1], tile, ALU.mult, ALU.add)
                     if t in EARLY[jh, b]:
@@ -222,14 +226,20 @@ def tile_list_transit_template_detrending_kernel(
         def inverse_root(y, x):
             nc.scalar.activation(y, x, ACT.Abs_reciprocal_sqrt, bias=1.0)
 
-        def roots(jh, b, rest):
+        def roots(jh, b, runs):
             tile = root[jh][b]
-            for t in range(PACK)[rest]:
-                square_residual(jh, b, t)
+            for run in runs:
+                for t in range(PACK)[run]:
+                    square_residual(jh, b, t)
             for t in EARLY[jh, b]:
                 nc.scalar.activation(tile[:, t, :], tile[:, t, :], ACT.Abs_reciprocal_sqrt, bias=1.0,
                                      scale=gain_inv_sq[:, b, t:t + 1])
-            inverse_root(tile[:, rest, :], tile[:, rest, :])
+            for run in runs:
+                inverse_root(tile[:, run, :], tile[:, run, :])
+
+        def weight_half(jh, b, k, tag=""):
+            tile = held([P, PACK, HALF // 2], F32, "weight%d%d%d" % (jh, b, k), tag)
+            return tile[:], root[jh][b][:, :, k * HALF // 2:(k + 1) * HALF // 2]
 
         def multiply(h, jh, b, cols, weights):
             nc.vector.tensor_tensor(h.rearrange("p (c e t) -> p c t e", e=2, t=PACK),
@@ -239,11 +249,11 @@ def tile_list_transit_template_detrending_kernel(
         def quantise_h(h, jh, b, cols):
             nc.vector.quantize_mx(h_codes[jh][b][:, cols].bitcast(FP8X4), h_scales[jh][b][:, cols], h)
 
-        def damp(jh, b, weight, h_tag):
+        def damp(jh, b, weights, h_tag):
             h = held([P, PACK * HALF], BF16, "h%d%d" % (jh, b), h_tag)
             halves = [slice(c, c + HALF // 2) for c in (0, HALF // 2)]
-            for cols in halves:
-                multiply(h[:, PACK * cols.start:PACK * cols.stop], jh, b, cols, weight[:, :, cols])
+            for cols, weight in zip(halves, weights):
+                multiply(h[:, PACK * cols.start:PACK * cols.stop], jh, b, cols, weight)
             for cols in halves:
                 quantise_h(h[:, PACK * cols.start:PACK * cols.stop], jh, b, cols)
 
@@ -280,7 +290,7 @@ def tile_list_transit_template_detrending_kernel(
             store(jh, c0, width)
 
         for jh in range(2):
-            gather_pixels(0, jh, WF_RAW + jh * 4 * HALF)
+            gather_pixels(0, jh, WS_BF1 + jh * 4 * HALF)
         wt_codes = placed([P, 2, N], I32, "wt_codes", PIX0)
         nc.sync.dma_start(wt_codes[:], wt_words.rearrange("b p c i -> p b (c i)").bitcast(I32))
         for jh in range(2):
@@ -288,21 +298,23 @@ def tile_list_transit_template_detrending_kernel(
         cat_sb = placed([P, N // P, S], F32, "cat_sb", PIX1)
         nc.sync.dma_start(cat_sb[:], cat.rearrange("(nt p) j -> p nt j", p=P))
 
-        for b, rest in enumerate((slice(0, PACK, 2), slice(1, PACK))):
-            roots(0, b, rest)
-            nc.scalar.activation(root[0][b][:], root[0][b][:], ACT.Square)
-            damp(0, b, root[0][b], "h_%d" % b)
+        for b, runs in enumerate(([slice(1, PACK, 2)], [slice(1, 3)])):
+            roots(0, b, runs)
+            halves = [weight_half(0, b, k) for k in range(2)]
+            for y, x in halves:
+                nc.scalar.activation(y, x, ACT.Square)
+            damp(0, b, [y for y, x in halves], "h_%d" % b)
         half_sums = [template_sums(0, c0, HALF // 2, c0 // P) for c0 in (0, HALF // 2)]
         for b in range(2):
             for k in range(2):
                 template_passes(half_sums[k], 0, k * HALF // 2, HALF // 2, b)
         for k in range(2):
             finish(half_sums[k], 0, k * HALF // 2, HALF // 2)
-        roots(1, 0, slice(3, PACK))
-        weight = held([P, PACK, HALF], F32, "weight10", "h_1")
-        nc.gpsimd.tensor_tensor(weight[:, 0:2, :], root[1][0][:, 0:2, :], root[1][0][:, 0:2, :], ALU.mult)
-        nc.scalar.activation(weight[:, 2:4, :], root[1][0][:, 2:4, :], ACT.Square)
-        damp(1, 0, weight, "h_0")
+        roots(1, 0, [slice(3, PACK)])
+        (y0, x0), (y1, x1) = weight_half(1, 0, 0), weight_half(1, 0, 1, "h_1")
+        nc.scalar.activation(y0, x0, ACT.Square)
+        nc.gpsimd.tensor_tensor(y1, x1, x1, ALU.mult)
+        damp(1, 0, [y0, y1], "h_0")
         piece_sums = [template_sums(1, c0, width, PACK + c0 // P) for c0, width in PIECES[:2]]
         last_sums = [bank(k, [P, 2, P]) for k in (7, 0)]
 

@@ -26,12 +26,13 @@ WS_RAW1 = 0
 ENG_SCALES = WS_RAW1 + 16 * HALF - LAP
 PIX0 = ENG_SCALES + T
 PIX_SCALES = PIX0 + 4 * T - LAP
-PIX1 = PIX_SCALES + T - LAP
+ENG_WORDS = PIX_SCALES + T
+PIX1 = ENG_WORDS + 2 * T - LAP
 WS_BF1 = PIX1 + 4 * T
 WS_BF0 = WS_BF1 + 8 * HALF
 PICKED1 = WS_BF0 + 8 * HALF
 PIECES = ((0, 256), (256, 128), (384, 128))
-EARLY = {(0, 0): (0, 2), (0, 1): (0, 3), (1, 0): (0, 1, 2), (1, 1): ()}
+EARLY = {(0, 0): (0, 3), (0, 1): (0, 2), (1, 0): (0, 1, 2), (1, 1): ()}
 
 
 def tile_list_transit_template_detrending_kernel(
@@ -55,20 +56,20 @@ def tile_list_transit_template_detrending_kernel(
 
         pix_list = keep.tile([P, S // 16], U16, name="pix_list")
         eng_list = keep.tile([P, S // 16], U16, name="eng_list")
-        eng_words = held([P, T], U16, "eng_words")
+        eng_words = placed([P, T], U16, "eng_words", ENG_WORDS)
         eng_scales = placed([P, T], U8, "eng_scales", ENG_SCALES)
         pix_scales = placed([P, T], U8, "pix_scales", PIX_SCALES)
         ws_raw = [held([P, PACK, HALF], F32, "ws_raw0")]
         gain_sb = held([P, 2, 2 * PACK], F32, "gain_sb")
         eng_plane = held([P, S], U8, "eng_plane")
-        pix_planes = held([P, 2 * S], U8, "pix_planes")
+        pix_planes = [held([P, S], U8, "pix_plane0")]
         warm_in = held([P, 16], F32, "warm_in")
 
         nc.vector.memset(warm_in[:], 1.0)
         nc.vector.memset(eng_scales[0:ENG_ROW, :].bitcast(I32), 0)
         nc.gpsimd.memset(pix_scales[0:PIX_ROW, :].bitcast(I32), 0)
         nc.vector.memset(eng_plane[:].bitcast(I32), 0)
-        nc.vector.memset(pix_planes[:].bitcast(I32), 0)
+        nc.vector.memset(pix_planes[0][:].bitcast(I32), 0)
 
         def load_scale_rows(tile, dram, first):
             nc.sync.dma_start(tile[first:P, :].bitcast(I32), dram.rearrange("a q c -> (a q) c").bitcast(I32))
@@ -99,12 +100,13 @@ def tile_list_transit_template_detrending_kernel(
         nc.scalar.activation(warm_out[:], warm_in[:], ACT.Abs_reciprocal_sqrt)
 
         gain_all = gain_sb[:, :, 0:PACK]
-        gain_neg = held([P, 2, PACK], F32, "gain_neg")
+        gain_neg = [placed([P, 2, PACK], F32, "gain_neg_first", PICKED1 + 4 * HALF), held([P, 2, PACK], F32, "gain_neg")]
         gain_safe = held([P, 2, PACK], F32, "gain_safe")
         gain_inv = held([P, 2, PACK], F32, "gain_inv")
         gain_inv_sq = held([P, 2, PACK], F32, "gain_inv_sq")
         nc.vector.scalar_tensor_tensor(gain_safe[:], gain_all, 0.0, gain_all, ALU.is_equal, ALU.add)
-        nc.vector.tensor_scalar(gain_neg[:], gain_all, -1.0, None, ALU.mult)
+        for tile in gain_neg:
+            nc.vector.tensor_scalar(tile[:], gain_all, -1.0, None, ALU.mult)
         nc.vector.reciprocal(gain_inv[:], gain_safe[:])
         nc.vector.tensor_tensor(gain_inv_sq[:], gain_inv[:], gain_inv[:], ALU.mult)
 
@@ -123,14 +125,9 @@ def tile_list_transit_template_detrending_kernel(
 
         pix_picked_scales = held([P, S], U8, "pix_picked_scales")
         nc.vector.tensor_copy(pix_picked_scales[:], pix_scales[:].indirect(pix_list[:]))
-        pix_words = [placed([P, T], I32, "pix_words%d" % a, offset) for a, offset in enumerate((PIX0, PIX1))]
-        load_pixels(0, 0, T // 2)
-        move_picked_rows(pix_planes[:, 0:S], pix_picked_scales, PIX_ROW)
-        load_pixels(0, T // 2, T)
-        load_pixels(1, 0, T)
-        move_picked_rows(pix_planes[:, S:2 * S], pix_picked_scales, PIX_ROW + 16)
-        wf_raw.append(placed([P, 2, HALF], U16, "wf_raw1", PIX_SCALES + LAP))
-        load_flux_weights(1)
+        pix_words = [placed([P, T], I32, "pix_words0", PIX0)]
+        load_pixels(0, 0, T)
+        move_picked_rows(pix_planes[0][:], pix_picked_scales, PIX_ROW)
 
         def round_ws(b, ws_bf, copy):
             for u in range(2):
@@ -170,19 +167,24 @@ def tile_list_transit_template_detrending_kernel(
         gather_engineering(0, ENG_SCALES + 576)
         quantise_ws(0, ws_bf0)
         gather_engineering(1, WS_BF0)
+        pix_words.append(placed([P, T], I32, "pix_words1", PIX1))
+        load_pixels(1, 0, T)
         systematics(0)
 
         ws_bf1 = placed([P, 2, PACK * HALF // 2], BF16, "ws_bf1", WS_BF1)
         round_ws(1, ws_bf1, nc.vector.tensor_copy)
         wf_scales_sb = placed([P, 2, H], U8, "wf_scales_sb", WS_RAW1)
-        nc.vector.tensor_copy(wf_scales_sb[:].rearrange("p a (b t m) -> p (a b) t m", b=2, t=PACK),
-                              wf_raw_scales[:].rearrange("p (ab m t) -> p ab t m", ab=4, t=PACK))
+        nc.vector.tensor_copy(wf_scales_sb[:].rearrange("p a (b t k e) -> p (a b) k t e", b=2, t=PACK, e=4),
+                              wf_raw_scales[:].rearrange("p (ab k e t) -> p ab k t e", ab=4, t=PACK, e=4))
         quantise_ws(1, ws_bf1)
+        pix_planes.append(placed([P, S], U8, "pix_plane1", WS_RAW1 + 4 * HALF))
+        move_picked_rows(pix_planes[1][:], pix_picked_scales, PIX_ROW + 16)
+        wf_raw.append(placed([P, 2, HALF], U16, "wf_raw1", WS_BF1 + 4 * HALF))
+        load_flux_weights(1)
         systematics(1)
         deal_flux_weights(1)
 
         wt_scales_sb = placed([P, 2 * N], U8, "wt_scales_sb", ENG_SCALES + 1600)
-        nc.gpsimd.memset(wt_scales_sb[:].bitcast(I32), 0)
         for q in range(4):
             nc.sync.dma_start(wt_scales_sb[32 * q:32 * q + 4, :].rearrange("s (b c) -> s b c", b=2).bitcast(I32),
                               wt_scales[:, 4 * q:4 * q + 4, :].rearrange("b s c -> s b c").bitcast(I32))
@@ -197,28 +199,20 @@ def tile_list_transit_template_detrending_kernel(
             entries = pix_list[:, jh * LIST_COLS:(jh + 1) * LIST_COLS]
             nc.vector.tensor_copy(pix_picked[a, jh][:], pix_words[a][:].bitcast(U32).indirect(entries))
 
-        def flux_pass(acc, jh, b, t, a):
+        def flux_pass(acc, jh, b, t, a, opens):
             cols = slice(b * HALF + t * P, b * HALF + (t + 1) * P)
             nc.tensor.matmul_mx(acc[:], lhsT=wf_codes[b][:, a, t * P:(t + 1) * P].bitcast(FP4X4), lhsT_scale=wf_scales_sb[:, a, cols],
                                 rhs=pix_picked[a, jh][:].bitcast(FP8X4),
-                                rhs_scale=pix_planes[:, a * S + jh * HALF:a * S + (jh + 1) * HALF],
-                                start=(a == 0), stop=(a == 1))
+                                rhs_scale=pix_planes[a][:, jh * HALF:(jh + 1) * HALF],
+                                start=opens, stop=not opens)
 
-        root = [[held([P, PACK, HALF], F32, "root%d%d" % (jh, b)) for b in range(2)] for jh in range(2)]
+        root = [[held([P, PACK, HALF], F32, "root%d%d" % (jh, b)) for b in range(2 - jh)] for jh in range(2)]
 
-        def flux(jh):
-            sums = [[bank(b * PACK + t, [P, HALF]) for t in range(PACK)] for b in range(2)]
-            for t in range(PACK):
-                flux_pass(sums[0][t], jh, 0, t, 0)
-            gather_pixels(1, jh, PICKED1)
-            for b in range(2):
-                for t in range(PACK):
-                    for a in range(1 - b, 2):
-                        flux_pass(sums[b][t], jh, b, t, a)
-                    tile = resid[jh][b][:, t, :]
-                    nc.vector.scalar_tensor_tensor(tile, sums[b][t][:], gain_neg[:, b, t:t + 1], tile, ALU.mult, ALU.add)
-                    if t in EARLY[jh, b]:
-                        nc.gpsimd.tensor_tensor(root[jh][b][:, t, :], tile, tile, ALU.mult)
+        def subtract_flux(acc, jh, b, t):
+            tile = resid[jh][b][:, t, :]
+            nc.vector.scalar_tensor_tensor(tile, acc[:], gain_neg[(jh, b) != (0, 0)][:, b, t:t + 1], tile, ALU.mult, ALU.add)
+            if t in EARLY[jh, b]:
+                nc.gpsimd.tensor_tensor(root[jh][b][:, t, :], tile, tile, ALU.mult)
 
         def square_residual(jh, b, t):
             nc.scalar.activation(root[jh][b][:, t, :], resid[jh][b][:, t, :], ACT.Square, scale=gain_inv[:, b, t:t + 1])
@@ -249,12 +243,13 @@ def tile_list_transit_template_detrending_kernel(
         def quantise_h(h, jh, b, cols):
             nc.vector.quantize_mx(h_codes[jh][b][:, cols].bitcast(FP8X4), h_scales[jh][b][:, cols], h)
 
-        def damp(jh, b, weights, h_tag):
+        def damp(jh, b, weights, h_tag, quantises):
             h = held([P, PACK * HALF], BF16, "h%d%d" % (jh, b), h_tag)
-            halves = [slice(c, c + HALF // 2) for c in (0, HALF // 2)]
-            for cols, weight in zip(halves, weights):
+            for k, weight in enumerate(weights):
+                cols = slice(k * HALF // len(weights), (k + 1) * HALF // len(weights))
                 multiply(h[:, PACK * cols.start:PACK * cols.stop], jh, b, cols, weight)
-            for cols in halves:
+            for k in range(quantises):
+                cols = slice(k * HALF // quantises, (k + 1) * HALF // quantises)
                 quantise_h(h[:, PACK * cols.start:PACK * cols.stop], jh, b, cols)
 
         def template_pass(acc, jh, c0, width, nt, b, start, stop):
@@ -290,20 +285,37 @@ def tile_list_transit_template_detrending_kernel(
             store(jh, c0, width)
 
         for jh in range(2):
-            gather_pixels(0, jh, WS_BF1 + jh * 4 * HALF)
+            gather_pixels(0, jh, (WS_BF1, WS_RAW1 + 8 * HALF)[jh])
         wt_codes = placed([P, 2, N], I32, "wt_codes", PIX0)
         nc.sync.dma_start(wt_codes[:], wt_words.rearrange("b p c i -> p b (c i)").bitcast(I32))
+        sums = [[bank(jh * PACK + t, [P, HALF]) for t in range(PACK)] for jh in range(2)]
         for jh in range(2):
-            flux(jh)
+            for t in range(PACK):
+                flux_pass(sums[jh][t], jh, 0, t, 0, True)
+        for jh in range(2):
+            if jh == 0:
+                gather_pixels(1, 0, PICKED1)
+            for t in range(PACK):
+                flux_pass(sums[jh][t], jh, 0, t, 1, False)
+                subtract_flux(sums[jh][t], jh, 0, t)
+            if jh == 0:
+                gather_pixels(1, 1, PICKED1 + 4 * HALF)
+            for t in range(PACK):
+                acc = bank(t, [P, HALF])
+                for a in range(2):
+                    flux_pass(acc, jh, 1, t, a, a == 0)
+                subtract_flux(acc, jh, 1, t)
         cat_sb = placed([P, N // P, S], F32, "cat_sb", PIX1)
         nc.sync.dma_start(cat_sb[:], cat.rearrange("(nt p) j -> p nt j", p=P))
 
-        for b, runs in enumerate(([slice(1, PACK, 2)], [slice(1, 3)])):
-            roots(0, b, runs)
-            halves = [weight_half(0, b, k) for k in range(2)]
-            for y, x in halves:
-                nc.scalar.activation(y, x, ACT.Square)
-            damp(0, b, [y for y, x in halves], "h_%d" % b)
+        roots(0, 0, [slice(1, 3)])
+        nc.scalar.activation(root[0][0][:], root[0][0][:], ACT.Square)
+        damp(0, 0, [root[0][0][:]], "h_0", 1)
+        roots(0, 1, [slice(1, PACK, 2)])
+        (y0, x0), (y1, x1) = weight_half(0, 1, 0), weight_half(0, 1, 1)
+        nc.scalar.activation(y0, x0, ACT.Square)
+        nc.vector.tensor_tensor(y1, x1, x1, ALU.mult)
+        damp(0, 1, [y0, y1], "h_1", 2)
         half_sums = [template_sums(0, c0, HALF // 2, c0 // P) for c0 in (0, HALF // 2)]
         for b in range(2):
             for k in range(2):
@@ -314,7 +326,7 @@ def tile_list_transit_template_detrending_kernel(
         (y0, x0), (y1, x1) = weight_half(1, 0, 0), weight_half(1, 0, 1, "h_1")
         nc.scalar.activation(y0, x0, ACT.Square)
         nc.gpsimd.tensor_tensor(y1, x1, x1, ALU.mult)
-        damp(1, 0, [y0, y1], "h_0")
+        damp(1, 0, [y0, y1], "h_0", 1)
         piece_sums = [template_sums(1, c0, width, PACK + c0 // P) for c0, width in PIECES[:2]]
         last_sums = [bank(k, [P, 2, P]) for k in (7, 0)]
 
@@ -326,26 +338,30 @@ def tile_list_transit_template_detrending_kernel(
         for sums, (c0, width) in zip(piece_sums, PIECES):
             template_passes(sums, 1, c0, width, 0)
         last_passes(0)
-        for t in range(PACK):
-            square_residual(1, 1, t)
         for k, (c0, width) in enumerate(PIECES):
             cols = slice(c0, c0 + width)
+            if c0 % (HALF // 2) == 0:
+                squared = held([P, PACK, HALF // 2], F32, "squared%d" % k)
+                for t in range(PACK):
+                    nc.scalar.activation(squared[:, t, :], resid[1][1][:, t, c0:c0 + HALF // 2], ACT.Square,
+                                         scale=gain_inv[:, 1, t:t + 1])
             weight = held([P, PACK, width], F32, "weight11_%d" % k)
-            inverse_root(weight[:], root[1][1][:, :, cols])
+            inverse_root(weight[:], squared[:, :, c0 % (HALF // 2):c0 % (HALF // 2) + width])
             nc.scalar.activation(weight[:], weight[:], ACT.Square)
-            h = held([P, PACK * width], BF16, "h11_%d" % k, ("h_1", "", "last")[k])
+            h = held([P, PACK * width], BF16, "h11_%d" % k, ("h_1", "middle", "last")[k])
             multiply(h[:], 1, 1, cols, weight[:])
             quantise_h(h[:], 1, 1, cols)
             if k < 2:
                 template_passes(piece_sums[k], 1, c0, width, 1)
-            if k == 0:
-                finish(piece_sums[k], 1, c0, width)
         last_passes(1)
-        c0, width = PIECES[1]
-        staged = held([P, N // P, width], F32, "staged", "last")
-        entries = slice(HALF + c0, HALF + c0 + width)
-        nc.vector.tensor_tensor(staged[:], piece_sums[1][0][:], cat_sb[:, :, entries], ALU.add)
-        nc.sync.dma_start(out_rows[:, :, entries], staged[:])
+        for sums, (c0, width), tag in zip(piece_sums, PIECES, ("middle", "last")):
+            staged = held([P, N // P, width], F32, "staged_" + tag, tag)
+            entries = slice(HALF + c0, HALF + c0 + width)
+            per_bank = HALF // width
+            for k, acc in enumerate(sums):
+                rows = slice(k * per_bank, (k + 1) * per_bank)
+                nc.vector.tensor_tensor(staged[:, rows, :], acc[:], cat_sb[:, rows, entries], ALU.add)
+                nc.sync.dma_start(out_rows[:, rows, entries], staged[:, rows, :])
         c0, width = PIECES[2]
         entries = slice(HALF + c0, HALF + c0 + width)
         for k in range(2):

@@ -32,7 +32,7 @@ WS_BF1 = PIX1 + 4 * T
 WS_BF0 = WS_BF1 + 8 * HALF
 PICKED1 = WS_BF0 + 8 * HALF
 PIECES = ((0, 256), (256, 128), (384, 128))
-EARLY = {(0, 0): (0, 3), (0, 1): (0, 2), (1, 0): (0, 1, 2), (1, 1): ()}
+EARLY = {(0, 0): (1, 3), (0, 1): (0, 2), (1, 0): (0, 1, 2), (1, 1): ()}
 
 
 def tile_list_transit_template_detrending_kernel(
@@ -308,7 +308,7 @@ def tile_list_transit_template_detrending_kernel(
         cat_sb = placed([P, N // P, S], F32, "cat_sb", PIX1)
         nc.sync.dma_start(cat_sb[:], cat.rearrange("(nt p) j -> p nt j", p=P))
 
-        roots(0, 0, [slice(1, 3)])
+        roots(0, 0, [slice(0, PACK, 2)])
         nc.scalar.activation(root[0][0][:], root[0][0][:], ACT.Square)
         damp(0, 0, [root[0][0][:]], "h_0", 1)
         roots(0, 1, [slice(1, PACK, 2)])
@@ -326,18 +326,10 @@ def tile_list_transit_template_detrending_kernel(
         (y0, x0), (y1, x1) = weight_half(1, 0, 0), weight_half(1, 0, 1, "h_1")
         nc.scalar.activation(y0, x0, ACT.Square)
         nc.gpsimd.tensor_tensor(y1, x1, x1, ALU.mult)
-        damp(1, 0, [y0, y1], "h_0", 1)
-        piece_sums = [template_sums(1, c0, width, PACK + c0 // P) for c0, width in PIECES[:2]]
-        last_sums = [bank(k, [P, 2, P]) for k in (7, 0)]
-
-        def last_passes(b):
-            for nt in range(N // P):
-                template_pass(last_sums[nt // 2][:, nt % 2, :], 1, PIECES[2][0], P, nt, b,
-                              b == 0 and nt % 2 == 0, b == 1 and nt % 2 == 1)
-
-        for sums, (c0, width) in zip(piece_sums, PIECES):
-            template_passes(sums, 1, c0, width, 0)
-        last_passes(0)
+        damp(1, 0, [y0, y1], "h_0", 2)
+        half_sums = [template_sums(1, c0, HALF // 2, PACK + c0 // P) for c0 in (0, HALF // 2)]
+        for k in range(2):
+            template_passes(half_sums[k], 1, k * HALF // 2, HALF // 2, 0)
         for k, (c0, width) in enumerate(PIECES):
             cols = slice(c0, c0 + width)
             if c0 % (HALF // 2) == 0:
@@ -348,22 +340,19 @@ def tile_list_transit_template_detrending_kernel(
             weight = held([P, PACK, width], F32, "weight11_%d" % k)
             inverse_root(weight[:], squared[:, :, c0 % (HALF // 2):c0 % (HALF // 2) + width])
             nc.scalar.activation(weight[:], weight[:], ACT.Square)
-            h = held([P, PACK * width], BF16, "h11_%d" % k, ("h_1", "middle", "last")[k])
+            h = held([P, PACK * width], BF16, "h11_%d" % k, ("h_1", "middle", "")[k])
             multiply(h[:], 1, 1, cols, weight[:])
             quantise_h(h[:], 1, 1, cols)
-            if k < 2:
-                template_passes(piece_sums[k], 1, c0, width, 1)
-        last_passes(1)
-        for sums, (c0, width), tag in zip(piece_sums, PIECES, ("middle", "last")):
-            staged = held([P, N // P, width], F32, "staged_" + tag, tag)
-            entries = slice(HALF + c0, HALF + c0 + width)
-            per_bank = HALF // width
-            for k, acc in enumerate(sums):
-                rows = slice(k * per_bank, (k + 1) * per_bank)
-                nc.vector.tensor_tensor(staged[:, rows, :], acc[:], cat_sb[:, rows, entries], ALU.add)
-                nc.sync.dma_start(out_rows[:, rows, entries], staged[:, rows, :])
-        c0, width = PIECES[2]
-        entries = slice(HALF + c0, HALF + c0 + width)
+            offset = c0 % (HALF // 2)
+            for nt in range(N // P):
+                template_pass(half_sums[c0 // (HALF // 2)][nt // 2][:, nt % 2, offset:offset + width], 1, c0, width, nt, 1,
+                              False, nt % 2 == 1 and offset + width == HALF // 2)
+        staged = held([P, N // P, HALF // 2], F32, "staged", "middle")
         for k in range(2):
-            add_catalogue(last_sums[k][:], 1, c0, width, 2 * k, 2 * k + 2)
-            nc.sync.dma_start(out_rows[:, 2 * k:2 * k + 2, entries], cat_sb[:, 2 * k:2 * k + 2, entries])
+            rows, entries = slice(2 * k, 2 * k + 2), slice(HALF, HALF + HALF // 2)
+            nc.vector.tensor_tensor(staged[:, rows, :], half_sums[0][k][:], cat_sb[:, rows, entries], ALU.add)
+            nc.sync.dma_start(out_rows[:, rows, entries], staged[:, rows, :])
+        for k in range(2):
+            rows, entries = slice(2 * k, 2 * k + 2), slice(HALF + HALF // 2, S)
+            add_catalogue(half_sums[1][k][:], 1, HALF // 2, HALF // 2, 2 * k, 2 * k + 2)
+            nc.sync.dma_start(out_rows[:, rows, entries], cat_sb[:, rows, entries])

@@ -310,11 +310,12 @@ def tile_list_transit_template_detrending_kernel(
 
         roots(0, 0, [slice(0, PACK, 2)])
         nc.scalar.activation(root[0][0][:], root[0][0][:], ACT.Square)
-        damp(0, 0, [root[0][0][:]], "h_0", 1)
+        damp(0, 0, [root[0][0][:, :, c:c + HALF // 2] for c in (0, HALF // 2)], "h_0", 2)
         roots(0, 1, [slice(1, PACK, 2)])
         (y0, x0), (y1, x1) = weight_half(0, 1, 0), weight_half(0, 1, 1)
         nc.scalar.activation(y0, x0, ACT.Square)
-        nc.vector.tensor_tensor(y1, x1, x1, ALU.mult)
+        nc.vector.tensor_tensor(y1[:, 0:2, :], x1[:, 0:2, :], x1[:, 0:2, :], ALU.mult)
+        nc.scalar.activation(y1[:, 2:4, :], x1[:, 2:4, :], ACT.Square)
         damp(0, 1, [y0, y1], "h_1", 2)
         half_sums = [template_sums(0, c0, HALF // 2, c0 // P) for c0 in (0, HALF // 2)]
         for b in range(2):

@@ -155,7 +155,10 @@ def tile_list_transit_template_detrending_kernel(
                                         rhs=eng_picked[jh][:].bitcast(FP4X4),
                                         rhs_scale=eng_plane[:, jh * HALF:(jh + 1) * HALF],
                                         start=True, stop=True)
-                    nc.scalar.activation(resid[jh][b][:, t, :], acc[:], ACT.Copy, scale=gain_sb[:, b, t:t + 1])
+                    if (b, jh) == (1, 0) and t >= 2:
+                        nc.vector.tensor_scalar(resid[jh][b][:, t, :], acc[:], gain_sb[:, b, t:t + 1], None, ALU.mult)
+                    else:
+                        nc.scalar.activation(resid[jh][b][:, t, :], acc[:], ACT.Copy, scale=gain_sb[:, b, t:t + 1])
 
         resid = [[held([P, PACK, HALF], F32, "resid%d%d" % (jh, b)) for b in range(2)] for jh in range(2)]
         eng_picked = []
@@ -173,10 +176,10 @@ def tile_list_transit_template_detrending_kernel(
 
         ws_bf1 = placed([P, 2, PACK * HALF // 2], BF16, "ws_bf1", WS_BF1)
         round_ws(1, ws_bf1, nc.vector.tensor_copy)
-        wf_scales_sb = placed([P, 2, H], U8, "wf_scales_sb", WS_RAW1)
-        nc.vector.tensor_copy(wf_scales_sb[:].rearrange("p a (b t k e) -> p (a b) k t e", b=2, t=PACK, e=4),
-                              wf_raw_scales[:].rearrange("p (ab k e t) -> p ab k t e", ab=4, t=PACK, e=4))
         quantise_ws(1, ws_bf1)
+        wf_scales_sb = placed([P, 2, H], U8, "wf_scales_sb", WS_BF1)
+        nc.gpsimd.tensor_copy(wf_scales_sb[:].rearrange("p a (b t m) -> p (a b) t m", b=2, t=PACK),
+                              wf_raw_scales[:].rearrange("p (ab m t) -> p ab t m", ab=4, t=PACK))
         pix_planes.append(placed([P, S], U8, "pix_plane1", WS_RAW1 + 4 * HALF))
         move_picked_rows(pix_planes[1][:], pix_picked_scales, PIX_ROW + 16)
         wf_raw.append(placed([P, 2, HALF], U16, "wf_raw1", WS_BF1 + 4 * HALF))
@@ -285,7 +288,7 @@ def tile_list_transit_template_detrending_kernel(
             store(jh, c0, width)
 
         for jh in range(2):
-            gather_pixels(0, jh, (WS_BF1, WS_RAW1 + 8 * HALF)[jh])
+            gather_pixels(0, jh, WS_RAW1 + (8 + 4 * jh) * HALF)
         wt_codes = placed([P, 2, N], I32, "wt_codes", PIX0)
         nc.sync.dma_start(wt_codes[:], wt_words.rearrange("b p c i -> p b (c i)").bitcast(I32))
         sums = [[bank(jh * PACK + t, [P, HALF]) for t in range(PACK)] for jh in range(2)]

@@ -25,8 +25,7 @@ LAP = 64
 WS_RAW1 = 0
 ENG_SCALES = WS_RAW1 + 16 * HALF - LAP
 PIX0 = ENG_SCALES + T
-PIX_SCALES = PIX0 + 4 * T - LAP
-ENG_WORDS = PIX_SCALES + T
+ENG_WORDS = PIX0 + 4 * T
 PIX1 = ENG_WORDS + 2 * T - LAP
 WS_BF1 = PIX1 + 4 * T
 WS_BF0 = WS_BF1 + 8 * HALF
@@ -58,7 +57,7 @@ def tile_list_transit_template_detrending_kernel(
         eng_list = keep.tile([P, S // 16], U16, name="eng_list")
         eng_words = placed([P, T], U16, "eng_words", ENG_WORDS)
         eng_scales = placed([P, T], U8, "eng_scales", ENG_SCALES)
-        pix_scales = placed([P, T], U8, "pix_scales", PIX_SCALES)
+        pix_scales = held([P, T], U8, "pix_scales")
         ws_raw = [held([P, PACK, HALF], F32, "ws_raw0")]
         gain_sb = held([P, 2, 2 * PACK], F32, "gain_sb")
         eng_plane = held([P, S], U8, "eng_plane")
@@ -68,6 +67,12 @@ def tile_list_transit_template_detrending_kernel(
         nc.vector.memset(warm_in[:], 1.0)
         nc.vector.memset(eng_scales[0:ENG_ROW, :].bitcast(I32), 0)
         nc.gpsimd.memset(pix_scales[0:PIX_ROW, :].bitcast(I32), 0)
+        wf_raw_scales = held([P, 2 * H], U8, "wf_raw_scales", "weight_scales")
+        nc.gpsimd.memset(wf_raw_scales[:].bitcast(I32), 0)
+        wf_scale_rows = wf_scales.rearrange("a (q s) c -> s q a c", s=4)
+        for s in range(4):
+            nc.gpsimd.dma_start(wf_raw_scales[s:P:32, :].rearrange("q (a c) -> q a c", a=2).bitcast(I32),
+                                wf_scale_rows[s].bitcast(I32))
         nc.vector.memset(eng_plane[:].bitcast(I32), 0)
         nc.vector.memset(pix_planes[0][:].bitcast(I32), 0)
 
@@ -101,14 +106,11 @@ def tile_list_transit_template_detrending_kernel(
 
         gain_all = gain_sb[:, :, 0:PACK]
         gain_neg = [placed([P, 2, PACK], F32, "gain_neg_first", PICKED1 + 4 * HALF), held([P, 2, PACK], F32, "gain_neg")]
-        gain_safe = held([P, 2, PACK], F32, "gain_safe")
-        gain_inv = held([P, 2, PACK], F32, "gain_inv")
+        gain_safe = placed([P, 2, PACK], F32, "gain_safe", PIX0)
         gain_inv_sq = held([P, 2, PACK], F32, "gain_inv_sq")
         nc.vector.scalar_tensor_tensor(gain_safe[:], gain_all, 0.0, gain_all, ALU.is_equal, ALU.add)
         for tile in gain_neg:
             nc.vector.tensor_scalar(tile[:], gain_all, -1.0, None, ALU.mult)
-        nc.vector.reciprocal(gain_inv[:], gain_safe[:])
-        nc.vector.tensor_tensor(gain_inv_sq[:], gain_inv[:], gain_inv[:], ALU.mult)
 
         ws_codes = [held([P, HALF], U32, "ws_codes%d" % b) for b in range(2)]
         eng_picked_scales = held([P, S], U8, "eng_picked_scales")
@@ -116,18 +118,15 @@ def tile_list_transit_template_detrending_kernel(
         move_picked_rows(eng_plane[:], eng_picked_scales, ENG_ROW)
         ws_raw.append(placed([P, PACK, HALF], F32, "ws_raw1", WS_RAW1))
         nc.sync.dma_start(ws_raw[1][:], ws_rows[:, :, HALF:H])
-        wf_raw_scales = placed([P, 2 * H], U8, "wf_raw_scales", ENG_SCALES + 1600)
-        nc.gpsimd.memset(wf_raw_scales[:].bitcast(I32), 0)
-        wf_scale_rows = wf_scales.rearrange("a (q s) c -> s q a c", s=4)
-        for s in range(4):
-            nc.sync.dma_start(wf_raw_scales[s:P:32, :].rearrange("q (a c) -> q a c", a=2).bitcast(I32),
-                              wf_scale_rows[s].bitcast(I32))
+        gain_inv = placed([P, 2, PACK], F32, "gain_inv", ENG_SCALES + 1600)
+        nc.vector.reciprocal(gain_inv[:], gain_safe[:])
+        pix_words = [placed([P, T], I32, "pix_words0", PIX0)]
+        load_pixels(0, 0, T)
 
         pix_picked_scales = held([P, S], U8, "pix_picked_scales")
         nc.vector.tensor_copy(pix_picked_scales[:], pix_scales[:].indirect(pix_list[:]))
-        pix_words = [placed([P, T], I32, "pix_words0", PIX0)]
-        load_pixels(0, 0, T)
         move_picked_rows(pix_planes[0][:], pix_picked_scales, PIX_ROW)
+        nc.vector.tensor_tensor(gain_inv_sq[:], gain_inv[:], gain_inv[:], ALU.mult)
 
         def round_ws(b, ws_bf, copy):
             for u in range(2):
@@ -187,9 +186,9 @@ def tile_list_transit_template_detrending_kernel(
         systematics(1)
         deal_flux_weights(1)
 
-        wt_scales_sb = placed([P, 2 * N], U8, "wt_scales_sb", ENG_SCALES + 1600)
+        wt_scales_sb = held([P, 2 * N], U8, "wt_scales_sb", "weight_scales")
         for q in range(4):
-            nc.sync.dma_start(wt_scales_sb[32 * q:32 * q + 4, :].rearrange("s (b c) -> s b c", b=2).bitcast(I32),
+            nc.gpsimd.dma_start(wt_scales_sb[32 * q:32 * q + 4, :].rearrange("s (b c) -> s b c", b=2).bitcast(I32),
                               wt_scales[:, 4 * q:4 * q + 4, :].rearrange("b s c -> s b c").bitcast(I32))
 
         pix_picked = {}
@@ -317,8 +316,8 @@ def tile_list_transit_template_detrending_kernel(
         roots(0, 1, [slice(1, PACK, 2)])
         (y0, x0), (y1, x1) = weight_half(0, 1, 0), weight_half(0, 1, 1)
         nc.scalar.activation(y0, x0, ACT.Square)
-        nc.vector.tensor_tensor(y1[:, 0:2, :], x1[:, 0:2, :], x1[:, 0:2, :], ALU.mult)
-        nc.scalar.activation(y1[:, 2:4, :], x1[:, 2:4, :], ACT.Square)
+        nc.vector.tensor_tensor(y1[:, 0, :], x1[:, 0, :], x1[:, 0, :], ALU.mult)
+        nc.scalar.activation(y1[:, 1:4, :], x1[:, 1:4, :], ACT.Square)
         damp(0, 1, [y0, y1], "h_1", 2)
         half_sums = [template_sums(0, c0, HALF // 2, c0 // P) for c0 in (0, HALF // 2)]
         for b in range(2):

@@ -23,13 +23,13 @@ LIST_COLS = HALF // 16
 ENG_ROW, PIX_ROW = P - 16, P - 32
 LAP = 64
 WS_RAW1 = 0
-ENG_SCALES = WS_RAW1 + 16 * HALF - LAP
+ENG_SCALES = WS_RAW1 + 16 * HALF
 PIX0 = ENG_SCALES + T
 ENG_WORDS = PIX0 + 4 * T
-PIX1 = ENG_WORDS + 2 * T - LAP
-WS_BF1 = PIX1 + 4 * T
-WS_BF0 = WS_BF1 + 8 * HALF
-PICKED1 = WS_BF0 + 8 * HALF
+PIX1 = ENG_WORDS + 2 * T
+WS_BF0 = PIX1 + 4 * T - LAP
+WS_BF1 = WS_BF0 + 8 * HALF
+PICKED1 = WS_BF1 + 8 * HALF
 PIECES = ((0, 256), (256, 128), (384, 128))
 EARLY = {(0, 0): (1, 3), (0, 1): (0, 2), (1, 0): (0, 1, 2), (1, 1): ()}
 
@@ -84,9 +84,9 @@ def tile_list_transit_template_detrending_kernel(
                 rows = slice(first + s, first + 16, 4)
                 nc.sync.dma_start(plane[s:P:32, :].bitcast(I32), picked[rows, :].bitcast(I32))
 
-        def load_flux_weights(b):
-            words = wf_words[:, :, 2 * b * HALF:2 * (b + 1) * HALF].rearrange("a p c -> p a c")
-            nc.sync.dma_start(wf_raw[b][:].bitcast(I32), words.bitcast(I32))
+        def load_flux_weights(tile, b, passes):
+            words = wf_words[passes, :, 2 * b * HALF:2 * (b + 1) * HALF].rearrange("a p c -> p a c")
+            nc.sync.dma_start(tile[:].bitcast(I32), words.bitcast(I32))
 
         def load_pixels(a, c0, c1):
             nc.sync.dma_start(pix_words[a][:, c0:c1], tab_words[a, :, c0:c1].rearrange("p t i -> p (t i)").bitcast(I32))
@@ -99,8 +99,8 @@ def tile_list_transit_template_detrending_kernel(
         nc.sync.dma_start(gain_sb[:, :, 0:PACK], gain.rearrange("(b p t) -> p b t", b=2, t=PACK))
         nc.sync.dma_start(ws_raw[0][:], ws_rows[:, :, 0:HALF])
         nc.sync.dma_start(eng_words[:].bitcast(I32), tab2_words[0].bitcast(I32))
-        wf_raw = [held([P, 2, HALF], U16, "wf_raw0")]
-        load_flux_weights(0)
+        wf_first = held([P, 1, HALF], U16, "wf_first")
+        load_flux_weights(wf_first, 0, slice(0, 1))
         warm_out = held([P, 16], F32, "warm_out")
         nc.scalar.activation(warm_out[:], warm_in[:], ACT.Abs_reciprocal_sqrt)
 
@@ -140,9 +140,9 @@ def tile_list_transit_template_detrending_kernel(
             eng_picked.append(placed([P, HALF], U16, "eng_picked%d" % jh, offset))
             nc.vector.tensor_copy(eng_picked[jh][:], eng_words[:].indirect(eng_list[:, jh * LIST_COLS:(jh + 1) * LIST_COLS]))
 
-        def deal_flux_weights(b):
-            nc.scalar.copy(wf_codes[b][:].rearrange("p a (t m) -> p a t m", t=PACK),
-                 wf_raw[b][:].rearrange("p a (m t) -> p a t m", t=PACK))
+        def deal_flux_weights(raw, b, passes):
+            nc.scalar.copy(wf_codes[b][:, passes].rearrange("p a (t m) -> p a t m", t=PACK),
+                           raw[:].rearrange("p a (m t) -> p a t m", t=PACK))
 
         def systematics(b):
             for jh in range(2):
@@ -165,10 +165,10 @@ def tile_list_transit_template_detrending_kernel(
         ws_bf0 = placed([P, 2, PACK * HALF // 2], BF16, "ws_bf0", WS_BF0)
         round_ws(0, ws_bf0, nc.scalar.copy)
         wf_codes = [held([P, 2, HALF], U16, "wf_codes%d" % b) for b in range(2)]
-        deal_flux_weights(0)
+        deal_flux_weights(wf_first, 0, slice(0, 1))
         gather_engineering(0, ENG_SCALES + 576)
         quantise_ws(0, ws_bf0)
-        gather_engineering(1, WS_BF0)
+        gather_engineering(1, WS_BF0 + LAP)
         pix_words.append(placed([P, T], I32, "pix_words1", PIX1))
         load_pixels(1, 0, T)
         systematics(0)
@@ -176,15 +176,19 @@ def tile_list_transit_template_detrending_kernel(
         ws_bf1 = placed([P, 2, PACK * HALF // 2], BF16, "ws_bf1", WS_BF1)
         round_ws(1, ws_bf1, nc.vector.tensor_copy)
         quantise_ws(1, ws_bf1)
-        wf_scales_sb = placed([P, 2, H], U8, "wf_scales_sb", WS_BF1)
-        nc.gpsimd.tensor_copy(wf_scales_sb[:].rearrange("p a (b t m) -> p (a b) t m", b=2, t=PACK),
-                              wf_raw_scales[:].rearrange("p (ab m t) -> p ab t m", ab=4, t=PACK))
+        wf_scales_sb = [placed([P, H], U8, "wf_scales_sb%d" % a, WS_BF1 + a * H) for a in range(2)]
+        for a in range(2):
+            nc.gpsimd.tensor_copy(wf_scales_sb[a][:].rearrange("p (b t m) -> p b t m", b=2, t=PACK),
+                                  wf_raw_scales[:, a * H:(a + 1) * H].rearrange("p (b m t) -> p b t m", b=2, t=PACK))
+        wf_second = placed([P, 1, HALF], U16, "wf_second", WS_RAW1)
+        load_flux_weights(wf_second, 0, slice(1, 2))
         pix_planes.append(placed([P, S], U8, "pix_plane1", WS_RAW1 + 4 * HALF))
         move_picked_rows(pix_planes[1][:], pix_picked_scales, PIX_ROW + 16)
-        wf_raw.append(placed([P, 2, HALF], U16, "wf_raw1", WS_BF1 + 4 * HALF))
-        load_flux_weights(1)
+        wf_rest = placed([P, 2, HALF], U16, "wf_rest", WS_BF1 + 4 * HALF)
+        load_flux_weights(wf_rest, 1, slice(0, 2))
         systematics(1)
-        deal_flux_weights(1)
+        deal_flux_weights(wf_second, 0, slice(1, 2))
+        deal_flux_weights(wf_rest, 1, slice(0, 2))
 
         wt_scales_sb = held([P, 2 * N], U8, "wt_scales_sb", "weight_scales")
         for q in range(4):
@@ -203,7 +207,7 @@ def tile_list_transit_template_detrending_kernel(
 
         def flux_pass(acc, jh, b, t, a, opens):
             cols = slice(b * HALF + t * P, b * HALF + (t + 1) * P)
-            nc.tensor.matmul_mx(acc[:], lhsT=wf_codes[b][:, a, t * P:(t + 1) * P].bitcast(FP4X4), lhsT_scale=wf_scales_sb[:, a, cols],
+            nc.tensor.matmul_mx(acc[:], lhsT=wf_codes[b][:, a, t * P:(t + 1) * P].bitcast(FP4X4), lhsT_scale=wf_scales_sb[a][:, cols],
                                 rhs=pix_picked[a, jh][:].bitcast(FP8X4),
                                 rhs_scale=pix_planes[a][:, jh * HALF:(jh + 1) * HALF],
                                 start=opens, stop=not opens)
@@ -280,12 +284,6 @@ def tile_list_transit_template_detrending_kernel(
                 template_pass(sums[nt // per_bank][:, k, :], jh, c0, width, nt, b,
                               b == 0 and k == 0, b == 1 and k == per_bank - 1)
 
-        def finish(sums, jh, c0, width):
-            per_bank = HALF // width
-            for k, acc in enumerate(sums):
-                add_catalogue(acc[:], jh, c0, width, k * per_bank, (k + 1) * per_bank)
-            store(jh, c0, width)
-
         for jh in range(2):
             gather_pixels(0, jh, WS_RAW1 + (8 + 4 * jh) * HALF)
         wt_codes = placed([P, 2, N], I32, "wt_codes", PIX0)
@@ -324,7 +322,9 @@ def tile_list_transit_template_detrending_kernel(
             for k in range(2):
                 template_passes(half_sums[k], 0, k * HALF // 2, HALF // 2, b)
         for k in range(2):
-            finish(half_sums[k], 0, k * HALF // 2, HALF // 2)
+            for pair, acc in enumerate(half_sums[k]):
+                add_catalogue(acc[:], 0, k * HALF // 2, HALF // 2, 2 * pair, 2 * pair + 2)
+        store(0, 0, HALF)
         roots(1, 0, [slice(3, PACK)])
         (y0, x0), (y1, x1) = weight_half(1, 0, 0), weight_half(1, 0, 1, "h_1")
         nc.scalar.activation(y0, x0, ACT.Square)

@@ -31,7 +31,7 @@ WS_BF0 = PIX1 + 4 * T - LAP
 WS_BF1 = WS_BF0 + 8 * HALF
 PICKED1 = WS_BF1 + 8 * HALF
 PIECES = ((0, 256), (256, 128), (384, 128))
-EARLY = {(0, 0): (1, 3), (0, 1): (0, 2), (1, 0): (0, 1, 2), (1, 1): ()}
+EARLY = {(0, 0): (1, 3), (0, 1): (0, 2), (1, 0): (0, 1), (1, 1): ()}
 
 
 def tile_list_transit_template_detrending_kernel(
@@ -105,12 +105,11 @@ def tile_list_transit_template_detrending_kernel(
         nc.scalar.activation(warm_out[:], warm_in[:], ACT.Abs_reciprocal_sqrt)
 
         gain_all = gain_sb[:, :, 0:PACK]
-        gain_neg = [placed([P, 2, PACK], F32, "gain_neg_first", PICKED1 + 4 * HALF), held([P, 2, PACK], F32, "gain_neg")]
+        gain_neg = held([P, 2, PACK], F32, "gain_neg")
         gain_safe = placed([P, 2, PACK], F32, "gain_safe", PIX0)
         gain_inv_sq = held([P, 2, PACK], F32, "gain_inv_sq")
         nc.vector.scalar_tensor_tensor(gain_safe[:], gain_all, 0.0, gain_all, ALU.is_equal, ALU.add)
-        for tile in gain_neg:
-            nc.vector.tensor_scalar(tile[:], gain_all, -1.0, None, ALU.mult)
+        nc.vector.tensor_scalar(gain_neg[:], gain_all, -1.0, None, ALU.mult)
 
         ws_codes = [held([P, HALF], U32, "ws_codes%d" % b) for b in range(2)]
         eng_picked_scales = held([P, S], U8, "eng_picked_scales")
@@ -216,7 +215,7 @@ def tile_list_transit_template_detrending_kernel(
 
         def subtract_flux(acc, jh, b, t):
             tile = resid[jh][b][:, t, :]
-            nc.vector.scalar_tensor_tensor(tile, acc[:], gain_neg[(jh, b) != (0, 0)][:, b, t:t + 1], tile, ALU.mult, ALU.add)
+            nc.vector.scalar_tensor_tensor(tile, acc[:], gain_neg[:, b, t:t + 1], tile, ALU.mult, ALU.add)
             if t in EARLY[jh, b]:
                 nc.gpsimd.tensor_tensor(root[jh][b][:, t, :], tile, tile, ALU.mult)
 
@@ -295,11 +294,10 @@ def tile_list_transit_template_detrending_kernel(
         for jh in range(2):
             if jh == 0:
                 gather_pixels(1, 0, PICKED1)
+                gather_pixels(1, 1, PICKED1 + 4 * HALF)
             for t in range(PACK):
                 flux_pass(sums[jh][t], jh, 0, t, 1, False)
                 subtract_flux(sums[jh][t], jh, 0, t)
-            if jh == 0:
-                gather_pixels(1, 1, PICKED1 + 4 * HALF)
             for t in range(PACK):
                 acc = bank(t, [P, HALF])
                 for a in range(2):
@@ -314,8 +312,8 @@ def tile_list_transit_template_detrending_kernel(
         roots(0, 1, [slice(1, PACK, 2)])
         (y0, x0), (y1, x1) = weight_half(0, 1, 0), weight_half(0, 1, 1)
         nc.scalar.activation(y0, x0, ACT.Square)
-        nc.vector.tensor_tensor(y1[:, 0, :], x1[:, 0, :], x1[:, 0, :], ALU.mult)
-        nc.scalar.activation(y1[:, 1:4, :], x1[:, 1:4, :], ACT.Square)
+        nc.vector.tensor_tensor(y1[:, 0:3, :], x1[:, 0:3, :], x1[:, 0:3, :], ALU.mult)
+        nc.scalar.activation(y1[:, 3, :], x1[:, 3, :], ACT.Square)
         damp(0, 1, [y0, y1], "h_1", 2)
         half_sums = [template_sums(0, c0, HALF // 2, c0 // P) for c0 in (0, HALF // 2)]
         for b in range(2):
@@ -325,7 +323,7 @@ def tile_list_transit_template_detrending_kernel(
             for pair, acc in enumerate(half_sums[k]):
                 add_catalogue(acc[:], 0, k * HALF // 2, HALF // 2, 2 * pair, 2 * pair + 2)
         store(0, 0, HALF)
-        roots(1, 0, [slice(3, PACK)])
+        roots(1, 0, [slice(2, PACK)])
         (y0, x0), (y1, x1) = weight_half(1, 0, 0), weight_half(1, 0, 1, "h_1")
         nc.scalar.activation(y0, x0, ACT.Square)
         nc.gpsimd.tensor_tensor(y1, x1, x1, ALU.mult)

@@ -230,11 +230,10 @@ def tile_list_transit_template_detrending_kernel(
             for run in runs:
                 for t in range(PACK)[run]:
                     square_residual(jh, b, t)
+                inverse_root(tile[:, run, :], tile[:, run, :])
             for t in EARLY[jh, b]:
                 nc.scalar.activation(tile[:, t, :], tile[:, t, :], ACT.Abs_reciprocal_sqrt, bias=1.0,
                                      scale=gain_inv_sq[:, b, t:t + 1])
-            for run in runs:
-                inverse_root(tile[:, run, :], tile[:, run, :])
 
         def weight_half(jh, b, k, tag=""):
             tile = held([P, PACK, HALF // 2], F32, "weight%d%d%d" % (jh, b, k), tag)
@@ -306,7 +305,7 @@ def tile_list_transit_template_detrending_kernel(
         cat_sb = placed([P, N // P, S], F32, "cat_sb", PIX1)
         nc.sync.dma_start(cat_sb[:], cat.rearrange("(nt p) j -> p nt j", p=P))
 
-        roots(0, 0, [slice(0, PACK, 2)])
+        roots(0, 0, [slice(0, 1), slice(2, 3)])
         nc.scalar.activation(root[0][0][:], root[0][0][:], ACT.Square)
         damp(0, 0, [root[0][0][:, :, c:c + HALF // 2] for c in (0, HALF // 2)], "h_0", 2)
         roots(0, 1, [slice(1, PACK, 2)])

from contextlib import ExitStack

import concourse.mybir as mybir

KP, KE, H, N, T, S = 1024, 512, 1024, 512, 4096, 1024
FLOPS = 2 * S * (KP * H + KE * H + H * N)

F32 = mybir.dt.float32
BF16 = mybir.dt.bfloat16
I32 = mybir.dt.int32
U32 = mybir.dt.uint32
U16 = mybir.dt.uint16
U8 = mybir.dt.uint8
FP8X4 = mybir.dt.float8_e4m3fn_x4
FP4X4 = mybir.dt.float4_e2m1fn_x4
ALU = mybir.AluOpType
ACT = mybir.ActivationFunctionType

P = 128
PACK = 4
HALF = 512
LIST_COLS = HALF // 16
ENG_ROW, PIX_ROW = P - 16, P - 32
LAP = 64
WS_RAW1 = 0
ENG_SCALES = WS_RAW1 + 16 * HALF
PIX0 = ENG_SCALES + T
ENG_WORDS = PIX0 + 4 * T
PIX1 = ENG_WORDS + 2 * T
WS_BF0 = PIX1 + 4 * T - LAP
WS_BF1 = WS_BF0 + 8 * HALF
PICKED1 = WS_BF1 + 8 * HALF
PIECES = ((0, 256), (256, 128), (384, 128))
EARLY = {(0, 0): (1, 3), (0, 1): (0, 2), (1, 0): (0, 1), (1, 1): ()}


def tile_list_transit_template_detrending_kernel(
    tc, tab_words, tab_scales, offs, tab2_words, tab2_scales, offs2,
    wf_words, wf_scales, ws, gain, wt_words, wt_scales, cat, out,
):
    nc = tc.nc
    with ExitStack() as ctx:
        keep = ctx.enter_context(tc.tile_pool(name="keep", bufs=1))
        shared = ctx.enter_context(tc.tile_pool(name="shared", bufs=1))
        banks = ctx.enter_context(tc.psum_pool(name="banks", bufs=1))

        def bank(k, shape):
            return banks.tile(shape, F32, name="bank%d" % k)

        def held(shape, dtype, name, tag=""):
            return keep.tile(shape, dtype, name=name, tag=tag, align_bytes=64)

        def placed(shape, dtype, name, offset):
            return shared.tile(shape, dtype, name=name, offset=offset, align_bytes=64)

        pix_list = keep.tile([P, S // 16], U16, name="pix_list")
        eng_list = keep.tile([P, S // 16], U16, name="eng_list")
        eng_words = placed([P, T], U16, "eng_words", ENG_WORDS)
        eng_scales = placed([P, T], U8, "eng_scales", ENG_SCALES)
        pix_scales = held([P, T], U8, "pix_scales")
        ws_raw = [held([P, PACK, HALF], F32, "ws_raw0")]
        gain_sb = held([P, 2, 2 * PACK], F32, "gain_sb")
        eng_plane = held([P, S], U8, "eng_plane")
        pix_planes = [held([P, S], U8, "pix_plane0")]
        warm_in = held([P, 16], F32, "warm_in")

        nc.vector.memset(warm_in[:], 1.0)
        nc.vector.memset(eng_scales[0:ENG_ROW, :].bitcast(I32), 0)
        nc.gpsimd.memset(pix_scales[0:PIX_ROW, :].bitcast(I32), 0)
        wf_raw_scales = held([P, 2 * H], U8, "wf_raw_scales", "weight_scales")
        nc.gpsimd.memset(wf_raw_scales[:].bitcast(I32), 0)
        wf_scale_rows = wf_scales.rearrange("a (q s) c -> s q a c", s=4)
        for s in range(4):
            nc.gpsimd.dma_start(wf_raw_scales[s:P:32, :].rearrange("q (a c) -> q a c", a=2).bitcast(I32),
                                wf_scale_rows[s].bitcast(I32))
        nc.vector.memset(eng_plane[:].bitcast(I32), 0)
        nc.vector.memset(pix_planes[0][:].bitcast(I32), 0)

        def load_scale_rows(tile, dram, first):
            nc.sync.dma_start(tile[first:P, :].bitcast(I32), dram.rearrange("a q c -> (a q) c").bitcast(I32))

        def move_picked_rows(plane, picked, first):
            for s in range(4):
                rows = slice(first + s, first + 16, 4)
                nc.sync.dma_start(plane[s:P:32, :].bitcast(I32), picked[rows, :].bitcast(I32))

        def load_flux_weights(tile, b, passes):
            words = wf_words[passes, :, 2 * b * HALF:2 * (b + 1) * HALF].rearrange("a p c -> p a c")
            nc.sync.dma_start(tile[:].bitcast(I32), words.bitcast(I32))

        def load_pixels(a, c0, c1):
            nc.sync.dma_start(pix_words[a][:, c0:c1], tab_words[a, :, c0:c1].rearrange("p t i -> p (t i)").bitcast(I32))

        ws_rows = ws.rearrange("(p i) c -> p i c", i=PACK)
        nc.sync.dma_start(eng_list[:], offs2)
        load_scale_rows(eng_scales, tab2_scales, ENG_ROW)
        nc.sync.dma_start(pix_list[:], offs)
        load_scale_rows(pix_scales, tab_scales, PIX_ROW)
        nc.sync.dma_start(gain_sb[:, :, 0:PACK], gain.rearrange("(b p t) -> p b t", b=2, t=PACK))
        nc.sync.dma_start(ws_raw[0][:], ws_rows[:, :, 0:HALF])
        nc.sync.dma_start(eng_words[:].bitcast(I32), tab2_words[0].bitcast(I32))
        wf_first = held([P, 1, HALF], U16, "wf_first")
        load_flux_weights(wf_first, 0, slice(0, 1))
        warm_out = held([P, 16], F32, "warm_out")
        nc.scalar.activation(warm_out[:], warm_in[:], ACT.Abs_reciprocal_sqrt)

        gain_all = gain_sb[:, :, 0:PACK]
        gain_neg = held([P, 2, PACK], F32, "gain_neg")
        gain_safe = placed([P, 2, PACK], F32, "gain_safe", PIX0)
        gain_inv_sq = held([P, 2, PACK], F32, "gain_inv_sq")
        nc.vector.scalar_tensor_tensor(gain_safe[:], gain_all, 0.0, gain_all, ALU.is_equal, ALU.add)
        nc.vector.tensor_scalar(gain_neg[:], gain_all, -1.0, None, ALU.mult)

        ws_codes = [held([P, HALF], U32, "ws_codes%d" % b) for b in range(2)]
        eng_picked_scales = held([P, S], U8, "eng_picked_scales")
        nc.vector.tensor_copy(eng_picked_scales[:], eng_scales[:].indirect(eng_list[:]))
        move_picked_rows(eng_plane[:], eng_picked_scales, ENG_ROW)
        ws_raw.append(placed([P, PACK, HALF], F32, "ws_raw1", WS_RAW1))
        nc.sync.dma_start(ws_raw[1][:], ws_rows[:, :, HALF:H])
        gain_inv = placed([P, 2, PACK], F32, "gain_inv", ENG_SCALES + 1600)
        nc.vector.reciprocal(gain_inv[:], gain_safe[:])
        pix_words = [placed([P, T], I32, "pix_words0", PIX0)]
        load_pixels(0, 0, T)

        pix_picked_scales = held([P, S], U8, "pix_picked_scales")
        nc.vector.tensor_copy(pix_picked_scales[:], pix_scales[:].indirect(pix_list[:]))
        move_picked_rows(pix_planes[0][:], pix_picked_scales, PIX_ROW)
        nc.vector.tensor_tensor(gain_inv_sq[:], gain_inv[:], gain_inv[:], ALU.mult)

        def round_ws(b, ws_bf, copy):
            for u in range(2):
                copy(ws_bf[:, u, :].rearrange("p (e m i) -> p m i e", e=2, i=PACK),
                     ws_raw[b][:].rearrange("p i (m u e) -> p u m i e", u=2, e=2)[:, u])

        def quantise_ws(b, ws_bf):
            nc.vector.quantize_mx(ws_codes[b][:].bitcast(FP8X4), ws_scales[b][:], ws_bf[:].rearrange("p u c -> p (u c)"))

        def gather_engineering(jh, offset):
            eng_picked.append(placed([P, HALF], U16, "eng_picked%d" % jh, offset))
            nc.vector.tensor_copy(eng_picked[jh][:], eng_words[:].indirect(eng_list[:, jh * LIST_COLS:(jh + 1) * LIST_COLS]))

        def deal_flux_weights(raw, b, passes):
            nc.scalar.copy(wf_codes[b][:, passes].rearrange("p a (t m) -> p a t m", t=PACK),
                           raw[:].rearrange("p a (m t) -> p a t m", t=PACK))

        def systematics(b):
            for jh in range(2):
                for t in range(PACK):
                    acc = bank(jh * PACK + t, [P, HALF])
                    cols = slice(t * P, (t + 1) * P)
                    nc.tensor.matmul_mx(acc[:], lhsT=ws_codes[b][:, cols].bitcast(FP8X4),
                                        lhsT_scale=ws_scales[b][:, cols],
                                        rhs=eng_picked[jh][:].bitcast(FP4X4),
                                        rhs_scale=eng_plane[:, jh * HALF:(jh + 1) * HALF],
                                        start=True, stop=True)
                    if (b, jh) == (1, 0) and t >= 2:
                        nc.vector.tensor_scalar(resid[jh][b][:, t, :], acc[:], gain_sb[:, b, t:t + 1], None, ALU.mult)
                    else:
                        nc.scalar.activation(resid[jh][b][:, t, :], acc[:], ACT.Copy, scale=gain_sb[:, b, t:t + 1])

        resid = [[held([P, PACK, HALF], F32, "resid%d%d" % (jh, b)) for b in range(2)] for jh in range(2)]
        eng_picked = []
        ws_scales = [placed([P, HALF], U8, "ws_scales0", ENG_SCALES + LAP), held([P, HALF], U8, "ws_scales1")]
        ws_bf0 = placed([P, 2, PACK * HALF // 2], BF16, "ws_bf0", WS_BF0)
        round_ws(0, ws_bf0, nc.scalar.copy)
        wf_codes = [held([P, 2, HALF], U16, "wf_codes%d" % b) for b in range(2)]
        deal_flux_weights(wf_first, 0, slice(0, 1))
        gather_engineering(0, ENG_SCALES + 576)
        quantise_ws(0, ws_bf0)
        gather_engineering(1, WS_BF0 + LAP)
        pix_words.append(placed([P, T], I32, "pix_words1", PIX1))
        load_pixels(1, 0, T)
        systematics(0)

        ws_bf1 = placed([P, 2, PACK * HALF // 2], BF16, "ws_bf1", WS_BF1)
        round_ws(1, ws_bf1, nc.vector.tensor_copy)
        quantise_ws(1, ws_bf1)
        wf_scales_sb = [placed([P, H], U8, "wf_scales_sb%d" % a, WS_BF1 + a * H) for a in range(2)]
        for a in range(2):
            nc.gpsimd.tensor_copy(wf_scales_sb[a][:].rearrange("p (b t m) -> p b t m", b=2, t=PACK),
                                  wf_raw_scales[:, a * H:(a + 1) * H].rearrange("p (b m t) -> p b t m", b=2, t=PACK))
        wf_second = placed([P, 1, HALF], U16, "wf_second", WS_RAW1)
        load_flux_weights(wf_second, 0, slice(1, 2))
        pix_planes.append(placed([P, S], U8, "pix_plane1", WS_RAW1 + 4 * HALF))
        move_picked_rows(pix_planes[1][:], pix_picked_scales, PIX_ROW + 16)
        wf_rest = placed([P, 2, HALF], U16, "wf_rest", WS_BF1 + 4 * HALF)
        load_flux_weights(wf_rest, 1, slice(0, 2))
        systematics(1)
        deal_flux_weights(wf_second, 0, slice(1, 2))
        deal_flux_weights(wf_rest, 1, slice(0, 2))

        wt_scales_sb = held([P, 2 * N], U8, "wt_scales_sb", "weight_scales")
        for q in range(4):
            nc.gpsimd.dma_start(wt_scales_sb[32 * q:32 * q + 4, :].rearrange("s (b c) -> s b c", b=2).bitcast(I32),
                              wt_scales[:, 4 * q:4 * q + 4, :].rearrange("b s c -> s b c").bitcast(I32))

        pix_picked = {}
        h_codes = [[held([P, HALF], U32, "h_codes%d%d" % (jh, b)) for b in range(2)] for jh in range(2)]
        h_scales = [[held([P, HALF], U8, "h_scales%d%d" % (jh, b)) for b in range(2)] for jh in range(2)]
        out_rows = out.rearrange("(nt p) j -> p nt j", p=P)

        def gather_pixels(a, jh, offset):
            pix_picked[a, jh] = placed([P, HALF], U32, "pix_picked%d%d" % (a, jh), offset)
            entries = pix_list[:, jh * LIST_COLS:(jh + 1) * LIST_COLS]
            nc.vector.tensor_copy(pix_picked[a, jh][:], pix_words[a][:].bitcast(U32).indirect(entries))

        def flux_pass(acc, jh, b, t, a, opens):
            cols = slice(b * HALF + t * P, b * HALF + (t + 1) * P)
            nc.tensor.matmul_mx(acc[:], lhsT=wf_codes[b][:, a, t * P:(t + 1) * P].bitcast(FP4X4), lhsT_scale=wf_scales_sb[a][:, cols],
                                rhs=pix_picked[a, jh][:].bitcast(FP8X4),
                                rhs_scale=pix_planes[a][:, jh * HALF:(jh + 1) * HALF],
                                start=opens, stop=not opens)

        root = [[held([P, PACK, HALF], F32, "root%d%d" % (jh, b)) for b in range(2 - jh)] for jh in range(2)]

        def subtract_flux(acc, jh, b, t):
            tile = resid[jh][b][:, t, :]
            nc.vector.scalar_tensor_tensor(tile, acc[:], gain_neg[:, b, t:t + 1], tile, ALU.mult, ALU.add)
            if t in EARLY[jh, b]:
                nc.gpsimd.tensor_tensor(root[jh][b][:, t, :], tile, tile, ALU.mult)

        def square_residual(jh, b, t):
            nc.scalar.activation(root[jh][b][:, t, :], resid[jh][b][:, t, :], ACT.Square, scale=gain_inv[:, b, t:t + 1])

        def inverse_root(y, x):
            nc.scalar.activation(y, x, ACT.Abs_reciprocal_sqrt, bias=1.0)

        def roots(jh, b, runs):
            tile = root[jh][b]
            for run in runs:
                for t in range(PACK)[run]:
                    square_residual(jh, b, t)
                inverse_root(tile[:, run, :], tile[:, run, :])
            for t in EARLY[jh, b]:
                nc.scalar.activation(tile[:, t, :], tile[:, t, :], ACT.Abs_reciprocal_sqrt, bias=1.0,
                                     scale=gain_inv_sq[:, b, t:t + 1])

        def weight_half(jh, b, k, tag=""):
            tile = held([P, PACK, HALF // 2], F32, "weight%d%d%d" % (jh, b, k), tag)
            return tile[:], root[jh][b][:, :, k * HALF // 2:(k + 1) * HALF // 2]

        def multiply(h, jh, b, cols, weights):
            nc.vector.tensor_tensor(h.rearrange("p (c e t) -> p c t e", e=2, t=PACK),
                                    resid[jh][b][:, :, cols].rearrange("p t (c e) -> p c t e", e=2),
                                    weights.rearrange("p t (c e) -> p c t e", e=2), ALU.mult)

        def quantise_h(h, jh, b, cols):
            nc.vector.quantize_mx(h_codes[jh][b][:, cols].bitcast(FP8X4), h_scales[jh][b][:, cols], h)

        def damp(jh, b, weights, h_tag, quantises):
            h = held([P, PACK * HALF], BF16, "h%d%d" % (jh, b), h_tag)
            for k, weight in enumerate(weights):
                cols = slice(k * HALF // len(weights), (k + 1) * HALF // len(weights))
                multiply(h[:, PACK * cols.start:PACK * cols.stop], jh, b, cols, weight)
            for k in range(quantises):
                cols = slice(k * HALF // quantises, (k + 1) * HALF // quantises)
                quantise_h(h[:, PACK * cols.start:PACK * cols.stop], jh, b, cols)

        def template_pass(acc, jh, c0, width, nt, b, start, stop):
            cols = slice(c0, c0 + width)
            nc.tensor.matmul_mx(acc, lhsT=wt_codes[:, b, nt * P:(nt + 1) * P].bitcast(FP8X4),
                                lhsT_scale=wt_scales_sb[:, b * N + nt * P:b * N + (nt + 1) * P],
                                rhs=h_codes[jh][b][:, cols].bitcast(FP8X4), rhs_scale=h_scales[jh][b][:, cols],
                                start=start, stop=stop)

        def add_catalogue(acc, jh, c0, width, nt0, nt1):
            scores = cat_sb[:, nt0:nt1, jh * HALF + c0:jh * HALF + c0 + width]
            nc.vector.tensor_tensor(scores, acc, scores, ALU.add)

        def store(jh, c0, width):
            entries = slice(jh * HALF + c0, jh * HALF + c0 + width)
            nc.sync.dma_start(out_rows[:, :, entries], cat_sb[:, :, entries])

        def template_sums(jh, c0, width, bank0):
            per_bank = HALF // width
            return [bank(bank0 + k, [P, per_bank, width]) for k in range(N // P // per_bank)]

        def template_passes(sums, jh, c0, width, b):
            per_bank = HALF // width
            for nt in range(N // P):
                k = nt % per_bank
                template_pass(sums[nt // per_bank][:, k, :], jh, c0, width, nt, b,
                              b == 0 and k == 0, b == 1 and k == per_bank - 1)

        for jh in range(2):
            gather_pixels(0, jh, WS_RAW1 + (8 + 4 * jh) * HALF)
        wt_codes = placed([P, 2, N], I32, "wt_codes", PIX0)
        nc.sync.dma_start(wt_codes[:], wt_words.rearrange("b p c i -> p b (c i)").bitcast(I32))
        sums = [[bank(jh * PACK + t, [P, HALF]) for t in range(PACK)] for jh in range(2)]
        for jh in range(2):
            for t in range(PACK):
                flux_pass(sums[jh][t], jh, 0, t, 0, True)
        for jh in range(2):
            if jh == 0:
                gather_pixels(1, 0, PICKED1)
                gather_pixels(1, 1, PICKED1 + 4 * HALF)
            for t in range(PACK):
                flux_pass(sums[jh][t], jh, 0, t, 1, False)
                subtract_flux(sums[jh][t], jh, 0, t)
            for t in range(PACK):
                acc = bank(t, [P, HALF])
                for a in range(2):
                    flux_pass(acc, jh, 1, t, a, a == 0)
                subtract_flux(acc, jh, 1, t)
        cat_sb = placed([P, N // P, S], F32, "cat_sb", PIX1)
        nc.sync.dma_start(cat_sb[:], cat.rearrange("(nt p) j -> p nt j", p=P))

        roots(0, 0, [slice(0, 1), slice(2, 3)])
        nc.scalar.activation(root[0][0][:], root[0][0][:], ACT.Square)
        damp(0, 0, [root[0][0][:, :, c:c + HALF // 2] for c in (0, HALF // 2)], "h_0", 2)
        roots(0, 1, [slice(1, PACK, 2)])
        (y0, x0), (y1, x1) = weight_half(0, 1, 0), weight_half(0, 1, 1)
        nc.scalar.activation(y0, x0, ACT.Square)
        nc.vector.tensor_tensor(y1[:, 0:3, :], x1[:, 0:3, :], x1[:, 0:3, :], ALU.mult)
        nc.scalar.activation(y1[:, 3, :], x1[:, 3, :], ACT.Square)
        damp(0, 1, [y0, y1], "h_1", 2)
        half_sums = [template_sums(0, c0, HALF // 2, c0 // P) for c0 in (0, HALF // 2)]
        for b in range(2):
            for k in range(2):
                template_passes(half_sums[k], 0, k * HALF // 2, HALF // 2, b)
        for k in range(2):
            for pair, acc in enumerate(half_sums[k]):
                add_catalogue(acc[:], 0, k * HALF // 2, HALF // 2, 2 * pair, 2 * pair + 2)
        store(0, 0, HALF)
        roots(1, 0, [slice(2, PACK)])
        (y0, x0), (y1, x1) = weight_half(1, 0, 0), weight_half(1, 0, 1, "h_1")
        nc.scalar.activation(y0, x0, ACT.Square)
        nc.gpsimd.tensor_tensor(y1, x1, x1, ALU.mult)
        damp(1, 0, [y0, y1], "h_0", 2)
        half_sums = [template_sums(1, c0, HALF // 2, PACK + c0 // P) for c0 in (0, HALF // 2)]
        for k in range(2):
            template_passes(half_sums[k], 1, k * HALF // 2, HALF // 2, 0)
        for k, (c0, width) in enumerate(PIECES):
            cols = slice(c0, c0 + width)
            if c0 % (HALF // 2) == 0:
                squared = held([P, PACK, HALF // 2], F32, "squared%d" % k)
                for t in range(PACK):
                    nc.scalar.activation(squared[:, t, :], resid[1][1][:, t, c0:c0 + HALF // 2], ACT.Square,
                                         scale=gain_inv[:, 1, t:t + 1])
            weight = held([P, PACK, width], F32, "weight11_%d" % k)
            inverse_root(weight[:], squared[:, :, c0 % (HALF // 2):c0 % (HALF // 2) + width])
            nc.scalar.activation(weight[:], weight[:], ACT.Square)
            h = held([P, PACK * width], BF16, "h11_%d" % k, ("h_1", "middle", "")[k])
            multiply(h[:], 1, 1, cols, weight[:])
            quantise_h(h[:], 1, 1, cols)
            offset = c0 % (HALF // 2)
            for nt in range(N // P):
                template_pass(half_sums[c0 // (HALF // 2)][nt // 2][:, nt % 2, offset:offset + width], 1, c0, width, nt, 1,
                              False, nt % 2 == 1 and offset + width == HALF // 2)
        staged = held([P, N // P, HALF // 2], F32, "staged", "middle")
        for k in range(2):
            rows, entries = slice(2 * k, 2 * k + 2), slice(HALF, HALF + HALF // 2)
            nc.vector.tensor_tensor(staged[:, rows, :], half_sums[0][k][:], cat_sb[:, rows, entries], ALU.add)
            nc.sync.dma_start(out_rows[:, rows, entries], staged[:, rows, :])
        for k in range(2):
            rows, entries = slice(2 * k, 2 * k + 2), slice(HALF + HALF // 2, S)
            add_catalogue(half_sums[1][k][:], 1, HALF // 2, HALF // 2, 2 * k, 2 * k + 2)
            nc.sync.dma_start(out_rows[:, rows, entries], cat_sb[:, rows, entries])
